import numpy as np
import ml_dtypes


def mxq(x, axis, fmt="e4m3"):
    dtype, down = {"e4m3": (ml_dtypes.float8_e4m3fn, 7), "e5m2": (ml_dtypes.float8_e5m2, 14)}[fmt]
    v = np.moveaxis(np.asarray(x, np.float32).astype(ml_dtypes.bfloat16).astype(np.float64), axis, -1)
    blocks = v.reshape(v.shape[:-1] + (-1, 32))
    amax = np.abs(blocks).max(-1, keepdims=True)
    byte = np.maximum(np.where(amax > 0, np.frexp(amax)[1] - 1 + 127, 0) - down, 1)
    scale = np.exp2(byte - 127.0)
    codes = (blocks / scale).astype(np.float32).astype(dtype).astype(np.float64)
    return np.moveaxis((codes * scale).reshape(v.shape), -1, axis)


WIDE = False


def mx_kscale(k):
    if not WIDE:
        return np.ones(k)
    levels = np.array([10, -10, 5, -5, 0])
    if k % 512:
        return np.exp2(np.random.permutation(np.resize(levels, k // 32))).repeat(32)
    a = np.empty((k // 512, 16))
    for p in range(k // 512):
        a[p, :8] = np.random.permutation(np.resize(levels, 8))
        for g in range(8):
            far = levels[np.abs(levels - a[p, g]) >= 10]
            a[p, g + 8] = far[np.random.randint(len(far))]
    return np.exp2(a.ravel()).repeat(32)


def f64(x):
    return np.asarray(x).astype(np.float64)


def striped(idx):
    return np.tile(idx.reshape(-1, 16).T, (8, 1)).astype(np.uint16)


def unstriped(offs):
    return offs[:16].T.reshape(-1).astype(np.int64)


E2M1 = np.array([0.0, 0.5, 1.0, 1.5, 2.0, 3.0, 4.0, 6.0, -0.0, -0.5, -1.0, -1.5, -2.0, -3.0, -4.0, -6.0])


def pack_weight(w, fmt):
    k, n = w.shape
    w = f64(np.asarray(w, np.float32).astype(ml_dtypes.bfloat16)).reshape(k // 32, 32, n)
    amax = np.abs(w).max(1)
    if fmt == "e4m3":
        byte = np.frexp(amax)[1] - 1 + 127 - 7
    else:
        mant, ex = np.frexp(amax / 6.0)
        byte = np.where(mant > 0.5, ex, ex - 1) + 127
    byte = np.clip(np.where(amax > 0, byte, 1), 1, 254)
    scaled = (w * np.exp2(127.0 - byte)[:, None, :]).reshape(k, n).astype(np.float32)
    by_word = np.ascontiguousarray(scaled.reshape(k // 512, 128, 4, n).transpose(0, 1, 3, 2))
    if fmt == "e4m3":
        words = by_word.astype(ml_dtypes.float8_e4m3fn).view(np.uint8)
    else:
        c = by_word.astype(ml_dtypes.float4_e2m1fn).view(np.uint8) & 0xF
        words = (c[..., 0::2] | (c[..., 1::2] << 4)).reshape(k // 512, 128, 2 * n)
    return np.ascontiguousarray(words), np.ascontiguousarray(byte.astype(np.uint8).reshape(k // 512, 16, n))


def unpack_weight(words, scales, fmt):
    g, _, n = scales.shape
    words = np.ascontiguousarray(words).reshape(g, 128, n, -1)
    if fmt == "e4m3":
        vals = words.view(ml_dtypes.float8_e4m3fn).astype(np.float64)
    else:
        nib = np.empty((g, 128, n, 4), np.uint8)
        nib[..., 0::2] = words & 0xF
        nib[..., 1::2] = words >> 4
        vals = E2M1[nib]
    vals = vals * np.repeat(np.exp2(scales.astype(np.float64) - 127.0), 8, axis=1)[..., None]
    return vals.transpose(0, 1, 3, 2).reshape(g * 512, n)


def gelu(v):
    return 0.5 * v * (1.0 + np.tanh(np.sqrt(2.0 / np.pi) * (v + 0.044715 * v**3)))


K, T, S, H, T2, P, N = 1536, 4096, 1024, 1024, 2048, 1024, 768

def setup_inputs():
    n = np.random.standard_normal
    s = mx_kscale(K)[:, None]
    u = mx_kscale(H)[:, None]
    d = {}
    d["tab_words"], d["tab_scales"] = pack_weight(n((K, T)) * s, "e4m3")
    d["offs"] = striped(np.random.permutation(T)[:S])
    d["w1"] = (n((K, H)) / np.sqrt(K) / s * u.T).astype(np.float32)
    d["wgs"] = np.exp(0.3 * n((128, S))).astype(np.float32)
    d["page0"] = (n((H, T2)) * u).astype(np.float32)
    d["offs2"] = striped(np.random.permutation(T2)[:S])
    d["offs3"] = striped(np.random.permutation(T2)[:P])
    d["b"] = (0.5 * n(H) * u[:, 0]).astype(np.float32)
    d["w2_words"], d["w2_scales"] = pack_weight(1.5 * n((H, N)) / np.sqrt(H) / u, "e2m1")
    return d

def reference(tab_words, tab_scales, offs, w1, wgs, page0, offs2, offs3, b, w2_words, w2_scales):
    v = unpack_weight(tab_words, tab_scales, "e4m3")[:, unstriped(offs)]
    w1q = mxq(f64(w1), 0, "e4m3")
    h = w1q.T @ v
    page = f64(page0).copy()
    page[:, unstriped(offs2)] = np.tile(f64(wgs), (H // 128, 1)) * h
    x = page[:, unstriped(offs3)]
    z = np.maximum(x + f64(b)[:, None], 0.0)
    zq = mxq(z, 0, "e4m3")
    w2 = unpack_weight(w2_words, w2_scales, "e2m1")
    out = w2.T @ zq
    return out

@@ -1,0 +1,331 @@
+from contextlib import ExitStack
+
+import concourse.mybir as mybir
+
+K, T, S, H, T2, M, N = 1536, 4096, 1024, 1024, 2048, 1024, 768
+FLOPS = 2 * K * H * S + 2 * H * N * M
+
+F32 = mybir.dt.float32
+BF16 = mybir.dt.bfloat16
+I32 = mybir.dt.int32
+U32 = mybir.dt.uint32
+U16 = mybir.dt.uint16
+U8 = mybir.dt.uint8
+FP8X4 = mybir.dt.float8_e4m3fn_x4
+FP4X4 = mybir.dt.float4_e2m1fn_x4
+MULT = mybir.AluOpType.mult
+RELU = mybir.ActivationFunctionType.Relu
+
+P = 128
+KP = 3
+TILES = 8
+CH = 256
+CHUNKS = M // CH
+
+
+def tile_list_pacing_board_kernel(
+    tc, tab_words, tab_scales, offs, w1, wgs, page0, offs2, offs3, b, w2_words, w2_scales, out
+):
+    nc = tc.nc
+    with ExitStack() as ctx:
+        keep = ctx.enter_context(tc.tile_pool(name="keep", bufs=1))
+        psum = ctx.enter_context(tc.psum_pool(name="psum", bufs=1))
+
+        def kt(name, shape, dtype):
+            return keep.tile(shape, dtype, name=name, align_bytes=64)
+
+        idx1 = kt("idx1", [P, S // 16], U16)
+        idx2 = kt("idx2", [P, S // 16], U16)
+        idx3 = kt("idx3", [P, M // 16], U16)
+        banks = [psum.tile([P, 512], F32, name="bank%d" % i) for i in range(8)]
+        gt = [kt("gt%d" % a, [P, S], U32) for a in range(KP)]
+        gs = kt("gs", [P, S], U8)
+        raw_n = [[kt("rawn%d_%d" % (n, a), [P, 512], F32) for a in range(KP)] for n in range(4)]
+        raw_q = [kt("rawq%d" % a, [P, 2048], F32) for a in range(KP)]
+        work = ctx.enter_context(tc.tile_pool(name="work", bufs=1))
+
+        def wt(name, offset, shape, dtype):
+            return work.tile(shape, dtype, name=name, offset=offset, align_bytes=64)
+
+        h_odd, x_at, h_even, spare0, spare1, z_at = 0, 4096, 8192, 12288, 15360, 18432
+        wb_at = [spare0, spare1] + [(x_at if n % 2 == 0 else h_even) - 1536 for n in range(2, TILES)]
+        wc_at = [wb_at[2], h_even] + [(spare0 - 1536 if n % 2 == 0 else h_odd) for n in range(2, TILES)]
+        wb = [wt("wb%d" % n, wb_at[n], [P, KP * 512], BF16) for n in range(TILES)]
+        wc = [wt("wc%d" % n, wc_at[n], [P, KP * P], U32) for n in range(TILES)]
+        ws = [wt("ws0", spare1, [P, KP * P], U8)] + [kt("ws%d" % n, [P, KP * P], U8) for n in range(1, TILES)]
+        hs0 = [wt("hs0_%d" % i, h_even + 2048 * i, [P, 512], F32) for i in range(2)]
+        hs = [None] + [wt("hs%d" % n, h_odd if n % 2 else h_even, [P, S], F32) for n in range(1, TILES - 1)]
+        zt0 = wt("zt0", z_at + 4096, [P, 4 * M], BF16)
+        hs7 = [wt("hs7_%d" % i, z_at + 4096 + 2048 * i, [P, 512], F32) for i in range(2)]
+        xs = [wt("x%d" % n, x_at, [P, M], F32) for n in range(6)]
+        zb0 = wt("zb0", h_odd, [P, 4 * M], BF16)
+        zc = [kt("zc0", [P, M], U32), kt("zc1", [P, M], U32)]
+        zs = [wt("zs0", z_at + 4096, [P, M], U8), kt("zs1", [P, M], U8)]
+        zb1_at = [z_at, z_at + 2048, spare0, spare0 + 2048]
+        zb1 = [wt("zb1_%d" % c, zb1_at[c], [P, 4 * CH], BF16) for c in range(CHUNKS)]
+        x7_at = [h_even, h_even + 1024, z_at, z_at + 1024]
+        x6 = kt("x6", [P, M], F32)
+        x7 = [wt("x7_%d" % c, x7_at[c], [P, CH], F32) for c in range(CHUNKS)]
+
+        def h_half(n, hh):
+            if n in (0, TILES - 1):
+                return (hs0 if n == 0 else hs7)[hh][:]
+            return hs[n][:, 512 * hh : 512 * (hh + 1)]
+
+        pages = [kt("page%d" % n, [P, T2], F32) for n in range(4)]
+        wg_n = kt("wg_n", [P, S], F32)
+        wg_q = kt("wg_q", [P, 4 * S], F32)
+        bias_n = kt("bias_n", [P, 4], F32)
+        bias_q = kt("bias_q", [P, 4], F32)
+        zn = [kt("zn%d" % n, [P, M], BF16) for n in range(4)]
+        w2w = kt("w2w", [P, 2, 2 * N], U8)
+        w2s = kt("w2s", [P, 2, N], U8)
+
+        def load_w1_natural(n):
+            for a in range(KP):
+                nc.sync.dma_start(
+                    out=raw_n[n][a][:].rearrange("p (j c) -> p j c", j=4),
+                    in_=w1[512 * a : 512 * (a + 1), P * n : P * (n + 1)].rearrange("(p j) c -> p j c", j=4),
+                )
+
+        def load_w1_quad(a):
+            nc.sync.dma_start(
+                out=raw_q[a][:].rearrange("p (j c) -> p j c", j=4),
+                in_=w1[512 * a : 512 * (a + 1), 512:1024].rearrange("(p j) c -> p j c", j=4),
+            )
+
+        def load_page(n):
+            if n < 4:
+                rows = page0[P * n : P * (n + 1), :]
+            else:
+                rows = page0[512:1024, :].rearrange("(p t) c -> t p c", t=4)[n - 4]
+            nc.sync.dma_start(out=pages[n][:], in_=rows)
+
+        def cast_w1(n):
+            for a in range(KP):
+                dst = wb[n][:, 512 * a : 512 * (a + 1)]
+                if n < 4:
+                    nc.scalar.copy(
+                        out=dst.rearrange("p (c i j) -> p c j i", i=4, j=4),
+                        in_=raw_n[n][a][:].rearrange("p (j c i) -> p c j i", j=4, i=4),
+                    )
+                else:
+                    nc.scalar.copy(
+                        out=dst.rearrange("p (m j) -> p m j", j=4),
+                        in_=raw_q[a][:].rearrange("p (j m t) -> p t m j", j=4, t=4)[:, n - 4],
+                    )
+
+        def quant_w1(n):
+            cuts = (0, 1, 2, 3) if n == 0 else (0, 2, 3)
+            for lo, hi in zip(cuts, cuts[1:]):
+                nc.vector.quantize_mx(
+                    out=wc[n][:, P * lo : P * hi].bitcast(FP8X4),
+                    scales=ws[n][:, P * lo : P * hi],
+                    in_=wb[n][:, 512 * lo : 512 * hi],
+                )
+
+        def product1(n):
+            for hh in range(2):
+                cols = slice(512 * hh, 512 * (hh + 1))
+                for a in range(KP):
+                    nc.tensor.matmul_mx(
+                        out=banks[2 * (n % 2) + hh][:],
+                        lhsT=wc[n][:, P * a : P * (a + 1)].bitcast(FP8X4),
+                        lhsT_scale=ws[n][:, P * a : P * (a + 1)],
+                        rhs=gt[a][:, cols].bitcast(FP8X4),
+                        rhs_scale=gs[4 * a : P, cols],
+                        start=(a == 0),
+                        stop=(a == KP - 1),
+                    )
+
+        def copy_h(n):
+            for hh in range(2):
+                nc.scalar.copy(out=h_half(n, hh), in_=banks[2 * (n % 2) + hh][:])
+
+        def scatter(n):
+            wg = wg_n[:] if n < 4 else wg_q[:, S * (n - 4) : S * (n - 3)]
+            parts = 2 if n in (0, TILES - 1) else 1
+            w = S // parts
+            for i in range(parts):
+                if n == 0 and i == 1:
+                    quant_w1(1)
+                    product1(1)
+                if n == TILES - 1 and i == 1:
+                    nc.vector.quantize_mx(out=zc[0][:].bitcast(FP8X4), scales=zs[0][:], in_=zb0[:])
+                nc.vector.tensor_tensor(
+                    pages[n][:].indirect(idx2[:, i * w // 16 : (i + 1) * w // 16]),
+                    h_half(n, i) if parts == 2 else hs[n][:],
+                    wg[:, i * w : (i + 1) * w],
+                    MULT,
+                )
+
+        def fetch(n, x, lo, hi):
+            nc.vector.tensor_copy(x[:], pages[n][:].indirect(idx3[:, lo // 16 : hi // 16]))
+
+        def rectify(n, x, lo, hi):
+            if n < 4:
+                dst, bias = zn[n][:, lo:hi], bias_n[:, n : n + 1]
+            else:
+                dst, bias = zt[1][:, M * (n - 4) + lo : M * (n - 4) + hi], bias_q[:, n - 4 : n - 3]
+            nc.scalar.activation(out=dst, in_=x[:], func=RELU, bias=bias)
+
+        with tc.tile_pool(name="table", bufs=1) as table:
+            tabw = [table.tile([P, T], I32, name="tabw%d" % a, align_bytes=64) for a in range(KP)]
+            tabs = table.tile([P, T], U8, name="tabs", align_bytes=64)
+
+            def load_table(a):
+                nc.sync.dma_start(out=tabw[a][:], in_=tab_words[a].rearrange("p t i -> p (t i)").bitcast(I32))
+
+            nc.vector.memset(tabs[:].bitcast(I32), 0)
+            nc.vector.memset(w2s[:].bitcast(I32), 0)
+            for q in range(4):
+                nc.scalar.dma_start(
+                    out=tabs[32 * q : 32 * q + 4 * KP, :].bitcast(I32),
+                    in_=tab_scales[:, 4 * q : 4 * q + 4, :].bitcast(I32),
+                )
+            nc.sync.dma_start(idx1[:], offs)
+            load_table(0)
+            load_w1_natural(0)
+            load_table(1)
+            load_table(2)
+            nc.sync.dma_start(idx2[:], offs2)
+            load_page(0)
+            for hh in range(2):
+                nc.sync.dma_start(out=wg_n[:, 512 * hh : 512 * (hh + 1)], in_=wgs[:, 512 * hh : 512 * (hh + 1)])
+
+            nc.vector.tensor_copy(gs[:], tabs[:].indirect(idx1[:]))
+            for a in range(KP):
+                parts = 2 if a == KP - 1 else 1
+                w = S // parts
+                for i in range(parts):
+                    nc.vector.tensor_copy(
+                        gt[a][:, i * w : (i + 1) * w],
+                        tabw[a][:].bitcast(U32).indirect(idx1[:, i * w // 16 : (i + 1) * w // 16]),
+                    )
+
+        late = ctx.enter_context(tc.tile_pool(name="late", bufs=1))
+        pages = pages + [late.tile([P, T2], F32, name="page%d" % n, align_bytes=64) for n in range(4, TILES)]
+        zt = [zt0, late.tile([P, 4 * M], BF16, name="zt1", align_bytes=64)]
+
+        load_w1_natural(1)
+        nc.sync.dma_start(idx3[:], offs3)
+        load_w1_natural(2)
+        load_page(1)
+        with nc.allow_non_contiguous_dma(reason="one bias value a partition"):
+            nc.sync.dma_start(out=bias_n[:], in_=b[0:512].rearrange("(g p) -> p g", p=P))
+        load_w1_natural(3)
+        load_w1_quad(0)
+        load_page(2)
+        load_w1_quad(1)
+        load_w1_quad(2)
+        load_page(3)
+        for q in range(4):
+            nc.sync.dma_start(out=wg_q[32 * q : 32 * (q + 1), :], in_=wgs.rearrange("(u t) j -> u (t j)", t=4))
+        nc.sync.dma_start(out=bias_q[:], in_=b[512:1024].rearrange("(p t) -> p t", t=4))
+        load_page(4)
+        nc.sync.dma_start(out=w2w[:].bitcast(I32), in_=w2_words.rearrange("a p c -> p a c").bitcast(I32))
+        for q in range(4):
+            nc.sync.dma_start(
+                out=w2s[32 * q : 32 * q + 4, :, :].bitcast(I32),
+                in_=w2_scales[:, 4 * q : 4 * q + 4, :].rearrange("a r c -> r a c").bitcast(I32),
+            )
+
+        def interleave(engine_copy, dst, a, lo, hi):
+            engine_copy(
+                out=dst.rearrange("p (c i t) -> p c t i", i=4, t=4),
+                in_=zt[a][:].rearrange("p (t m) -> p t m", t=4)[:, :, lo:hi].rearrange("p t (c i) -> p c t i", i=4),
+            )
+
+        def out_bank(c, i):
+            return banks[(4 + 3 * c + i) % 8]
+
+        def product2(c, a, which):
+            for i in which:
+                for j in range(2):
+                    nt = 2 * i + j
+                    for h in range(2):
+                        cols = slice(CH * c + P * h, CH * c + P * (h + 1))
+                        nc.tensor.matmul_mx(
+                            out=out_bank(c, i)[:, CH * j + P * h : CH * j + P * (h + 1)],
+                            lhsT=w2w[:, a, 2 * P * nt : 2 * P * (nt + 1)].bitcast(FP4X4),
+                            lhsT_scale=w2s[:, a, P * nt : P * (nt + 1)],
+                            rhs=zc[a][:, cols].bitcast(FP8X4),
+                            rhs_scale=zs[a][:, cols],
+                            start=(a == 0 and j == 0 and h == 0),
+                            stop=(a == 1 and j == 1 and h == 1),
+                        )
+
+        cast_w1(0)
+        quant_w1(0)
+        product1(0)
+        copy_h(0)
+        cast_w1(1)
+        cast_w1(2)
+        for n in range(6):
+            scatter(n)
+            quant_w1(n + 2)
+            product1(n + 2)
+            copy_h(n + 1)
+            fetch(n, xs[n], 0, M)
+            rectify(n, xs[n], 0, M)
+            if n + 3 < TILES:
+                cast_w1(n + 3)
+            if n < 4:
+                for t in range(4):
+                    nc.sync.dma_start(out=zt[0][32 * n : 32 * (n + 1), M * t : M * (t + 1)], in_=zn[n][t:P:4, :])
+            if n == 3:
+                for later in range(5, TILES):
+                    load_page(later)
+        for c in range(CHUNKS):
+            interleave(nc.scalar.copy, zb0[:, 4 * CH * c : 4 * CH * (c + 1)], 0, CH * c, CH * (c + 1))
+        scatter(6)
+        copy_h(7)
+        fetch(6, x6, 0, M)
+        rectify(6, x6, 0, M)
+        scatter(7)
+        product2(0, 0, range(3))
+        product2(1, 0, range(3))
+        product2(2, 0, range(2))
+
+        def finish(c, i):
+            stage = raw_n[c][i]
+            if c >= 2 and (c + i) % 2 == 0:
+                nc.vector.tensor_copy(out=stage[:], in_=out_bank(c, i)[:])
+            else:
+                nc.scalar.copy(out=stage[:], in_=out_bank(c, i)[:])
+            nc.sync.dma_start(
+                out=out[2 * P * i : 2 * P * (i + 1), CH * c : CH * (c + 1)].rearrange("(j p) m -> p j m", p=P),
+                in_=stage[:].rearrange("p (j m) -> p j m", j=2),
+            )
+
+        def second_pass(c):
+            lo, hi = CH * c, CH * (c + 1)
+            interleave(nc.vector.tensor_copy, zb1[c][:], 1, lo, hi)
+            nc.vector.quantize_mx(out=zc[1][:, lo:hi].bitcast(FP8X4), scales=zs[1][:, lo:hi], in_=zb1[c][:])
+
+        def fetch_last(c):
+            fetch(7, x7[c], CH * c, CH * (c + 1))
+            rectify(7, x7[c], CH * c, CH * (c + 1))
+
+        fetch_last(0)
+        fetch_last(1)
+        second_pass(0)
+        product2(0, 1, range(3))
+        fetch_last(2)
+        fetch_last(3)
+        second_pass(1)
+        second_pass(2)
+        second_pass(3)
+        product2(1, 1, range(3))
+        for i in range(3):
+            finish(0, i)
+        product2(2, 0, (2,))
+        product2(2, 1, range(3))
+        product2(3, 0, range(2))
+        for i in range(3):
+            finish(1, i)
+        product2(3, 0, (2,))
+        product2(3, 1, range(3))
+        for c in (2, 3):
+            for i in range(3):
+                finish(c, i)

@@ -38,9 +38,9 @@ def tile_list_pacing_board_kernel(
         idx2 = kt("idx2", [P, S // 16], U16)
         idx3 = kt("idx3", [P, M // 16], U16)
         banks = [psum.tile([P, 512], F32, name="bank%d" % i) for i in range(8)]
-        gt = [kt("gt%d" % a, [P, S], U32) for a in range(KP)]
         gs = kt("gs", [P, S], U8)
-        raw_n = [[kt("rawn%d_%d" % (n, a), [P, 512], F32) for a in range(KP)] for n in range(4)]
+        raw_n = [[kt("rawn%d_%d" % (n, a), [P, 512], F32) for a in range(KP)] for n in range(2)]
+        raw_m = [kt("rawm%d" % a, [P, 1024], F32) for a in range(KP)]
         raw_q = [kt("rawq%d" % a, [P, 2048], F32) for a in range(KP)]
         work = ctx.enter_context(tc.tile_pool(name="work", bufs=1))
 
@@ -49,9 +49,12 @@ def tile_list_pacing_board_kernel(
 
         h_odd, x_at, h_even, spare0, spare1, z_at = 0, 4096, 8192, 12288, 15360, 18432
         wb_at = [spare0, spare1] + [(x_at if n % 2 == 0 else h_even) - 1536 for n in range(2, TILES)]
-        wc_at = [wb_at[2], h_even] + [(spare0 - 1536 if n % 2 == 0 else h_odd) for n in range(2, TILES)]
+        wc_at = [wb_at[2], h_even, spare0 - 1536]
         wb = [wt("wb%d" % n, wb_at[n], [P, KP * 512], BF16) for n in range(TILES)]
-        wc = [wt("wc%d" % n, wc_at[n], [P, KP * P], U32) for n in range(TILES)]
+        wc = [wt("wc%d" % n, wc_at[n], [P, KP * P], U32) for n in range(3)]
+        wc = wc + [kt("wc%d" % n, [P, KP * P], U32) for n in range(3, TILES)]
+        tabs = wt("tabs", z_at + 12288, [P, T], U8)
+        gt = [kt("gt0", [P, S], U32), kt("gt1", [P, S], U32), wt("gt2", z_at + 12288, [P, S], U32)]
         ws = [wt("ws0", spare1, [P, KP * P], U8)] + [kt("ws%d" % n, [P, KP * P], U8) for n in range(1, TILES)]
         hs0 = [wt("hs0_%d" % i, h_even + 2048 * i, [P, 512], F32) for i in range(2)]
         hs = [None] + [wt("hs%d" % n, h_odd if n % 2 else h_even, [P, S], F32) for n in range(1, TILES - 1)]
@@ -88,6 +91,13 @@ def tile_list_pacing_board_kernel(
                     in_=w1[512 * a : 512 * (a + 1), P * n : P * (n + 1)].rearrange("(p j) c -> p j c", j=4),
                 )
 
+        def load_w1_pair():
+            for a in range(KP):
+                nc.sync.dma_start(
+                    out=raw_m[a][:].rearrange("p (j c) -> p j c", j=4),
+                    in_=w1[512 * a : 512 * (a + 1), 2 * P : 4 * P].rearrange("(p j) c -> p j c", j=4),
+                )
+
         def load_w1_quad(a):
             nc.sync.dma_start(
                 out=raw_q[a][:].rearrange("p (j c) -> p j c", j=4),
@@ -105,9 +115,13 @@ def tile_list_pacing_board_kernel(
             for a in range(KP):
                 dst = wb[n][:, 512 * a : 512 * (a + 1)]
                 if n < 4:
+                    if n < 2:
+                        src = raw_n[n][a][:].rearrange("p (j c) -> p j c", j=4)
+                    else:
+                        src = raw_m[a][:].rearrange("p (j c) -> p j c", j=4)[:, :, P * (n - 2) : P * (n - 1)]
                     nc.scalar.copy(
                         out=dst.rearrange("p (c i j) -> p c j i", i=4, j=4),
-                        in_=raw_n[n][a][:].rearrange("p (j c i) -> p c j i", j=4, i=4),
+                        in_=src.rearrange("p j (c i) -> p c j i", i=4),
                     )
                 else:
                     nc.scalar.copy(
@@ -144,7 +158,7 @@ def tile_list_pacing_board_kernel(
 
         def scatter(n):
             wg = wg_n[:] if n < 4 else wg_q[:, S * (n - 4) : S * (n - 3)]
-            parts = 2 if n in (0, TILES - 1) else 1
+            parts = 2 if n in (0, 1, TILES - 1) else 1
             w = S // parts
             for i in range(parts):
                 if n == 0 and i == 1:
@@ -171,7 +185,6 @@ def tile_list_pacing_board_kernel(
 
         with tc.tile_pool(name="table", bufs=1) as table:
             tabw = [table.tile([P, T], I32, name="tabw%d" % a, align_bytes=64) for a in range(KP)]
-            tabs = table.tile([P, T], U8, name="tabs", align_bytes=64)
 
             def load_table(a):
                 nc.sync.dma_start(out=tabw[a][:], in_=tab_words[a].rearrange("p t i -> p (t i)").bitcast(I32))
@@ -179,7 +192,7 @@ def tile_list_pacing_board_kernel(
             nc.vector.memset(tabs[:].bitcast(I32), 0)
             nc.vector.memset(w2s[:].bitcast(I32), 0)
             for q in range(4):
-                nc.scalar.dma_start(
+                nc.gpsimd.dma_start(
                     out=tabs[32 * q : 32 * q + 4 * KP, :].bitcast(I32),
                     in_=tab_scales[:, 4 * q : 4 * q + 4, :].bitcast(I32),
                 )
@@ -208,18 +221,17 @@ def tile_list_pacing_board_kernel(
         zt = [zt0, late.tile([P, 4 * M], BF16, name="zt1", align_bytes=64)]
 
         load_w1_natural(1)
+        load_w1_pair()
         nc.sync.dma_start(idx3[:], offs3)
-        load_w1_natural(2)
         load_page(1)
         with nc.allow_non_contiguous_dma(reason="one bias value a partition"):
             nc.sync.dma_start(out=bias_n[:], in_=b[0:512].rearrange("(g p) -> p g", p=P))
-        load_w1_natural(3)
         load_w1_quad(0)
         load_page(2)
         load_w1_quad(1)
         load_w1_quad(2)
         load_page(3)
-        for q in range(4):
+        for q in (0, 2, 1, 3):
             nc.sync.dma_start(out=wg_q[32 * q : 32 * (q + 1), :], in_=wgs.rearrange("(u t) j -> u (t j)", t=4))
         nc.sync.dma_start(out=bias_q[:], in_=b[512:1024].rearrange("(p t) -> p t", t=4))
         load_page(4)
@@ -288,14 +300,14 @@ def tile_list_pacing_board_kernel(
         product2(2, 0, range(2))
 
         def finish(c, i):
-            stage = raw_n[c][i]
+            stage = raw_n[c][i][:] if c < 2 else raw_m[i][:, 512 * (c - 2) : 512 * (c - 1)]
             if c >= 2 and (c + i) % 2 == 0:
-                nc.vector.tensor_copy(out=stage[:], in_=out_bank(c, i)[:])
+                nc.vector.tensor_copy(out=stage, in_=out_bank(c, i)[:])
             else:
-                nc.scalar.copy(out=stage[:], in_=out_bank(c, i)[:])
+                nc.scalar.copy(out=stage, in_=out_bank(c, i)[:])
             nc.sync.dma_start(
                 out=out[2 * P * i : 2 * P * (i + 1), CH * c : CH * (c + 1)].rearrange("(j p) m -> p j m", p=P),
-                in_=stage[:].rearrange("p (j m) -> p j m", j=2),
+                in_=stage.rearrange("p (j m) -> p j m", j=2),
             )
 
         def second_pass(c):

@@ -49,10 +49,9 @@ def tile_list_pacing_board_kernel(
 
         h_odd, x_at, h_even, spare0, spare1, z_at = 0, 4096, 8192, 12288, 15360, 18432
         wb_at = [spare0, spare1] + [(x_at if n % 2 == 0 else h_even) - 1536 for n in range(2, TILES)]
-        wc_at = [wb_at[2], h_even, spare0 - 1536]
+        wc_at = [wb_at[2], h_even] + [(spare0 - 1536 if n % 2 == 0 else h_odd) for n in range(2, TILES)]
         wb = [wt("wb%d" % n, wb_at[n], [P, KP * 512], BF16) for n in range(TILES)]
-        wc = [wt("wc%d" % n, wc_at[n], [P, KP * P], U32) for n in range(3)]
-        wc = wc + [kt("wc%d" % n, [P, KP * P], U32) for n in range(3, TILES)]
+        wc = [wt("wc%d" % n, wc_at[n], [P, KP * P], U32) for n in range(TILES)]
         tabs = wt("tabs", z_at + 12288, [P, T], U8)
         gt = [kt("gt0", [P, S], U32), kt("gt1", [P, S], U32), wt("gt2", z_at + 12288, [P, S], U32)]
         ws = [wt("ws0", spare1, [P, KP * P], U8)] + [kt("ws%d" % n, [P, KP * P], U8) for n in range(1, TILES)]
@@ -66,7 +65,7 @@ def tile_list_pacing_board_kernel(
         zs = [wt("zs0", z_at + 4096, [P, M], U8), kt("zs1", [P, M], U8)]
         zb1_at = [z_at, z_at + 2048, spare0, spare0 + 2048]
         zb1 = [wt("zb1_%d" % c, zb1_at[c], [P, 4 * CH], BF16) for c in range(CHUNKS)]
-        x7_at = [h_even, h_even + 1024, z_at, z_at + 1024]
+        x7_at = [h_even, h_even + 1024, z_at + 2048, z_at + 3072]
         x6 = kt("x6", [P, M], F32)
         x7 = [wt("x7_%d" % c, x7_at[c], [P, CH], F32) for c in range(CHUNKS)]
 
@@ -323,14 +322,15 @@ def tile_list_pacing_board_kernel(
         fetch_last(1)
         second_pass(0)
         product2(0, 1, range(3))
+        second_pass(1)
+        product2(1, 1, range(3))
+        finish(0, 0)
+        finish(0, 1)
         fetch_last(2)
         fetch_last(3)
-        second_pass(1)
+        finish(0, 2)
         second_pass(2)
         second_pass(3)
-        product2(1, 1, range(3))
-        for i in range(3):
-            finish(0, i)
         product2(2, 0, (2,))
         product2(2, 1, range(3))
         product2(3, 0, range(2))

@@ -39,8 +39,7 @@ def tile_list_pacing_board_kernel(
         idx3 = kt("idx3", [P, M // 16], U16)
         banks = [psum.tile([P, 512], F32, name="bank%d" % i) for i in range(8)]
         gs = kt("gs", [P, S], U8)
-        raw_n = [[kt("rawn%d_%d" % (n, a), [P, 512], F32) for a in range(KP)] for n in range(2)]
-        raw_m = [kt("rawm%d" % a, [P, 1024], F32) for a in range(KP)]
+        raw_n = [[kt("rawn%d_%d" % (n, a), [P, 512], F32) for a in range(KP)] for n in range(4)]
         raw_q = [kt("rawq%d" % a, [P, 2048], F32) for a in range(KP)]
         work = ctx.enter_context(tc.tile_pool(name="work", bufs=1))
 
@@ -58,15 +57,15 @@ def tile_list_pacing_board_kernel(
         hs0 = [wt("hs0_%d" % i, h_even + 2048 * i, [P, 512], F32) for i in range(2)]
         hs = [None] + [wt("hs%d" % n, h_odd if n % 2 else h_even, [P, S], F32) for n in range(1, TILES - 1)]
         zt0 = wt("zt0", z_at + 4096, [P, 4 * M], BF16)
-        hs7 = [wt("hs7_%d" % i, z_at + 4096 + 2048 * i, [P, 512], F32) for i in range(2)]
+        hs7 = [wt("hs7_0", z_at + 16384, [P, 512], F32), wt("hs7_1", z_at + 4096, [P, 512], F32)]
         xs = [wt("x%d" % n, x_at, [P, M], F32) for n in range(6)]
         zb0 = wt("zb0", h_odd, [P, 4 * M], BF16)
         zc = [kt("zc0", [P, M], U32), kt("zc1", [P, M], U32)]
-        zs = [wt("zs0", z_at + 4096, [P, M], U8), kt("zs1", [P, M], U8)]
+        zs = [wt("zs0", z_at + 16384, [P, M], U8), kt("zs1", [P, M], U8)]
         zb1_at = [z_at, z_at + 2048, spare0, spare0 + 2048]
         zb1 = [wt("zb1_%d" % c, zb1_at[c], [P, 4 * CH], BF16) for c in range(CHUNKS)]
-        x7_at = [h_even, h_even + 1024, z_at + 2048, z_at + 3072]
-        x6 = kt("x6", [P, M], F32)
+        x7_at = [h_even, h_even + 1024, z_at + 1024, z_at + 3072]
+        x6 = [kt("x6", [P, 2 * CH], F32), None, wt("x6_2", z_at, [P, CH], F32), wt("x6_3", z_at + 2048, [P, CH], F32)]
         x7 = [wt("x7_%d" % c, x7_at[c], [P, CH], F32) for c in range(CHUNKS)]
 
         def h_half(n, hh):
@@ -90,13 +89,6 @@ def tile_list_pacing_board_kernel(
                     in_=w1[512 * a : 512 * (a + 1), P * n : P * (n + 1)].rearrange("(p j) c -> p j c", j=4),
                 )
 
-        def load_w1_pair():
-            for a in range(KP):
-                nc.sync.dma_start(
-                    out=raw_m[a][:].rearrange("p (j c) -> p j c", j=4),
-                    in_=w1[512 * a : 512 * (a + 1), 2 * P : 4 * P].rearrange("(p j) c -> p j c", j=4),
-                )
-
         def load_w1_quad(a):
             nc.sync.dma_start(
                 out=raw_q[a][:].rearrange("p (j c) -> p j c", j=4),
@@ -114,13 +106,9 @@ def tile_list_pacing_board_kernel(
             for a in range(KP):
                 dst = wb[n][:, 512 * a : 512 * (a + 1)]
                 if n < 4:
-                    if n < 2:
-                        src = raw_n[n][a][:].rearrange("p (j c) -> p j c", j=4)
-                    else:
-                        src = raw_m[a][:].rearrange("p (j c) -> p j c", j=4)[:, :, P * (n - 2) : P * (n - 1)]
                     nc.scalar.copy(
                         out=dst.rearrange("p (c i j) -> p c j i", i=4, j=4),
-                        in_=src.rearrange("p j (c i) -> p c j i", i=4),
+                        in_=raw_n[n][a][:].rearrange("p (j c i) -> p c j i", j=4, i=4),
                     )
                 else:
                     nc.scalar.copy(
@@ -197,13 +185,14 @@ def tile_list_pacing_board_kernel(
                 )
             nc.sync.dma_start(idx1[:], offs)
             load_table(0)
-            load_w1_natural(0)
             load_table(1)
+            load_w1_natural(0)
             load_table(2)
             nc.sync.dma_start(idx2[:], offs2)
             load_page(0)
-            for hh in range(2):
-                nc.sync.dma_start(out=wg_n[:, 512 * hh : 512 * (hh + 1)], in_=wgs[:, 512 * hh : 512 * (hh + 1)])
+            nc.sync.dma_start(out=wg_n[:, 0:512], in_=wgs[:, 0:512])
+            load_w1_natural(1)
+            nc.sync.dma_start(out=wg_n[:, 512:S], in_=wgs[:, 512:S])
 
             nc.vector.tensor_copy(gs[:], tabs[:].indirect(idx1[:]))
             for a in range(KP):
@@ -219,12 +208,12 @@ def tile_list_pacing_board_kernel(
         pages = pages + [late.tile([P, T2], F32, name="page%d" % n, align_bytes=64) for n in range(4, TILES)]
         zt = [zt0, late.tile([P, 4 * M], BF16, name="zt1", align_bytes=64)]
 
-        load_w1_natural(1)
-        load_w1_pair()
+        load_w1_natural(2)
         nc.sync.dma_start(idx3[:], offs3)
         load_page(1)
         with nc.allow_non_contiguous_dma(reason="one bias value a partition"):
             nc.sync.dma_start(out=bias_n[:], in_=b[0:512].rearrange("(g p) -> p g", p=P))
+        load_w1_natural(3)
         load_w1_quad(0)
         load_page(2)
         load_w1_quad(1)
@@ -291,15 +280,15 @@ def tile_list_pacing_board_kernel(
             interleave(nc.scalar.copy, zb0[:, 4 * CH * c : 4 * CH * (c + 1)], 0, CH * c, CH * (c + 1))
         scatter(6)
         copy_h(7)
-        fetch(6, x6, 0, M)
-        rectify(6, x6, 0, M)
+        fetch(6, x6[0], 0, 2 * CH)
+        rectify(6, x6[0], 0, 2 * CH)
         scatter(7)
         product2(0, 0, range(3))
         product2(1, 0, range(3))
         product2(2, 0, range(2))
 
         def finish(c, i):
-            stage = raw_n[c][i][:] if c < 2 else raw_m[i][:, 512 * (c - 2) : 512 * (c - 1)]
+            stage = raw_n[c][i][:]
             if c >= 2 and (c + i) % 2 == 0:
                 nc.vector.tensor_copy(out=stage, in_=out_bank(c, i)[:])
             else:
@@ -311,10 +300,13 @@ def tile_list_pacing_board_kernel(
 
         def second_pass(c):
             lo, hi = CH * c, CH * (c + 1)
-            interleave(nc.vector.tensor_copy, zb1[c][:], 1, lo, hi)
+            interleave(nc.scalar.copy if c == 1 else nc.vector.tensor_copy, zb1[c][:], 1, lo, hi)
             nc.vector.quantize_mx(out=zc[1][:, lo:hi].bitcast(FP8X4), scales=zs[1][:, lo:hi], in_=zb1[c][:])
 
         def fetch_last(c):
+            if c >= 2:
+                fetch(6, x6[c], CH * c, CH * (c + 1))
+                rectify(6, x6[c], CH * c, CH * (c + 1))
             fetch(7, x7[c], CH * c, CH * (c + 1))
             rectify(7, x7[c], CH * c, CH * (c + 1))
 
@@ -326,9 +318,9 @@ def tile_list_pacing_board_kernel(
         product2(1, 1, range(3))
         finish(0, 0)
         finish(0, 1)
+        finish(0, 2)
         fetch_last(2)
         fetch_last(3)
-        finish(0, 2)
         second_pass(2)
         second_pass(3)
         product2(2, 0, (2,))

@@ -14,13 +14,19 @@ U8 = mybir.dt.uint8
 FP8X4 = mybir.dt.float8_e4m3fn_x4
 FP4X4 = mybir.dt.float4_e2m1fn_x4
 MULT = mybir.AluOpType.mult
+ADD = mybir.AluOpType.add
+MAX = mybir.AluOpType.max
 RELU = mybir.ActivationFunctionType.Relu
 
 P = 128
+KB = 1024
 KP = 3
 TILES = 8
+HALF = 512
 CH = 256
 CHUNKS = M // CH
+CUTS = (0, 256, 512, 1024)
+PLANE = (2, 0, 1, 3)
 
 
 def tile_list_pacing_board_kernel(
@@ -30,57 +36,72 @@ def tile_list_pacing_board_kernel(
     with ExitStack() as ctx:
         keep = ctx.enter_context(tc.tile_pool(name="keep", bufs=1))
         psum = ctx.enter_context(tc.psum_pool(name="psum", bufs=1))
-
-        def kt(name, shape, dtype):
-            return keep.tile(shape, dtype, name=name, align_bytes=64)
-
-        idx1 = kt("idx1", [P, S // 16], U16)
-        idx2 = kt("idx2", [P, S // 16], U16)
-        idx3 = kt("idx3", [P, M // 16], U16)
-        banks = [psum.tile([P, 512], F32, name="bank%d" % i) for i in range(8)]
-        gs = kt("gs", [P, S], U8)
-        raw_n = [[kt("rawn%d_%d" % (n, a), [P, 512], F32) for a in range(KP)] for n in range(4)]
-        raw_q = [kt("rawq%d" % a, [P, 2048], F32) for a in range(KP)]
         work = ctx.enter_context(tc.tile_pool(name="work", bufs=1))
+
+        idx1 = keep.tile([P, S // 16], U16, name="idx1", align_bytes=64)
+        idx2 = keep.tile([P, S // 16], U16, name="idx2", align_bytes=64)
+        idx3 = keep.tile([P, M // 16], U16, name="idx3", align_bytes=64)
+        banks = [psum.tile([P, 512], F32, name="bank%d" % i) for i in range(8)]
 
         def wt(name, offset, shape, dtype):
             return work.tile(shape, dtype, name=name, offset=offset, align_bytes=64)
 
-        h_odd, x_at, h_even, spare0, spare1, z_at = 0, 4096, 8192, 12288, 15360, 18432
-        wb_at = [spare0, spare1] + [(x_at if n % 2 == 0 else h_even) - 1536 for n in range(2, TILES)]
-        wc_at = [wb_at[2], h_even] + [(spare0 - 1536 if n % 2 == 0 else h_odd) for n in range(2, TILES)]
-        wb = [wt("wb%d" % n, wb_at[n], [P, KP * 512], BF16) for n in range(TILES)]
-        wc = [wt("wc%d" % n, wc_at[n], [P, KP * P], U32) for n in range(TILES)]
-        tabs = wt("tabs", z_at + 12288, [P, T], U8)
-        gt = [kt("gt0", [P, S], U32), kt("gt1", [P, S], U32), wt("gt2", z_at + 12288, [P, S], U32)]
-        ws = [wt("ws0", spare1, [P, KP * P], U8)] + [kt("ws%d" % n, [P, KP * P], U8) for n in range(1, TILES)]
-        hs0 = [wt("hs0_%d" % i, h_even + 2048 * i, [P, 512], F32) for i in range(2)]
-        hs = [None] + [wt("hs%d" % n, h_odd if n % 2 else h_even, [P, S], F32) for n in range(1, TILES - 1)]
-        zt0 = wt("zt0", z_at + 4096, [P, 4 * M], BF16)
-        hs7 = [wt("hs7_0", z_at + 16384, [P, 512], F32), wt("hs7_1", z_at + 4096, [P, 512], F32)]
-        xs = [wt("x%d" % n, x_at, [P, M], F32) for n in range(6)]
-        zb0 = wt("zb0", h_odd, [P, 4 * M], BF16)
-        zc = [kt("zc0", [P, M], U32), kt("zc1", [P, M], U32)]
-        zs = [wt("zs0", z_at + 16384, [P, M], U8), kt("zs1", [P, M], U8)]
-        zb1_at = [z_at, z_at + 2048, spare0, spare0 + 2048]
-        zb1 = [wt("zb1_%d" % c, zb1_at[c], [P, 4 * CH], BF16) for c in range(CHUNKS)]
-        x7_at = [h_even, h_even + 1024, z_at + 1024, z_at + 3072]
-        x6 = [kt("x6", [P, 2 * CH], F32), None, wt("x6_2", z_at, [P, CH], F32), wt("x6_3", z_at + 2048, [P, CH], F32)]
-        x7 = [wt("x7_%d" % c, x7_at[c], [P, CH], F32) for c in range(CHUNKS)]
+        table_at, scale_at, picked_at, rawn_at, rawq_at = 0, 48 * KB, 52 * KB, 61 * KB, 85 * KB
+        page_at, wg_at, h_at, x_at, zn_at = 109 * KB, 141 * KB, 161 * KB, 169 * KB, 177 * KB
+        wb_at, wc_at, misc_at = 185 * KB, 197 * KB, 209 * KB
+
+        tabw = [wt("tabw%d" % a, table_at + 16 * KB * a, [P, T], I32) for a in range(KP)]
+        tabs = wt("tabs", scale_at, [P, T], U8)
+        gt = [wt("gt%d" % a, picked_at + 4 * KB * a, [P, S], U32) for a in range(2)]
+        gt = gt + [wt("gt2", scale_at, [P, S], U32)]
+        gs = wt("gs", table_at + 28 * KB, [P, S], U8)
+        raw_n = [
+            [wt("rawn%d_%d" % (n, a), rawn_at + 6 * KB * n + 2 * KB * a, [P, 512], F32) for a in range(KP)]
+            for n in range(4)
+        ]
+        raw_q = [wt("rawq%d" % a, rawq_at + 8 * KB * a, [P, 2048], F32) for a in range(KP)]
+        pages = [wt("page%d" % n, page_at + 8 * KB * n, [P, T2], F32) for n in range(4)]
+        pages = pages + [wt("page%d" % (4 + n), table_at + 8 * KB * n + 16 * KB * (n // 2), [P, T2], F32) for n in range(4)]
+        wg_n = wt("wg_n", wg_at, [P, S], F32)
+        wg_q = [wt("wg_q%d" % t, wg_at + 4 * KB * (t + 1), [P, S], F32) for t in range(4)]
+        wb_n = [wt("wbn%d" % n, wb_at + 3 * KB * n, [P, KP * 512], BF16) for n in range(4)]
+        wb_q = wt("wbq", table_at + 16 * KB, [P, 4 * KP * 512], BF16)
+        wc_place = [wc_at, zn_at] + [x_at + 4 * KB * ((n - 1) % 2) for n in range(2, TILES)]
+        wc = [wt("wc%d" % n, wc_place[n], [P, KP * P], U32) for n in range(TILES)]
+
+        halved = (0, 1, TILES - 1)
+
+        def h_place(n, hh=0):
+            return h_at + 4 * KB * (n % 2) + 2 * KB * hh
+
+        hs = [
+            [wt("h%d_%d" % (n, hh), h_place(n, hh), [P, HALF], F32) for hh in range(2)]
+            if n in halved
+            else wt("h%d" % n, h_place(n), [P, S], F32)
+            for n in range(TILES)
+        ]
+        ws_at = [misc_at, h_place(0, 1), h_place(1, 0), h_place(1, 1)] + [h_place(n) for n in range(4, TILES)]
+        ws = [wt("ws%d" % n, ws_at[n], [P, KP * P], U8) for n in range(TILES)]
+        xs = [wt("x%d" % n, x_at + 4 * KB * (n % 2), [P, M], F32) for n in range(TILES - 1)]
+        x7_at = (x_at + 4 * KB, x_at + 5 * KB, rawq_at)
+        x7 = [wt("x7_%d" % c, x7_at[c], [P, CUTS[c + 1] - CUTS[c]], F32) for c in range(3)]
+        zn = [wt("zn%d" % n, rawq_at + 18 * KB if n == 2 else zn_at + 2 * KB * n, [P, M], BF16) for n in range(4)]
+        zt0 = wt("zt0", rawn_at, [P, 4 * M], BF16)
+        zb0 = wt("zb0", rawn_at + 12 * KB, [P, 4 * M], BF16)
+        zb1 = [wt("zb1_%d" % c, rawq_at + 8 * CUTS[c], [P, 4 * (CUTS[c + 1] - CUTS[c])], BF16) for c in range(3)]
+        zc = [wt("zc%d" % a, rawq_at + 8 * KB + 4 * KB * a, [P, M], U32) for a in range(2)]
+        zs = [wt("zs0", h_place(TILES - 1, 0), [P, M], U8), wt("zs1", rawq_at + 16 * KB, [P, M], U8)]
+        stage = [[wt("st%d_%d" % (c, i), rawn_at + 2 * KB * (3 * c + i), [P, 512], F32) for i in range(3)] for c in range(CHUNKS)]
+        w2w = wt("w2w", misc_at + 512, [P, 2, 2 * N], U8)
+        w2s = wt("w2s", misc_at + 512 + 3 * KB, [P, 2, N], U8)
+        bias_n = wt("bias_n", misc_at + 5 * KB, [P, 4], F32)
+        bias_q = wt("bias_q", misc_at + 5 * KB + 64, [P, 4], F32)
 
         def h_half(n, hh):
-            if n in (0, TILES - 1):
-                return (hs0 if n == 0 else hs7)[hh][:]
-            return hs[n][:, 512 * hh : 512 * (hh + 1)]
+            return hs[n][hh][:] if n in halved else hs[n][:, HALF * hh : HALF * (hh + 1)]
 
-        pages = [kt("page%d" % n, [P, T2], F32) for n in range(4)]
-        wg_n = kt("wg_n", [P, S], F32)
-        wg_q = kt("wg_q", [P, 4 * S], F32)
-        bias_n = kt("bias_n", [P, 4], F32)
-        bias_q = kt("bias_q", [P, 4], F32)
-        zn = [kt("zn%d" % n, [P, M], BF16) for n in range(4)]
-        w2w = kt("w2w", [P, 2, 2 * N], U8)
-        w2s = kt("w2s", [P, 2, N], U8)
+        def load_table(a):
+            nc.sync.dma_start(out=tabw[a][:], in_=tab_words[a].rearrange("p t i -> p (t i)").bitcast(I32))
 
         def load_w1_natural(n):
             for a in range(KP):
@@ -99,35 +120,48 @@ def tile_list_pacing_board_kernel(
             if n < 4:
                 rows = page0[P * n : P * (n + 1), :]
             else:
-                rows = page0[512:1024, :].rearrange("(p t) c -> t p c", t=4)[n - 4]
+                rows = page0[512:1024, :].rearrange("(p t) c -> t p c", t=4)[PLANE[n - 4]]
             nc.sync.dma_start(out=pages[n][:], in_=rows)
 
-        def cast_w1(n):
+        def load_wg_quad(n):
+            t = PLANE[n - 4]
+            for q in (0, 2, 1, 3):
+                nc.sync.dma_start(out=wg_q[t][32 * q : 32 * (q + 1), :], in_=wgs.rearrange("(u t) j -> t u j", t=4)[t])
+
+        def load_w2():
+            nc.sync.dma_start(out=w2w[:].bitcast(I32), in_=w2_words.rearrange("a p c -> p a c").bitcast(I32))
+            for q in range(4):
+                nc.sync.dma_start(
+                    out=w2s[32 * q : 32 * q + 4, :, :].bitcast(I32),
+                    in_=w2_scales[:, 4 * q : 4 * q + 4, :].rearrange("a r c -> r a c").bitcast(I32),
+                )
+
+        def cast_natural(n):
             for a in range(KP):
-                dst = wb[n][:, 512 * a : 512 * (a + 1)]
-                if n < 4:
-                    nc.scalar.copy(
-                        out=dst.rearrange("p (c i j) -> p c j i", i=4, j=4),
-                        in_=raw_n[n][a][:].rearrange("p (j c i) -> p c j i", j=4, i=4),
-                    )
-                else:
-                    nc.scalar.copy(
-                        out=dst.rearrange("p (m j) -> p m j", j=4),
-                        in_=raw_q[a][:].rearrange("p (j m t) -> p t m j", j=4, t=4)[:, n - 4],
-                    )
+                nc.scalar.copy(
+                    out=wb_n[n][:, 512 * a : 512 * (a + 1)].rearrange("p (c i j) -> p c j i", i=4, j=4),
+                    in_=raw_n[n][a][:].rearrange("p (j c i) -> p c j i", j=4, i=4),
+                )
+
+        def cast_quad(a):
+            nc.scalar.copy(
+                out=wb_q[:].rearrange("p (t a m j) -> p a m t j", t=4, a=KP, j=4)[:, a],
+                in_=raw_q[a][:].rearrange("p (j m t) -> p m t j", j=4, t=4),
+            )
 
         def quant_w1(n):
+            src = wb_n[n][:] if n < 4 else wb_q[:, 1536 * PLANE[n - 4] : 1536 * (PLANE[n - 4] + 1)]
             cuts = (0, 1, 2, 3) if n == 0 else (0, 2, 3)
             for lo, hi in zip(cuts, cuts[1:]):
                 nc.vector.quantize_mx(
                     out=wc[n][:, P * lo : P * hi].bitcast(FP8X4),
                     scales=ws[n][:, P * lo : P * hi],
-                    in_=wb[n][:, 512 * lo : 512 * hi],
+                    in_=src[:, 512 * lo : 512 * hi],
                 )
 
         def product1(n):
             for hh in range(2):
-                cols = slice(512 * hh, 512 * (hh + 1))
+                cols = slice(HALF * hh, HALF * (hh + 1))
                 for a in range(KP):
                     nc.tensor.matmul_mx(
                         out=banks[2 * (n % 2) + hh][:],
@@ -138,75 +172,68 @@ def tile_list_pacing_board_kernel(
                         start=(a == 0),
                         stop=(a == KP - 1),
                     )
-
-        def copy_h(n):
             for hh in range(2):
                 nc.scalar.copy(out=h_half(n, hh), in_=banks[2 * (n % 2) + hh][:])
 
-        def scatter(n):
-            wg = wg_n[:] if n < 4 else wg_q[:, S * (n - 4) : S * (n - 3)]
-            parts = 2 if n in (0, 1, TILES - 1) else 1
-            w = S // parts
-            for i in range(parts):
-                if n == 0 and i == 1:
-                    quant_w1(1)
-                    product1(1)
-                if n == TILES - 1 and i == 1:
-                    nc.vector.quantize_mx(out=zc[0][:].bitcast(FP8X4), scales=zs[0][:], in_=zb0[:])
-                nc.vector.tensor_tensor(
-                    pages[n][:].indirect(idx2[:, i * w // 16 : (i + 1) * w // 16]),
-                    h_half(n, i) if parts == 2 else hs[n][:],
-                    wg[:, i * w : (i + 1) * w],
-                    MULT,
-                )
+        def make_h(n):
+            quant_w1(n)
+            product1(n)
+
+        def scatter(n, lo, hi):
+            if n < 4:
+                wg = wg_n[:, lo:hi]
+            else:
+                wg = wg_q[PLANE[n - 4]][:, lo:hi]
+            h = h_half(n, lo // HALF) if n in halved else hs[n][:, lo:hi]
+            nc.vector.tensor_tensor(pages[n][:].indirect(idx2[:, lo // 16 : hi // 16]), h, wg, MULT)
 
         def fetch(n, x, lo, hi):
-            nc.vector.tensor_copy(x[:], pages[n][:].indirect(idx3[:, lo // 16 : hi // 16]))
+            nc.vector.tensor_copy(x, pages[n][:].indirect(idx3[:, lo // 16 : hi // 16]))
+
+        def z_plane(n, c):
+            return zb1[c][:].rearrange("p (m t) -> p t m", t=4)[:, PLANE[n - 4]]
 
         def rectify(n, x, lo, hi):
             if n < 4:
-                dst, bias = zn[n][:, lo:hi], bias_n[:, n : n + 1]
+                nc.scalar.activation(out=zn[n][:, lo:hi], in_=x, func=RELU, bias=bias_n[:, n : n + 1])
             else:
-                dst, bias = zt[1][:, M * (n - 4) + lo : M * (n - 4) + hi], bias_q[:, n - 4 : n - 3]
-            nc.scalar.activation(out=dst, in_=x[:], func=RELU, bias=bias)
-
-        with tc.tile_pool(name="table", bufs=1) as table:
-            tabw = [table.tile([P, T], I32, name="tabw%d" % a, align_bytes=64) for a in range(KP)]
-
-            def load_table(a):
-                nc.sync.dma_start(out=tabw[a][:], in_=tab_words[a].rearrange("p t i -> p (t i)").bitcast(I32))
-
-            nc.vector.memset(tabs[:].bitcast(I32), 0)
-            nc.vector.memset(w2s[:].bitcast(I32), 0)
-            for q in range(4):
-                nc.gpsimd.dma_start(
-                    out=tabs[32 * q : 32 * q + 4 * KP, :].bitcast(I32),
-                    in_=tab_scales[:, 4 * q : 4 * q + 4, :].bitcast(I32),
-                )
-            nc.sync.dma_start(idx1[:], offs)
-            load_table(0)
-            load_table(1)
-            load_w1_natural(0)
-            load_table(2)
-            nc.sync.dma_start(idx2[:], offs2)
-            load_page(0)
-            nc.sync.dma_start(out=wg_n[:, 0:512], in_=wgs[:, 0:512])
-            load_w1_natural(1)
-            nc.sync.dma_start(out=wg_n[:, 512:S], in_=wgs[:, 512:S])
-
-            nc.vector.tensor_copy(gs[:], tabs[:].indirect(idx1[:]))
-            for a in range(KP):
-                parts = 2 if a == KP - 1 else 1
-                w = S // parts
-                for i in range(parts):
-                    nc.vector.tensor_copy(
-                        gt[a][:, i * w : (i + 1) * w],
-                        tabw[a][:].bitcast(U32).indirect(idx1[:, i * w // 16 : (i + 1) * w // 16]),
+                t = PLANE[n - 4]
+                for c in range(3):
+                    nc.scalar.activation(
+                        out=z_plane(n, c), in_=x[:, CUTS[c] : CUTS[c + 1]], func=RELU, bias=bias_q[:, t : t + 1]
                     )
 
-        late = ctx.enter_context(tc.tile_pool(name="late", bufs=1))
-        pages = pages + [late.tile([P, T2], F32, name="page%d" % n, align_bytes=64) for n in range(4, TILES)]
-        zt = [zt0, late.tile([P, 4 * M], BF16, name="zt1", align_bytes=64)]
+        def deal_rows(n):
+            nc.sync.dma_start(out=zt0[32 * n : 32 * (n + 1), :], in_=zn[n][:])
+
+        nc.vector.memset(tabs[:].bitcast(I32), 0)
+        nc.vector.memset(w2s[:].bitcast(I32), 0)
+        for q in range(4):
+            nc.gpsimd.dma_start(
+                out=tabs[32 * q : 32 * q + 4 * KP, :].bitcast(I32),
+                in_=tab_scales[:, 4 * q : 4 * q + 4, :].bitcast(I32),
+            )
+        nc.sync.dma_start(idx1[:], offs)
+        load_table(0)
+        load_table(1)
+        load_w1_natural(0)
+        load_table(2)
+        nc.sync.dma_start(idx2[:], offs2)
+        load_page(0)
+        nc.sync.dma_start(out=wg_n[:, 0:HALF], in_=wgs[:, 0:HALF])
+        load_w1_natural(1)
+        nc.sync.dma_start(out=wg_n[:, HALF:S], in_=wgs[:, HALF:S])
+
+        for a in range(KP):
+            parts = 2 if a == KP - 1 else 1
+            if a == KP - 1:
+                nc.vector.tensor_copy(gs[:], tabs[:].indirect(idx1[:]))
+            w = S // parts
+            for i in range(parts):
+                nc.vector.tensor_copy(
+                    gt[a][:, i * w : (i + 1) * w],
+                    tabw[a][:].bitcast(U32).indirect(idx1[:, i * w // 16 : (i + 1) * w // 16]),
+                )
 
         load_w1_natural(2)
         nc.sync.dma_start(idx3[:], offs3)
@@ -214,27 +241,14 @@ def tile_list_pacing_board_kernel(
         with nc.allow_non_contiguous_dma(reason="one bias value a partition"):
             nc.sync.dma_start(out=bias_n[:], in_=b[0:512].rearrange("(g p) -> p g", p=P))
         load_w1_natural(3)
-        load_w1_quad(0)
         load_page(2)
-        load_w1_quad(1)
-        load_w1_quad(2)
+        for a in range(KP):
+            load_w1_quad(a)
+        load_wg_quad(4)
         load_page(3)
-        for q in (0, 2, 1, 3):
-            nc.sync.dma_start(out=wg_q[32 * q : 32 * (q + 1), :], in_=wgs.rearrange("(u t) j -> u (t j)", t=4))
         nc.sync.dma_start(out=bias_q[:], in_=b[512:1024].rearrange("(p t) -> p t", t=4))
         load_page(4)
-        nc.sync.dma_start(out=w2w[:].bitcast(I32), in_=w2_words.rearrange("a p c -> p a c").bitcast(I32))
-        for q in range(4):
-            nc.sync.dma_start(
-                out=w2s[32 * q : 32 * q + 4, :, :].bitcast(I32),
-                in_=w2_scales[:, 4 * q : 4 * q + 4, :].rearrange("a r c -> r a c").bitcast(I32),
-            )
-
-        def interleave(engine_copy, dst, a, lo, hi):
-            engine_copy(
-                out=dst.rearrange("p (c i t) -> p c t i", i=4, t=4),
-                in_=zt[a][:].rearrange("p (t m) -> p t m", t=4)[:, :, lo:hi].rearrange("p t (c i) -> p c t i", i=4),
-            )
+        load_wg_quad(5)
 
         def out_bank(c, i):
             return banks[(4 + 3 * c + i) % 8]
@@ -255,81 +269,106 @@ def tile_list_pacing_board_kernel(
                             stop=(a == 1 and j == 1 and h == 1),
                         )
 
-        cast_w1(0)
-        quant_w1(0)
-        product1(0)
-        copy_h(0)
-        cast_w1(1)
-        cast_w1(2)
-        for n in range(6):
-            scatter(n)
-            quant_w1(n + 2)
-            product1(n + 2)
-            copy_h(n + 1)
-            fetch(n, xs[n], 0, M)
-            rectify(n, xs[n], 0, M)
-            if n + 3 < TILES:
-                cast_w1(n + 3)
-            if n < 4:
-                for t in range(4):
-                    nc.sync.dma_start(out=zt[0][32 * n : 32 * (n + 1), M * t : M * (t + 1)], in_=zn[n][t:P:4, :])
-            if n == 3:
-                for later in range(5, TILES):
-                    load_page(later)
-        for c in range(CHUNKS):
-            interleave(nc.scalar.copy, zb0[:, 4 * CH * c : 4 * CH * (c + 1)], 0, CH * c, CH * (c + 1))
-        scatter(6)
-        copy_h(7)
-        fetch(6, x6[0], 0, 2 * CH)
-        rectify(6, x6[0], 0, 2 * CH)
-        scatter(7)
-        product2(0, 0, range(3))
-        product2(1, 0, range(3))
-        product2(2, 0, range(2))
+        def wide_bank(nt):
+            return banks[2 + nt]
 
-        def finish(c, i):
-            stage = raw_n[c][i][:]
-            if c >= 2 and (c + i) % 2 == 0:
-                nc.vector.tensor_copy(out=stage, in_=out_bank(c, i)[:])
-            else:
-                nc.scalar.copy(out=stage, in_=out_bank(c, i)[:])
-            nc.sync.dma_start(
-                out=out[2 * P * i : 2 * P * (i + 1), CH * c : CH * (c + 1)].rearrange("(j p) m -> p j m", p=P),
-                in_=stage.rearrange("p (j m) -> p j m", j=2),
+        def product2_wide(nt, a):
+            nc.tensor.matmul_mx(
+                out=wide_bank(nt)[:],
+                lhsT=w2w[:, a, 2 * P * nt : 2 * P * (nt + 1)].bitcast(FP4X4),
+                lhsT_scale=w2s[:, a, P * nt : P * (nt + 1)],
+                rhs=zc[a][:, HALF:M].bitcast(FP8X4),
+                rhs_scale=zs[a][:, HALF:M],
+                start=(a == 0),
+                stop=(a == 1),
             )
 
-        def second_pass(c):
-            lo, hi = CH * c, CH * (c + 1)
-            interleave(nc.scalar.copy if c == 1 else nc.vector.tensor_copy, zb1[c][:], 1, lo, hi)
-            nc.vector.quantize_mx(out=zc[1][:, lo:hi].bitcast(FP8X4), scales=zs[1][:, lo:hi], in_=zb1[c][:])
+        def quant_z(a, lo, hi, src):
+            nc.vector.quantize_mx(out=zc[a][:, lo:hi].bitcast(FP8X4), scales=zs[a][:, lo:hi], in_=src)
 
-        def fetch_last(c):
-            if c >= 2:
-                fetch(6, x6[c], CH * c, CH * (c + 1))
-                rectify(6, x6[c], CH * c, CH * (c + 1))
-            fetch(7, x7[c], CH * c, CH * (c + 1))
-            rectify(7, x7[c], CH * c, CH * (c + 1))
+        def fetch_whole(n):
+            fetch(n, xs[n][:], 0, M)
+            rectify(n, xs[n][:], 0, M)
 
-        fetch_last(0)
-        fetch_last(1)
-        second_pass(0)
+        cast_natural(0)
+        make_h(0)
+        cast_natural(1)
+        scatter(0, 0, HALF)
+        scatter(0, HALF, S)
+        make_h(1)
+        fetch_whole(0)
+        cast_natural(2)
+        cast_natural(3)
+        scatter(1, 0, HALF)
+        make_h(2)
+        scatter(1, HALF, S)
+        make_h(3)
+        fetch_whole(1)
+        for a in range(KP):
+            cast_quad(a)
+        for n in range(2, TILES - 1):
+            scatter(n, 0, S)
+            if n + 2 < TILES:
+                make_h(n + 2)
+            fetch_whole(n)
+            if n == 3:
+                for early in range(4):
+                    deal_rows(early)
+                load_page(5)
+                load_w2()
+                for later in (6, 7):
+                    load_wg_quad(later)
+                    load_page(later)
+                for c in range(CHUNKS):
+                    nc.scalar.copy(
+                        out=zb0[:, 4 * CH * c : 4 * CH * (c + 1)].rearrange("p (c i t) -> p c t i", i=4, t=4),
+                        in_=zt0[:].rearrange("p (t m) -> p t m", t=4)[:, :, CH * c : CH * (c + 1)].rearrange("p t (c i) -> p c t i", i=4),
+                    )
+        last = TILES - 1
+        scatter(last, 0, HALF)
+        quant_z(0, 0, M, zb0[:])
+        scatter(last, HALF, S)
+        product2(0, 0, range(3))
+        product2(1, 0, range(3))
+        for nt in range(2):
+            product2_wide(nt, 0)
+
+        def finish(c, i):
+            nc.scalar.copy(out=stage[c][i][:], in_=out_bank(c, i)[:])
+            nc.sync.dma_start(
+                out=out[2 * P * i : 2 * P * (i + 1), CH * c : CH * (c + 1)].rearrange("(j p) m -> p j m", p=P),
+                in_=stage[c][i][:].rearrange("p (j m) -> p j m", j=2),
+            )
+
+        def finish_wide(nt):
+            staged = stage[2 + nt // 3][nt % 3][:]
+            if nt % 2 == 0:
+                nc.vector.tensor_copy(out=staged, in_=wide_bank(nt)[:])
+            else:
+                nc.scalar.copy(out=staged, in_=wide_bank(nt)[:])
+            nc.sync.dma_start(out=out[P * nt : P * (nt + 1), HALF:M], in_=staged)
+
+        def last_plane(c):
+            lo, hi = CUTS[c], CUTS[c + 1]
+            fetch(last, x7[c][:], lo, hi)
+            if c == 1:
+                nc.scalar.activation(out=z_plane(last, c), in_=x7[c][:], func=RELU, bias=bias_q[:, 3:4])
+            else:
+                nc.vector.tensor_scalar(z_plane(last, c), x7[c][:], bias_q[:, 3:4], 0.0, ADD, MAX)
+            quant_z(1, lo, hi, zb1[c][:])
+
+        last_plane(0)
         product2(0, 1, range(3))
-        second_pass(1)
+        last_plane(1)
         product2(1, 1, range(3))
-        finish(0, 0)
-        finish(0, 1)
-        finish(0, 2)
-        fetch_last(2)
-        fetch_last(3)
-        second_pass(2)
-        second_pass(3)
-        product2(2, 0, (2,))
-        product2(2, 1, range(3))
-        product2(3, 0, range(2))
+        last_plane(2)
         for i in range(3):
-            finish(1, i)
-        product2(3, 0, (2,))
-        product2(3, 1, range(3))
-        for c in (2, 3):
-            for i in range(3):
-                finish(c, i)
+            finish(0, i)
+            product2_wide(2 + i, 0)
+        finish(1, 0)
+        product2_wide(5, 0)
+        finish(1, 1)
+        finish(1, 2)
+        for nt in range(6):
+            product2_wide(nt, 1)
+            finish_wide(nt)

@@ -66,10 +66,13 @@ def tile_list_pacing_board_kernel(
         wg_q = [wt("wg_q%d" % t, wg_at + 4 * KB * (t + 1), [P, S], F32) for t in range(4)]
         wb_n = [wt("wbn%d" % n, wb_at + 3 * KB * n, [P, KP * 512], BF16) for n in range(4)]
         wb_q = wt("wbq", table_at + 16 * KB, [P, 4 * KP * 512], BF16)
-        wc_place = [wc_at, zn_at] + [x_at + 4 * KB * ((n - 1) % 2) for n in range(2, TILES)]
+        more_at = 216 * KB
+        x_place = [x_at + 2 * KB] * 5 + [x_at, x_at + 4 * KB]
+        small_at = more_at + 8 * KB
+        wc_place = [small_at, zn_at, small_at + 2 * KB] + [wc_at + 2 * KB * n for n in range(5)]
         wc = [wt("wc%d" % n, wc_place[n], [P, KP * P], U32) for n in range(TILES)]
 
-        halved = (0, 1, TILES - 1)
+        halved = (0,)
 
         def h_place(n, hh=0):
             return h_at + 4 * KB * (n % 2) + 2 * KB * hh
@@ -80,21 +83,22 @@ def tile_list_pacing_board_kernel(
             else wt("h%d" % n, h_place(n), [P, S], F32)
             for n in range(TILES)
         ]
-        ws_at = [misc_at, h_place(0, 1), h_place(1, 0), h_place(1, 1)] + [h_place(n) for n in range(4, TILES)]
+        ws_at = [misc_at, h_place(0, 0), h_place(0, 0) + 512, small_at + 8 * KB]
+        ws_at = ws_at + [small_at + 6 * KB + 512 * n for n in range(3)] + [small_at + 6 * KB + 1536]
         ws = [wt("ws%d" % n, ws_at[n], [P, KP * P], U8) for n in range(TILES)]
-        xs = [wt("x%d" % n, x_at + 4 * KB * (n % 2), [P, M], F32) for n in range(TILES - 1)]
-        x7_at = (x_at + 4 * KB, x_at + 5 * KB, rawq_at)
+        xs = [wt("x%d" % n, x_place[n], [P, M], F32) for n in range(TILES - 1)]
+        x7_at = (x_at, x_at + KB, rawq_at)
         x7 = [wt("x7_%d" % c, x7_at[c], [P, CUTS[c + 1] - CUTS[c]], F32) for c in range(3)]
-        zn = [wt("zn%d" % n, rawq_at + 18 * KB if n == 2 else zn_at + 2 * KB * n, [P, M], BF16) for n in range(4)]
+        zn = [wt("zn%d" % n, rawq_at + 18 * KB if n == 1 else zn_at + 2 * KB * n, [P, M], BF16) for n in range(4)]
         zt0 = wt("zt0", rawn_at, [P, 4 * M], BF16)
         zb0 = wt("zb0", rawn_at + 12 * KB, [P, 4 * M], BF16)
         zb1 = [wt("zb1_%d" % c, rawq_at + 8 * CUTS[c], [P, 4 * (CUTS[c + 1] - CUTS[c])], BF16) for c in range(3)]
         zc = [wt("zc%d" % a, rawq_at + 8 * KB + 4 * KB * a, [P, M], U32) for a in range(2)]
-        zs = [wt("zs0", h_place(TILES - 1, 0), [P, M], U8), wt("zs1", rawq_at + 16 * KB, [P, M], U8)]
+        zs = [wt("zs0", wg_at + 4 * KB * (PLANE[1] + 1), [P, M], U8), wt("zs1", rawq_at + 16 * KB, [P, M], U8)]
         stage = [[wt("st%d_%d" % (c, i), rawn_at + 2 * KB * (3 * c + i), [P, 512], F32) for i in range(3)] for c in range(CHUNKS)]
         w2w = wt("w2w", misc_at + 512, [P, 2, 2 * N], U8)
         w2s = wt("w2s", misc_at + 512 + 3 * KB, [P, 2, N], U8)
-        bias_n = wt("bias_n", misc_at + 5 * KB, [P, 4], F32)
+        bias_n = [wt("bias_n%d" % n, misc_at + 5 * KB + 128 + 64 * n, [P, 1], F32) for n in range(4)]
         bias_q = wt("bias_q", misc_at + 5 * KB + 64, [P, 4], F32)
 
         def h_half(n, hh):
@@ -128,6 +132,13 @@ def tile_list_pacing_board_kernel(
             for q in (0, 2, 1, 3):
                 nc.sync.dma_start(out=wg_q[t][32 * q : 32 * (q + 1), :], in_=wgs.rearrange("(u t) j -> t u j", t=4)[t])
 
+        def load_bias(n):
+            with nc.allow_non_contiguous_dma(reason="one bias value a partition"):
+                if n < 4:
+                    nc.sync.dma_start(out=bias_n[n][:], in_=b[P * n : P * (n + 1)].rearrange("(p g) -> p g", g=1))
+                else:
+                    nc.sync.dma_start(out=bias_q[:], in_=b[512:1024].rearrange("(p t) -> p t", t=4))
+
         def load_w2():
             nc.sync.dma_start(out=w2w[:].bitcast(I32), in_=w2_words.rearrange("a p c -> p a c").bitcast(I32))
             for q in range(4):
@@ -138,10 +149,8 @@ def tile_list_pacing_board_kernel(
 
         def cast_natural(n):
             for a in range(KP):
-                nc.scalar.copy(
-                    out=wb_n[n][:, 512 * a : 512 * (a + 1)].rearrange("p (c i j) -> p c j i", i=4, j=4),
-                    in_=raw_n[n][a][:].rearrange("p (j c i) -> p c j i", j=4, i=4),
-                )
+                src = raw_n[n][a][:].rearrange("p (j c i) -> p c j i", j=4, i=4)
+                nc.scalar.copy(out=wb_n[n][:, 512 * a : 512 * (a + 1)].rearrange("p (c i j) -> p c j i", i=4, j=4), in_=src)
 
         def cast_quad(a):
             nc.scalar.copy(
@@ -151,7 +160,7 @@ def tile_list_pacing_board_kernel(
 
         def quant_w1(n):
             src = wb_n[n][:] if n < 4 else wb_q[:, 1536 * PLANE[n - 4] : 1536 * (PLANE[n - 4] + 1)]
-            cuts = (0, 1, 2, 3) if n == 0 else (0, 2, 3)
+            cuts = (0, 1, 2, 3) if n < 2 else (0, 2, 3)
             for lo, hi in zip(cuts, cuts[1:]):
                 nc.vector.quantize_mx(
                     out=wc[n][:, P * lo : P * hi].bitcast(FP8X4),
@@ -195,7 +204,7 @@ def tile_list_pacing_board_kernel(
 
         def rectify(n, x, lo, hi):
             if n < 4:
-                nc.scalar.activation(out=zn[n][:, lo:hi], in_=x, func=RELU, bias=bias_n[:, n : n + 1])
+                nc.scalar.activation(out=zn[n][:, lo:hi], in_=x, func=RELU, bias=bias_n[n][:])
             else:
                 t = PLANE[n - 4]
                 for c in range(3):
@@ -204,7 +213,7 @@ def tile_list_pacing_board_kernel(
                     )
 
         def deal_rows(n):
-            nc.sync.dma_start(out=zt0[32 * n : 32 * (n + 1), :], in_=zn[n][:])
+            nc.gpsimd.dma_start(out=zt0[32 * n : 32 * (n + 1), :], in_=zn[n][:])
 
         nc.vector.memset(tabs[:].bitcast(I32), 0)
         nc.vector.memset(w2s[:].bitcast(I32), 0)
@@ -238,17 +247,23 @@ def tile_list_pacing_board_kernel(
         load_w1_natural(2)
         nc.sync.dma_start(idx3[:], offs3)
         load_page(1)
-        with nc.allow_non_contiguous_dma(reason="one bias value a partition"):
-            nc.sync.dma_start(out=bias_n[:], in_=b[0:512].rearrange("(g p) -> p g", p=P))
         load_w1_natural(3)
         load_page(2)
+        load_bias(0)
         for a in range(KP):
             load_w1_quad(a)
         load_wg_quad(4)
         load_page(3)
-        nc.sync.dma_start(out=bias_q[:], in_=b[512:1024].rearrange("(p t) -> p t", t=4))
+        load_bias(1)
         load_page(4)
-        load_wg_quad(5)
+        load_bias(2)
+        for later in range(5, TILES):
+            load_wg_quad(later)
+            load_page(later)
+            if later < TILES - 1:
+                load_bias(later - 2)
+            else:
+                load_w2()
 
         def out_bank(c, i):
             return banks[(4 + 3 * c + i) % 8]
@@ -289,45 +304,43 @@ def tile_list_pacing_board_kernel(
         def fetch_whole(n):
             fetch(n, xs[n][:], 0, M)
             rectify(n, xs[n][:], 0, M)
+            if n < 4:
+                deal_rows(n)
 
         cast_natural(0)
         make_h(0)
         cast_natural(1)
         scatter(0, 0, HALF)
-        scatter(0, HALF, S)
         make_h(1)
-        fetch_whole(0)
+        scatter(0, HALF, S)
         cast_natural(2)
-        cast_natural(3)
-        scatter(1, 0, HALF)
+        fetch_whole(0)
         make_h(2)
-        scatter(1, HALF, S)
+        cast_natural(3)
+        scatter(1, 0, S)
         make_h(3)
-        fetch_whole(1)
         for a in range(KP):
             cast_quad(a)
-        for n in range(2, TILES - 1):
+        scatter(2, 0, S)
+        fetch_whole(1)
+        for n in range(4, TILES):
+            quant_w1(n)
+        product1(4)
+        for n in range(3, 7):
             scatter(n, 0, S)
             if n + 2 < TILES:
-                make_h(n + 2)
-            fetch_whole(n)
-            if n == 3:
-                for early in range(4):
-                    deal_rows(early)
-                load_page(5)
-                load_w2()
-                for later in (6, 7):
-                    load_wg_quad(later)
-                    load_page(later)
+                product1(n + 2)
+            fetch_whole(n - 1)
+            if n == 4:
                 for c in range(CHUNKS):
                     nc.scalar.copy(
                         out=zb0[:, 4 * CH * c : 4 * CH * (c + 1)].rearrange("p (c i t) -> p c t i", i=4, t=4),
                         in_=zt0[:].rearrange("p (t m) -> p t m", t=4)[:, :, CH * c : CH * (c + 1)].rearrange("p t (c i) -> p c t i", i=4),
                     )
-        last = TILES - 1
-        scatter(last, 0, HALF)
+        fetch_whole(6)
         quant_z(0, 0, M, zb0[:])
-        scatter(last, HALF, S)
+        last = TILES - 1
+        scatter(last, 0, S)
         product2(0, 0, range(3))
         product2(1, 0, range(3))
         for nt in range(2):

@@ -80,7 +80,7 @@ def tile_list_pacing_board_kernel(
         hs = [
             [wt("h%d_%d" % (n, hh), h_place(n, hh), [P, HALF], F32) for hh in range(2)]
             if n in halved
-            else wt("h%d" % n, h_place(n), [P, S], F32)
+            else wt("h%d" % n, {3: rawq_at, 7: rawn_at}.get(n, h_place(n)), [P, S], F32)
             for n in range(TILES)
         ]
         ws_at = [misc_at, h_place(0, 0), h_place(0, 0) + 512, small_at + 8 * KB]
@@ -109,7 +109,7 @@ def tile_list_pacing_board_kernel(
 
         def load_w1_natural(n):
             for a in range(KP):
-                nc.sync.dma_start(
+                (nc.scalar if n == 0 else nc.sync).dma_start(
                     out=raw_n[n][a][:].rearrange("p (j c) -> p j c", j=4),
                     in_=w1[512 * a : 512 * (a + 1), P * n : P * (n + 1)].rearrange("(p j) c -> p j c", j=4),
                 )
@@ -250,11 +250,12 @@ def tile_list_pacing_board_kernel(
         load_w1_natural(3)
         load_page(2)
         load_bias(0)
-        for a in range(KP):
-            load_w1_quad(a)
-        load_wg_quad(4)
+        load_w1_quad(0)
+        load_w1_quad(1)
         load_page(3)
         load_bias(1)
+        load_w1_quad(2)
+        load_wg_quad(4)
         load_page(4)
         load_bias(2)
         for later in range(5, TILES):
@@ -262,8 +263,7 @@ def tile_list_pacing_board_kernel(
             load_page(later)
             if later < TILES - 1:
                 load_bias(later - 2)
-            else:
-                load_w2()
+        load_w2()
 
         def out_bank(c, i):
             return banks[(4 + 3 * c + i) % 8]
@@ -318,16 +318,18 @@ def tile_list_pacing_board_kernel(
         make_h(2)
         cast_natural(3)
         scatter(1, 0, S)
+        cast_quad(0)
         make_h(3)
-        for a in range(KP):
-            cast_quad(a)
+        cast_quad(1)
+        cast_quad(2)
         scatter(2, 0, S)
         fetch_whole(1)
-        for n in range(4, TILES):
-            quant_w1(n)
-        product1(4)
         for n in range(3, 7):
             scatter(n, 0, S)
+            if n == 3:
+                for later in range(4, TILES):
+                    quant_w1(later)
+                product1(4)
             if n + 2 < TILES:
                 product1(n + 2)
             fetch_whole(n - 1)

@@ -87,14 +87,16 @@ def tile_list_pacing_board_kernel(
         ws_at = ws_at + [small_at + 6 * KB + 512 * n for n in range(3)] + [small_at + 6 * KB + 1536]
         ws = [wt("ws%d" % n, ws_at[n], [P, KP * P], U8) for n in range(TILES)]
         xs = [wt("x%d" % n, x_place[n], [P, M], F32) for n in range(TILES - 1)]
-        x7_at = (x_at, x_at + KB, rawq_at)
+        x7_at = (x_at, x_at + 2 * KB, rawq_at)
         x7 = [wt("x7_%d" % c, x7_at[c], [P, CUTS[c + 1] - CUTS[c]], F32) for c in range(3)]
         zn = [wt("zn%d" % n, rawq_at + 18 * KB if n == 1 else zn_at + 2 * KB * n, [P, M], BF16) for n in range(4)]
         zt0 = wt("zt0", rawn_at, [P, 4 * M], BF16)
         zb0 = wt("zb0", rawn_at + 12 * KB, [P, 4 * M], BF16)
         zb1 = [wt("zb1_%d" % c, rawq_at + 8 * CUTS[c], [P, 4 * (CUTS[c + 1] - CUTS[c])], BF16) for c in range(3)]
-        zc = [wt("zc%d" % a, rawq_at + 8 * KB + 4 * KB * a, [P, M], U32) for a in range(2)]
-        zs = [wt("zs0", wg_at + 4 * KB * (PLANE[1] + 1), [P, M], U8), wt("zs1", rawq_at + 16 * KB, [P, M], U8)]
+        zc_at = [[rawq_at + 8 * KB, x_at], [rawq_at + 12 * KB, rawq_at + 14 * KB]]
+        zc = [[wt("zc%d_%d" % (a, hh), zc_at[a][hh], [P, HALF], U32) for hh in range(2)] for a in range(2)]
+        zs_at = [[wg_at + 4 * KB * (PLANE[1] + 1), rawq_at + 16 * KB], [rawq_at + 17 * KB, rawq_at + 17 * KB + HALF]]
+        zs = [[wt("zs%d_%d" % (a, hh), zs_at[a][hh], [P, HALF], U8) for hh in range(2)] for a in range(2)]
         stage = [[wt("st%d_%d" % (c, i), rawn_at + 2 * KB * (3 * c + i), [P, 512], F32) for i in range(3)] for c in range(CHUNKS)]
         w2w = wt("w2w", misc_at + 512, [P, 2, 2 * N], U8)
         w2s = wt("w2s", misc_at + 512 + 3 * KB, [P, 2, N], U8)
@@ -109,7 +111,7 @@ def tile_list_pacing_board_kernel(
 
         def load_w1_natural(n):
             for a in range(KP):
-                (nc.scalar if n == 0 else nc.sync).dma_start(
+                nc.sync.dma_start(
                     out=raw_n[n][a][:].rearrange("p (j c) -> p j c", j=4),
                     in_=w1[512 * a : 512 * (a + 1), P * n : P * (n + 1)].rearrange("(p j) c -> p j c", j=4),
                 )
@@ -278,8 +280,8 @@ def tile_list_pacing_board_kernel(
                             out=out_bank(c, i)[:, CH * j + P * h : CH * j + P * (h + 1)],
                             lhsT=w2w[:, a, 2 * P * nt : 2 * P * (nt + 1)].bitcast(FP4X4),
                             lhsT_scale=w2s[:, a, P * nt : P * (nt + 1)],
-                            rhs=zc[a][:, cols].bitcast(FP8X4),
-                            rhs_scale=zs[a][:, cols],
+                            rhs=zc[a][0][:, cols].bitcast(FP8X4),
+                            rhs_scale=zs[a][0][:, cols],
                             start=(a == 0 and j == 0 and h == 0),
                             stop=(a == 1 and j == 1 and h == 1),
                         )
@@ -292,14 +294,15 @@ def tile_list_pacing_board_kernel(
                 out=wide_bank(nt)[:],
                 lhsT=w2w[:, a, 2 * P * nt : 2 * P * (nt + 1)].bitcast(FP4X4),
                 lhsT_scale=w2s[:, a, P * nt : P * (nt + 1)],
-                rhs=zc[a][:, HALF:M].bitcast(FP8X4),
-                rhs_scale=zs[a][:, HALF:M],
+                rhs=zc[a][1][:].bitcast(FP8X4),
+                rhs_scale=zs[a][1][:],
                 start=(a == 0),
                 stop=(a == 1),
             )
 
         def quant_z(a, lo, hi, src):
-            nc.vector.quantize_mx(out=zc[a][:, lo:hi].bitcast(FP8X4), scales=zs[a][:, lo:hi], in_=src)
+            cols = slice(lo % HALF, lo % HALF + hi - lo)
+            nc.vector.quantize_mx(out=zc[a][lo // HALF][:, cols].bitcast(FP8X4), scales=zs[a][lo // HALF][:, cols], in_=src)
 
         def fetch_whole(n):
             fetch(n, xs[n][:], 0, M)
@@ -340,13 +343,11 @@ def tile_list_pacing_board_kernel(
                         in_=zt0[:].rearrange("p (t m) -> p t m", t=4)[:, :, CH * c : CH * (c + 1)].rearrange("p t (c i) -> p c t i", i=4),
                     )
         fetch_whole(6)
-        quant_z(0, 0, M, zb0[:])
+        quant_z(0, 0, HALF, zb0[:, 0 : 4 * HALF])
         last = TILES - 1
         scatter(last, 0, S)
         product2(0, 0, range(3))
         product2(1, 0, range(3))
-        for nt in range(2):
-            product2_wide(nt, 0)
 
         def finish(c, i):
             nc.scalar.copy(out=stage[c][i][:], in_=out_bank(c, i)[:])
@@ -373,7 +374,10 @@ def tile_list_pacing_board_kernel(
             quant_z(1, lo, hi, zb1[c][:])
 
         last_plane(0)
+        quant_z(0, HALF, M, zb0[:, 4 * HALF : 4 * M])
         product2(0, 1, range(3))
+        for nt in range(2):
+            product2_wide(nt, 0)
         last_plane(1)
         product2(1, 1, range(3))
         last_plane(2)

@@ -67,7 +67,7 @@ def tile_list_pacing_board_kernel(
         wb_n = [wt("wbn%d" % n, wb_at + 3 * KB * n, [P, KP * 512], BF16) for n in range(4)]
         wb_q = wt("wbq", table_at + 16 * KB, [P, 4 * KP * 512], BF16)
         more_at = 216 * KB
-        x_place = [x_at + 2 * KB] * 5 + [x_at, x_at + 4 * KB]
+        x_place = [x_at + 2 * KB] + [x_at + 2 * KB, x_at, x_at + 4 * KB] * 2
         small_at = more_at + 8 * KB
         wc_place = [small_at, zn_at, small_at + 2 * KB] + [wc_at + 2 * KB * n for n in range(5)]
         wc = [wt("wc%d" % n, wc_place[n], [P, KP * P], U32) for n in range(TILES)]
@@ -80,7 +80,7 @@ def tile_list_pacing_board_kernel(
         hs = [
             [wt("h%d_%d" % (n, hh), h_place(n, hh), [P, HALF], F32) for hh in range(2)]
             if n in halved
-            else wt("h%d" % n, {3: rawq_at, 7: rawn_at}.get(n, h_place(n)), [P, S], F32)
+            else wt("h%d" % n, {1: rawn_at + 14 * KB, 3: rawq_at, 7: rawn_at}.get(n, h_place(n)), [P, S], F32)
             for n in range(TILES)
         ]
         ws_at = [misc_at, h_place(0, 0), h_place(0, 0) + 512, small_at + 8 * KB]
@@ -95,7 +95,7 @@ def tile_list_pacing_board_kernel(
         zb1 = [wt("zb1_%d" % c, rawq_at + 8 * CUTS[c], [P, 4 * (CUTS[c + 1] - CUTS[c])], BF16) for c in range(3)]
         zc_at = [[rawq_at + 8 * KB, x_at], [rawq_at + 12 * KB, rawq_at + 14 * KB]]
         zc = [[wt("zc%d_%d" % (a, hh), zc_at[a][hh], [P, HALF], U32) for hh in range(2)] for a in range(2)]
-        zs_at = [[wg_at + 4 * KB * (PLANE[1] + 1), rawq_at + 16 * KB], [rawq_at + 17 * KB, rawq_at + 17 * KB + HALF]]
+        zs_at = [[table_at + 8 * KB, rawq_at + 16 * KB], [rawq_at + 17 * KB, rawq_at + 17 * KB + HALF]]
         zs = [[wt("zs%d_%d" % (a, hh), zs_at[a][hh], [P, HALF], U8) for hh in range(2)] for a in range(2)]
         stage = [[wt("st%d_%d" % (c, i), rawn_at + 2 * KB * (3 * c + i), [P, 512], F32) for i in range(3)] for c in range(CHUNKS)]
         w2w = wt("w2w", misc_at + 512, [P, 2, 2 * N], U8)
@@ -257,14 +257,13 @@ def tile_list_pacing_board_kernel(
         load_page(3)
         load_bias(1)
         load_w1_quad(2)
-        load_wg_quad(4)
-        load_page(4)
         load_bias(2)
-        for later in range(5, TILES):
+        load_bias(3)
+        for later in range(4, TILES):
             load_wg_quad(later)
             load_page(later)
-            if later < TILES - 1:
-                load_bias(later - 2)
+            if later == 6:
+                load_bias(4)
         load_w2()
 
         def out_bank(c, i):
@@ -327,21 +326,25 @@ def tile_list_pacing_board_kernel(
         cast_quad(2)
         scatter(2, 0, S)
         fetch_whole(1)
-        for n in range(3, 7):
-            scatter(n, 0, S)
-            if n == 3:
-                for later in range(4, TILES):
-                    quant_w1(later)
-                product1(4)
-            if n + 2 < TILES:
-                product1(n + 2)
-            fetch_whole(n - 1)
-            if n == 4:
-                for c in range(CHUNKS):
-                    nc.scalar.copy(
-                        out=zb0[:, 4 * CH * c : 4 * CH * (c + 1)].rearrange("p (c i t) -> p c t i", i=4, t=4),
-                        in_=zt0[:].rearrange("p (t m) -> p t m", t=4)[:, :, CH * c : CH * (c + 1)].rearrange("p t (c i) -> p c t i", i=4),
-                    )
+        scatter(3, 0, S)
+        for n in range(4, TILES):
+            quant_w1(n)
+        product1(4)
+        product1(5)
+        fetch_whole(2)
+        fetch_whole(3)
+        scatter(4, 0, S)
+        product1(6)
+        fetch_whole(4)
+        for c in range(CHUNKS):
+            nc.scalar.copy(
+                out=zb0[:, 4 * CH * c : 4 * CH * (c + 1)].rearrange("p (c i t) -> p c t i", i=4, t=4),
+                in_=zt0[:].rearrange("p (t m) -> p t m", t=4)[:, :, CH * c : CH * (c + 1)].rearrange("p t (c i) -> p c t i", i=4),
+            )
+        scatter(5, 0, S)
+        product1(7)
+        scatter(6, 0, S)
+        fetch_whole(5)
         fetch_whole(6)
         quant_z(0, 0, HALF, zb0[:, 0 : 4 * HALF])
         last = TILES - 1

@@ -83,7 +83,7 @@ def tile_list_pacing_board_kernel(
             else wt("h%d" % n, {1: rawn_at + 14 * KB, 3: rawq_at, 7: rawn_at}.get(n, h_place(n)), [P, S], F32)
             for n in range(TILES)
         ]
-        ws_at = [misc_at, h_place(0, 0), h_place(0, 0) + 512, small_at + 8 * KB]
+        ws_at = [misc_at] + [small_at + 8 * KB + 512 * n for n in range(3)]
         ws_at = ws_at + [small_at + 6 * KB + 512 * n for n in range(3)] + [small_at + 6 * KB + 1536]
         ws = [wt("ws%d" % n, ws_at[n], [P, KP * P], U8) for n in range(TILES)]
         xs = [wt("x%d" % n, x_place[n], [P, M], F32) for n in range(TILES - 1)]
@@ -93,11 +93,14 @@ def tile_list_pacing_board_kernel(
         zt0 = wt("zt0", rawn_at, [P, 4 * M], BF16)
         zb0 = wt("zb0", rawn_at + 12 * KB, [P, 4 * M], BF16)
         zb1 = [wt("zb1_%d" % c, rawq_at + 8 * CUTS[c], [P, 4 * (CUTS[c + 1] - CUTS[c])], BF16) for c in range(3)]
-        zc_at = [[rawq_at + 8 * KB, x_at], [rawq_at + 12 * KB, rawq_at + 14 * KB]]
-        zc = [[wt("zc%d_%d" % (a, hh), zc_at[a][hh], [P, HALF], U32) for hh in range(2)] for a in range(2)]
-        zs_at = [[table_at + 8 * KB, rawq_at + 16 * KB], [rawq_at + 17 * KB, rawq_at + 17 * KB + HALF]]
-        zs = [[wt("zs%d_%d" % (a, hh), zs_at[a][hh], [P, HALF], U8) for hh in range(2)] for a in range(2)]
-        stage = [[wt("st%d_%d" % (c, i), rawn_at + 2 * KB * (3 * c + i), [P, 512], F32) for i in range(3)] for c in range(CHUNKS)]
+        zc_at = [[wg_at + 4 * KB * (PLANE[3] + 1), x_at, rawq_at + 8 * CUTS[1]], [rawq_at + 12 * KB + 4 * lo for lo in CUTS[:3]]]
+        zc = [[wt("zc%d_%d" % (a, c), zc_at[a][c], [P, CUTS[c + 1] - CUTS[c]], U32) for c in range(3)] for a in range(2)]
+        zs = [
+            [wt("zs%d_%d" % (a, c), rawq_at + (16 + a) * KB + CUTS[c], [P, CUTS[c + 1] - CUTS[c]], U8) for c in range(3)]
+            for a in range(2)
+        ]
+        stage = [[wt("st%d_%d" % (c, i), rawn_at + 2 * KB * (3 * c + i), [P, 512], F32) for i in range(3)] for c in range(2)]
+        stage_wide = [wt("stw%d" % i, rawn_at + 12 * KB + 4 * KB * i, [P, 2 * HALF], F32) for i in range(3)]
         w2w = wt("w2w", misc_at + 512, [P, 2, 2 * N], U8)
         w2s = wt("w2s", misc_at + 512 + 3 * KB, [P, 2, N], U8)
         bias_n = [wt("bias_n%d" % n, misc_at + 5 * KB + 128 + 64 * n, [P, 1], F32) for n in range(4)]
@@ -224,8 +227,8 @@ def tile_list_pacing_board_kernel(
                 out=tabs[32 * q : 32 * q + 4 * KP, :].bitcast(I32),
                 in_=tab_scales[:, 4 * q : 4 * q + 4, :].bitcast(I32),
             )
-        nc.sync.dma_start(idx1[:], offs)
         load_table(0)
+        nc.sync.dma_start(idx1[:], offs)
         load_table(1)
         load_w1_natural(0)
         load_table(2)
@@ -264,7 +267,7 @@ def tile_list_pacing_board_kernel(
             load_page(later)
             if later == 6:
                 load_bias(4)
-        load_w2()
+                load_w2()
 
         def out_bank(c, i):
             return banks[(4 + 3 * c + i) % 8]
@@ -274,13 +277,13 @@ def tile_list_pacing_board_kernel(
                 for j in range(2):
                     nt = 2 * i + j
                     for h in range(2):
-                        cols = slice(CH * c + P * h, CH * c + P * (h + 1))
+                        cols = slice(P * h, P * (h + 1))
                         nc.tensor.matmul_mx(
                             out=out_bank(c, i)[:, CH * j + P * h : CH * j + P * (h + 1)],
                             lhsT=w2w[:, a, 2 * P * nt : 2 * P * (nt + 1)].bitcast(FP4X4),
                             lhsT_scale=w2s[:, a, P * nt : P * (nt + 1)],
-                            rhs=zc[a][0][:, cols].bitcast(FP8X4),
-                            rhs_scale=zs[a][0][:, cols],
+                            rhs=zc[a][c][:, cols].bitcast(FP8X4),
+                            rhs_scale=zs[a][c][:, cols],
                             start=(a == 0 and j == 0 and h == 0),
                             stop=(a == 1 and j == 1 and h == 1),
                         )
@@ -293,15 +296,15 @@ def tile_list_pacing_board_kernel(
                 out=wide_bank(nt)[:],
                 lhsT=w2w[:, a, 2 * P * nt : 2 * P * (nt + 1)].bitcast(FP4X4),
                 lhsT_scale=w2s[:, a, P * nt : P * (nt + 1)],
-                rhs=zc[a][1][:].bitcast(FP8X4),
-                rhs_scale=zs[a][1][:],
+                rhs=zc[a][2][:].bitcast(FP8X4),
+                rhs_scale=zs[a][2][:],
                 start=(a == 0),
                 stop=(a == 1),
             )
 
-        def quant_z(a, lo, hi, src):
-            cols = slice(lo % HALF, lo % HALF + hi - lo)
-            nc.vector.quantize_mx(out=zc[a][lo // HALF][:, cols].bitcast(FP8X4), scales=zs[a][lo // HALF][:, cols], in_=src)
+        def quant_z(a, c):
+            src = zb0[:, 4 * CUTS[c] : 4 * CUTS[c + 1]] if a == 0 else zb1[c][:]
+            nc.vector.quantize_mx(out=zc[a][c][:].bitcast(FP8X4), scales=zs[a][c][:], in_=src)
 
         def fetch_whole(n):
             fetch(n, xs[n][:], 0, M)
@@ -346,11 +349,8 @@ def tile_list_pacing_board_kernel(
         scatter(6, 0, S)
         fetch_whole(5)
         fetch_whole(6)
-        quant_z(0, 0, HALF, zb0[:, 0 : 4 * HALF])
         last = TILES - 1
         scatter(last, 0, S)
-        product2(0, 0, range(3))
-        product2(1, 0, range(3))
 
         def finish(c, i):
             nc.scalar.copy(out=stage[c][i][:], in_=out_bank(c, i)[:])
@@ -359,38 +359,45 @@ def tile_list_pacing_board_kernel(
                 in_=stage[c][i][:].rearrange("p (j m) -> p j m", j=2),
             )
 
-        def finish_wide(nt):
-            staged = stage[2 + nt // 3][nt % 3][:]
-            if nt % 2 == 0:
-                nc.vector.tensor_copy(out=staged, in_=wide_bank(nt)[:])
-            else:
-                nc.scalar.copy(out=staged, in_=wide_bank(nt)[:])
-            nc.sync.dma_start(out=out[P * nt : P * (nt + 1), HALF:M], in_=staged)
+        def finish_wide(i):
+            nc.vector.tensor_copy(out=stage_wide[i][:, 0:HALF], in_=wide_bank(2 * i)[:])
+            nc.scalar.copy(out=stage_wide[i][:, HALF : 2 * HALF], in_=wide_bank(2 * i + 1)[:])
+            nc.sync.dma_start(
+                out=out[2 * P * i : 2 * P * (i + 1), HALF:M].rearrange("(j p) m -> p j m", p=P),
+                in_=stage_wide[i][:].rearrange("p (j m) -> p j m", j=2),
+            )
 
-        def last_plane(c):
-            lo, hi = CUTS[c], CUTS[c + 1]
-            fetch(last, x7[c][:], lo, hi)
+        def fetch_last(c):
+            fetch(last, x7[c][:], CUTS[c], CUTS[c + 1])
+
+        def rectify_last(c):
             if c == 1:
                 nc.scalar.activation(out=z_plane(last, c), in_=x7[c][:], func=RELU, bias=bias_q[:, 3:4])
             else:
                 nc.vector.tensor_scalar(z_plane(last, c), x7[c][:], bias_q[:, 3:4], 0.0, ADD, MAX)
-            quant_z(1, lo, hi, zb1[c][:])
 
-        last_plane(0)
-        quant_z(0, HALF, M, zb0[:, 4 * HALF : 4 * M])
+        fetch_last(0)
+        quant_z(0, 0)
+        product2(0, 0, range(3))
+        rectify_last(0)
+        fetch_last(1)
+        rectify_last(1)
+        quant_z(1, 0)
         product2(0, 1, range(3))
-        for nt in range(2):
-            product2_wide(nt, 0)
-        last_plane(1)
+        quant_z(0, 1)
+        product2(1, 0, range(3))
+        fetch_last(2)
+        quant_z(1, 1)
         product2(1, 1, range(3))
-        last_plane(2)
+        rectify_last(2)
+        quant_z(0, 2)
+        quant_z(1, 2)
         for i in range(3):
             finish(0, i)
-            product2_wide(2 + i, 0)
-        finish(1, 0)
-        product2_wide(5, 0)
-        finish(1, 1)
-        finish(1, 2)
-        for nt in range(6):
-            product2_wide(nt, 1)
-            finish_wide(nt)
+        for i in range(3):
+            finish(1, i)
+        for i in range(3):
+            for a in range(2):
+                product2_wide(2 * i, a)
+                product2_wide(2 * i + 1, a)
+            finish_wide(i)

@@ -53,7 +53,7 @@ def tile_list_pacing_board_kernel(
         tabw = [wt("tabw%d" % a, table_at + 16 * KB * a, [P, T], I32) for a in range(KP)]
         tabs = wt("tabs", scale_at, [P, T], U8)
         gt = [wt("gt%d" % a, picked_at + 4 * KB * a, [P, S], U32) for a in range(2)]
-        gt = gt + [wt("gt2", scale_at, [P, S], U32)]
+        gt_last = [wt("gt2_0", scale_at, [P, HALF], U32), wt("gt2_1", wb_at, [P, HALF], U32)]
         gs = wt("gs", table_at + 28 * KB, [P, S], U8)
         raw_n = [
             [wt("rawn%d_%d" % (n, a), rawn_at + 6 * KB * n + 2 * KB * a, [P, 512], F32) for a in range(KP)]
@@ -69,7 +69,7 @@ def tile_list_pacing_board_kernel(
         more_at = 216 * KB
         x_place = [x_at + 2 * KB] + [x_at + 2 * KB, x_at, x_at + 4 * KB] * 2
         small_at = more_at + 8 * KB
-        wc_place = [small_at, zn_at, small_at + 2 * KB] + [wc_at + 2 * KB * n for n in range(5)]
+        wc_place = [small_at, zn_at, small_at + 2 * KB] + [wc_at + 2 * KB * n for n in range(4)] + [x_at + 6 * KB]
         wc = [wt("wc%d" % n, wc_place[n], [P, KP * P], U32) for n in range(TILES)]
 
         halved = (0,)
@@ -87,13 +87,13 @@ def tile_list_pacing_board_kernel(
         ws_at = ws_at + [small_at + 6 * KB + 512 * n for n in range(3)] + [small_at + 6 * KB + 1536]
         ws = [wt("ws%d" % n, ws_at[n], [P, KP * P], U8) for n in range(TILES)]
         xs = [wt("x%d" % n, x_place[n], [P, M], F32) for n in range(TILES - 1)]
-        x7_at = (x_at, x_at + 2 * KB, rawq_at)
+        x7_at = (x_at, x_at + 2 * KB, x_at)
         x7 = [wt("x7_%d" % c, x7_at[c], [P, CUTS[c + 1] - CUTS[c]], F32) for c in range(3)]
         zn = [wt("zn%d" % n, rawq_at + 18 * KB if n == 1 else zn_at + 2 * KB * n, [P, M], BF16) for n in range(4)]
         zt0 = wt("zt0", rawn_at, [P, 4 * M], BF16)
         zb0 = wt("zb0", rawn_at + 12 * KB, [P, 4 * M], BF16)
         zb1 = [wt("zb1_%d" % c, rawq_at + 8 * CUTS[c], [P, 4 * (CUTS[c + 1] - CUTS[c])], BF16) for c in range(3)]
-        zc_at = [[wg_at + 4 * KB * (PLANE[3] + 1), x_at, rawq_at + 8 * CUTS[1]], [rawq_at + 12 * KB + 4 * lo for lo in CUTS[:3]]]
+        zc_at = [[x_at + 4 * KB, x_at + 5 * KB, rawq_at + 8 * CUTS[1]], [rawq_at + 12 * KB + 4 * lo for lo in CUTS[:3]]]
         zc = [[wt("zc%d_%d" % (a, c), zc_at[a][c], [P, CUTS[c + 1] - CUTS[c]], U32) for c in range(3)] for a in range(2)]
         zs = [
             [wt("zs%d_%d" % (a, c), rawq_at + (16 + a) * KB + CUTS[c], [P, CUTS[c + 1] - CUTS[c]], U8) for c in range(3)]
@@ -103,8 +103,7 @@ def tile_list_pacing_board_kernel(
         stage_wide = [wt("stw%d" % i, rawn_at + 12 * KB + 4 * KB * i, [P, 2 * HALF], F32) for i in range(3)]
         w2w = wt("w2w", misc_at + 512, [P, 2, 2 * N], U8)
         w2s = wt("w2s", misc_at + 512 + 3 * KB, [P, 2, N], U8)
-        bias_n = [wt("bias_n%d" % n, misc_at + 5 * KB + 128 + 64 * n, [P, 1], F32) for n in range(4)]
-        bias_q = wt("bias_q", misc_at + 5 * KB + 64, [P, 4], F32)
+        bias = [wt("bias%d" % n, misc_at + 5 * KB + 64 * n, [P, 1], F32) for n in range(TILES)]
 
         def h_half(n, hh):
             return hs[n][hh][:] if n in halved else hs[n][:, HALF * hh : HALF * (hh + 1)]
@@ -112,8 +111,8 @@ def tile_list_pacing_board_kernel(
         def load_table(a):
             nc.sync.dma_start(out=tabw[a][:], in_=tab_words[a].rearrange("p t i -> p (t i)").bitcast(I32))
 
-        def load_w1_natural(n):
-            for a in range(KP):
+        def load_w1_natural(n, passes=range(KP)):
+            for a in passes:
                 nc.sync.dma_start(
                     out=raw_n[n][a][:].rearrange("p (j c) -> p j c", j=4),
                     in_=w1[512 * a : 512 * (a + 1), P * n : P * (n + 1)].rearrange("(p j) c -> p j c", j=4),
@@ -125,12 +124,12 @@ def tile_list_pacing_board_kernel(
                 in_=w1[512 * a : 512 * (a + 1), 512:1024].rearrange("(p j) c -> p j c", j=4),
             )
 
-        def load_page(n):
+        def load_page(n, lo=0, hi=T2):
             if n < 4:
                 rows = page0[P * n : P * (n + 1), :]
             else:
                 rows = page0[512:1024, :].rearrange("(p t) c -> t p c", t=4)[PLANE[n - 4]]
-            nc.sync.dma_start(out=pages[n][:], in_=rows)
+            nc.sync.dma_start(out=pages[n][:, lo:hi], in_=rows[:, lo:hi])
 
         def load_wg_quad(n):
             t = PLANE[n - 4]
@@ -138,11 +137,12 @@ def tile_list_pacing_board_kernel(
                 nc.sync.dma_start(out=wg_q[t][32 * q : 32 * (q + 1), :], in_=wgs.rearrange("(u t) j -> t u j", t=4)[t])
 
         def load_bias(n):
+            if n < 4:
+                rows = b[P * n : P * (n + 1)].rearrange("(p g) -> p g", g=1)
+            else:
+                rows = b[512:1024].rearrange("(p t) -> p t", t=4)[:, PLANE[n - 4] : PLANE[n - 4] + 1]
             with nc.allow_non_contiguous_dma(reason="one bias value a partition"):
-                if n < 4:
-                    nc.sync.dma_start(out=bias_n[n][:], in_=b[P * n : P * (n + 1)].rearrange("(p g) -> p g", g=1))
-                else:
-                    nc.sync.dma_start(out=bias_q[:], in_=b[512:1024].rearrange("(p t) -> p t", t=4))
+                nc.sync.dma_start(out=bias[n][:], in_=rows)
 
         def load_w2():
             nc.sync.dma_start(out=w2w[:].bitcast(I32), in_=w2_words.rearrange("a p c -> p a c").bitcast(I32))
@@ -181,7 +181,7 @@ def tile_list_pacing_board_kernel(
                         out=banks[2 * (n % 2) + hh][:],
                         lhsT=wc[n][:, P * a : P * (a + 1)].bitcast(FP8X4),
                         lhsT_scale=ws[n][:, P * a : P * (a + 1)],
-                        rhs=gt[a][:, cols].bitcast(FP8X4),
+                        rhs=(gt[a][:, cols] if a < KP - 1 else gt_last[hh][:]).bitcast(FP8X4),
                         rhs_scale=gs[4 * a : P, cols],
                         start=(a == 0),
                         stop=(a == KP - 1),
@@ -209,12 +209,11 @@ def tile_list_pacing_board_kernel(
 
         def rectify(n, x, lo, hi):
             if n < 4:
-                nc.scalar.activation(out=zn[n][:, lo:hi], in_=x, func=RELU, bias=bias_n[n][:])
+                nc.scalar.activation(out=zn[n][:, lo:hi], in_=x, func=RELU, bias=bias[n][:])
             else:
-                t = PLANE[n - 4]
                 for c in range(3):
                     nc.scalar.activation(
-                        out=z_plane(n, c), in_=x[:, CUTS[c] : CUTS[c + 1]], func=RELU, bias=bias_q[:, t : t + 1]
+                        out=z_plane(n, c), in_=x[:, CUTS[c] : CUTS[c + 1]], func=RELU, bias=bias[n][:]
                     )
 
         def deal_rows(n):
@@ -230,24 +229,22 @@ def tile_list_pacing_board_kernel(
         load_table(0)
         nc.sync.dma_start(idx1[:], offs)
         load_table(1)
-        load_w1_natural(0)
+        load_w1_natural(0, (0, 1))
         load_table(2)
+        load_w1_natural(0, (2,))
         nc.sync.dma_start(idx2[:], offs2)
         load_page(0)
         nc.sync.dma_start(out=wg_n[:, 0:HALF], in_=wgs[:, 0:HALF])
         load_w1_natural(1)
         nc.sync.dma_start(out=wg_n[:, HALF:S], in_=wgs[:, HALF:S])
 
-        for a in range(KP):
-            parts = 2 if a == KP - 1 else 1
-            if a == KP - 1:
-                nc.vector.tensor_copy(gs[:], tabs[:].indirect(idx1[:]))
-            w = S // parts
-            for i in range(parts):
-                nc.vector.tensor_copy(
-                    gt[a][:, i * w : (i + 1) * w],
-                    tabw[a][:].bitcast(U32).indirect(idx1[:, i * w // 16 : (i + 1) * w // 16]),
-                )
+        def pick_words(dst, a, lo, hi):
+            nc.vector.tensor_copy(dst, tabw[a][:].bitcast(U32).indirect(idx1[:, lo // 16 : hi // 16]))
+
+        for a in range(KP - 1):
+            pick_words(gt[a][:], a, 0, S)
+        nc.vector.tensor_copy(gs[:], tabs[:].indirect(idx1[:]))
+        pick_words(gt_last[0][:], KP - 1, 0, HALF)
 
         load_w1_natural(2)
         nc.sync.dma_start(idx3[:], offs3)
@@ -261,13 +258,19 @@ def tile_list_pacing_board_kernel(
         load_bias(1)
         load_w1_quad(2)
         load_bias(2)
-        load_bias(3)
-        for later in range(4, TILES):
+        for later in range(4, TILES - 1):
             load_wg_quad(later)
             load_page(later)
+            if later == 4:
+                load_bias(3)
             if later == 6:
-                load_bias(4)
+                for n in (4, 5, 7):
+                    load_bias(n)
                 load_w2()
+        load_wg_quad(7)
+        load_page(7, 0, T2 // 2)
+        load_bias(6)
+        load_page(7, T2 // 2, T2)
 
         def out_bank(c, i):
             return banks[(4 + 3 * c + i) % 8]
@@ -313,7 +316,9 @@ def tile_list_pacing_board_kernel(
                 deal_rows(n)
 
         cast_natural(0)
-        make_h(0)
+        quant_w1(0)
+        pick_words(gt_last[1][:], KP - 1, HALF, S)
+        product1(0)
         cast_natural(1)
         scatter(0, 0, HALF)
         make_h(1)
@@ -330,7 +335,7 @@ def tile_list_pacing_board_kernel(
         scatter(2, 0, S)
         fetch_whole(1)
         scatter(3, 0, S)
-        for n in range(4, TILES):
+        for n in range(4, TILES - 1):
             quant_w1(n)
         product1(4)
         product1(5)
@@ -338,6 +343,7 @@ def tile_list_pacing_board_kernel(
         fetch_whole(3)
         scatter(4, 0, S)
         product1(6)
+        quant_w1(7)
         fetch_whole(4)
         for c in range(CHUNKS):
             nc.scalar.copy(
@@ -372,19 +378,19 @@ def tile_list_pacing_board_kernel(
 
         def rectify_last(c):
             if c == 1:
-                nc.scalar.activation(out=z_plane(last, c), in_=x7[c][:], func=RELU, bias=bias_q[:, 3:4])
+                nc.scalar.activation(out=z_plane(last, c), in_=x7[c][:], func=RELU, bias=bias[last][:])
             else:
-                nc.vector.tensor_scalar(z_plane(last, c), x7[c][:], bias_q[:, 3:4], 0.0, ADD, MAX)
+                nc.vector.tensor_scalar(z_plane(last, c), x7[c][:], bias[last][:], 0.0, ADD, MAX)
 
-        fetch_last(0)
         quant_z(0, 0)
         product2(0, 0, range(3))
+        fetch_last(0)
+        quant_z(0, 1)
         rectify_last(0)
         fetch_last(1)
         rectify_last(1)
         quant_z(1, 0)
         product2(0, 1, range(3))
-        quant_z(0, 1)
         product2(1, 0, range(3))
         fetch_last(2)
         quant_z(1, 1)

@@ -89,6 +89,7 @@ def tile_list_pacing_board_kernel(
         xs = [wt("x%d" % n, x_place[n], [P, M], F32) for n in range(TILES - 1)]
         x7_at = (x_at, x_at + 2 * KB, x_at)
         x7 = [wt("x7_%d" % c, x7_at[c], [P, CUTS[c + 1] - CUTS[c]], F32) for c in range(3)]
+        x6_late = wt("x6_late", rawq_at, [P, CH], F32)
         zn = [wt("zn%d" % n, rawq_at + 18 * KB if n == 1 else zn_at + 2 * KB * n, [P, M], BF16) for n in range(4)]
         zt0 = wt("zt0", rawn_at, [P, 4 * M], BF16)
         zb0 = wt("zb0", rawn_at + 12 * KB, [P, 4 * M], BF16)
@@ -212,8 +213,9 @@ def tile_list_pacing_board_kernel(
                 nc.scalar.activation(out=zn[n][:, lo:hi], in_=x, func=RELU, bias=bias[n][:])
             else:
                 for c in range(3):
+                    end = min(hi, CUTS[c + 1])
                     nc.scalar.activation(
-                        out=z_plane(n, c), in_=x[:, CUTS[c] : CUTS[c + 1]], func=RELU, bias=bias[n][:]
+                        out=z_plane(n, c)[:, 0 : end - CUTS[c]], in_=x[:, CUTS[c] : end], func=RELU, bias=bias[n][:]
                     )
 
         def deal_rows(n):
@@ -268,9 +270,9 @@ def tile_list_pacing_board_kernel(
                     load_bias(n)
                 load_w2()
         load_wg_quad(7)
-        load_page(7, 0, T2 // 2)
+        load_page(7, 0, 3 * T2 // 4)
         load_bias(6)
-        load_page(7, T2 // 2, T2)
+        load_page(7, 3 * T2 // 4, T2)
 
         def out_bank(c, i):
             return banks[(4 + 3 * c + i) % 8]
@@ -354,7 +356,8 @@ def tile_list_pacing_board_kernel(
         product1(7)
         scatter(6, 0, S)
         fetch_whole(5)
-        fetch_whole(6)
+        fetch(6, xs[6][:, 0 : 3 * CH], 0, 3 * CH)
+        rectify(6, xs[6][:], 0, 3 * CH)
         last = TILES - 1
         scatter(last, 0, S)
 
@@ -393,12 +396,17 @@ def tile_list_pacing_board_kernel(
         product2(0, 1, range(3))
         product2(1, 0, range(3))
         fetch_last(2)
+        fetch(6, x6_late[:], 3 * CH, M)
         quant_z(1, 1)
         product2(1, 1, range(3))
+        nc.vector.tensor_scalar(z_plane(6, 2)[:, CH : 2 * CH], x6_late[:], bias[6][:], 0.0, ADD, MAX)
         rectify_last(2)
         quant_z(0, 2)
         quant_z(1, 2)
-        for i in range(3):
+        for j in range(2):
+            nc.scalar.copy(out=stage[0][0][:, CH * j : CH * (j + 1)], in_=out_bank(0, 0)[:, CH * j : CH * (j + 1)])
+            nc.sync.dma_start(out=out[P * j : P * (j + 1), 0:CH], in_=stage[0][0][:, CH * j : CH * (j + 1)])
+        for i in range(1, 3):
             finish(0, i)
         for i in range(3):
             finish(1, i)

@@ -25,7 +25,6 @@ TILES = 8
 HALF = 512
 CH = 256
 CHUNKS = M // CH
-CUTS = (0, 256, 512, 1024)
 PLANE = (2, 0, 1, 3)
 
 
@@ -87,21 +86,16 @@ def tile_list_pacing_board_kernel(
         ws_at = ws_at + [small_at + 6 * KB + 512 * n for n in range(3)] + [small_at + 6 * KB + 1536]
         ws = [wt("ws%d" % n, ws_at[n], [P, KP * P], U8) for n in range(TILES)]
         xs = [wt("x%d" % n, x_place[n], [P, M], F32) for n in range(TILES - 1)]
-        x7_at = (x_at, x_at + 2 * KB, x_at)
-        x7 = [wt("x7_%d" % c, x7_at[c], [P, CUTS[c + 1] - CUTS[c]], F32) for c in range(3)]
-        x6_late = wt("x6_late", rawq_at, [P, CH], F32)
+        x7 = [wt("x7_%d" % c, x_at + (2 * KB if c == 1 else 0), [P, CH], F32) for c in range(CHUNKS)]
+        x6_late = {c: wt("x6_late%d" % c, rawq_at, [P, CH], F32) for c in (2, 3)}
         zn = [wt("zn%d" % n, rawq_at + 18 * KB if n == 1 else zn_at + 2 * KB * n, [P, M], BF16) for n in range(4)]
         zt0 = wt("zt0", rawn_at, [P, 4 * M], BF16)
         zb0 = wt("zb0", rawn_at + 12 * KB, [P, 4 * M], BF16)
-        zb1 = [wt("zb1_%d" % c, rawq_at + 8 * CUTS[c], [P, 4 * (CUTS[c + 1] - CUTS[c])], BF16) for c in range(3)]
-        zc_at = [[x_at + 4 * KB, x_at + 5 * KB, rawq_at + 8 * CUTS[1]], [rawq_at + 12 * KB + 4 * lo for lo in CUTS[:3]]]
-        zc = [[wt("zc%d_%d" % (a, c), zc_at[a][c], [P, CUTS[c + 1] - CUTS[c]], U32) for c in range(3)] for a in range(2)]
-        zs = [
-            [wt("zs%d_%d" % (a, c), rawq_at + (16 + a) * KB + CUTS[c], [P, CUTS[c + 1] - CUTS[c]], U8) for c in range(3)]
-            for a in range(2)
-        ]
-        stage = [[wt("st%d_%d" % (c, i), rawn_at + 2 * KB * (3 * c + i), [P, 512], F32) for i in range(3)] for c in range(2)]
-        stage_wide = [wt("stw%d" % i, rawn_at + 12 * KB + 4 * KB * i, [P, 2 * HALF], F32) for i in range(3)]
+        zb1 = [wt("zb1_%d" % c, rawq_at + 2 * KB * c, [P, 4 * CH], BF16) for c in range(CHUNKS)]
+        zc_at = [[x_at + 4 * KB, x_at + 5 * KB, rawq_at + 2 * KB, rawq_at + 4 * KB], [rawq_at + (12 + c) * KB for c in range(CHUNKS)]]
+        zc = [[wt("zc%d_%d" % (a, c), zc_at[a][c], [P, CH], U32) for c in range(CHUNKS)] for a in range(2)]
+        zs = [[wt("zs%d_%d" % (a, c), rawq_at + (16 + a) * KB + CH * c, [P, CH], U8) for c in range(CHUNKS)] for a in range(2)]
+        stage = [[wt("st%d_%d" % (c, i), rawn_at + 2 * KB * (3 * c + i), [P, 512], F32) for i in range(3)] for c in range(CHUNKS)]
         w2w = wt("w2w", misc_at + 512, [P, 2, 2 * N], U8)
         w2s = wt("w2s", misc_at + 512 + 3 * KB, [P, 2, N], U8)
         bias = [wt("bias%d" % n, misc_at + 5 * KB + 64 * n, [P, 1], F32) for n in range(TILES)]
@@ -212,11 +206,8 @@ def tile_list_pacing_board_kernel(
             if n < 4:
                 nc.scalar.activation(out=zn[n][:, lo:hi], in_=x, func=RELU, bias=bias[n][:])
             else:
-                for c in range(3):
-                    end = min(hi, CUTS[c + 1])
-                    nc.scalar.activation(
-                        out=z_plane(n, c)[:, 0 : end - CUTS[c]], in_=x[:, CUTS[c] : end], func=RELU, bias=bias[n][:]
-                    )
+                for c in range(lo // CH, hi // CH):
+                    nc.scalar.activation(out=z_plane(n, c), in_=x[:, CH * c : CH * (c + 1)], func=RELU, bias=bias[n][:])
 
         def deal_rows(n):
             nc.gpsimd.dma_start(out=zt0[32 * n : 32 * (n + 1), :], in_=zn[n][:])
@@ -275,7 +266,7 @@ def tile_list_pacing_board_kernel(
         load_page(7, 3 * T2 // 4, T2)
 
         def out_bank(c, i):
-            return banks[(4 + 3 * c + i) % 8]
+            return banks[(3 * c + i) % 8]
 
         def product2(c, a, which):
             for i in which:
@@ -293,22 +284,8 @@ def tile_list_pacing_board_kernel(
                             stop=(a == 1 and j == 1 and h == 1),
                         )
 
-        def wide_bank(nt):
-            return banks[2 + nt]
-
-        def product2_wide(nt, a):
-            nc.tensor.matmul_mx(
-                out=wide_bank(nt)[:],
-                lhsT=w2w[:, a, 2 * P * nt : 2 * P * (nt + 1)].bitcast(FP4X4),
-                lhsT_scale=w2s[:, a, P * nt : P * (nt + 1)],
-                rhs=zc[a][2][:].bitcast(FP8X4),
-                rhs_scale=zs[a][2][:],
-                start=(a == 0),
-                stop=(a == 1),
-            )
-
         def quant_z(a, c):
-            src = zb0[:, 4 * CUTS[c] : 4 * CUTS[c + 1]] if a == 0 else zb1[c][:]
+            src = zb0[:, 4 * CH * c : 4 * CH * (c + 1)] if a == 0 else zb1[c][:]
             nc.vector.quantize_mx(out=zc[a][c][:].bitcast(FP8X4), scales=zs[a][c][:], in_=src)
 
         def fetch_whole(n):
@@ -356,28 +333,23 @@ def tile_list_pacing_board_kernel(
         product1(7)
         scatter(6, 0, S)
         fetch_whole(5)
-        fetch(6, xs[6][:, 0 : 3 * CH], 0, 3 * CH)
-        rectify(6, xs[6][:], 0, 3 * CH)
+        fetch(6, xs[6][:, 0:HALF], 0, HALF)
+        rectify(6, xs[6][:], 0, HALF)
         last = TILES - 1
         scatter(last, 0, S)
 
         def finish(c, i):
-            nc.scalar.copy(out=stage[c][i][:], in_=out_bank(c, i)[:])
+            if c == CHUNKS - 1 and i != 1:
+                nc.vector.tensor_copy(out=stage[c][i][:], in_=out_bank(c, i)[:])
+            else:
+                nc.scalar.copy(out=stage[c][i][:], in_=out_bank(c, i)[:])
             nc.sync.dma_start(
                 out=out[2 * P * i : 2 * P * (i + 1), CH * c : CH * (c + 1)].rearrange("(j p) m -> p j m", p=P),
                 in_=stage[c][i][:].rearrange("p (j m) -> p j m", j=2),
             )
 
-        def finish_wide(i):
-            nc.vector.tensor_copy(out=stage_wide[i][:, 0:HALF], in_=wide_bank(2 * i)[:])
-            nc.scalar.copy(out=stage_wide[i][:, HALF : 2 * HALF], in_=wide_bank(2 * i + 1)[:])
-            nc.sync.dma_start(
-                out=out[2 * P * i : 2 * P * (i + 1), HALF:M].rearrange("(j p) m -> p j m", p=P),
-                in_=stage_wide[i][:].rearrange("p (j m) -> p j m", j=2),
-            )
-
         def fetch_last(c):
-            fetch(last, x7[c][:], CUTS[c], CUTS[c + 1])
+            fetch(last, x7[c][:], CH * c, CH * (c + 1))
 
         def rectify_last(c):
             if c == 1:
@@ -395,14 +367,16 @@ def tile_list_pacing_board_kernel(
         quant_z(1, 0)
         product2(0, 1, range(3))
         product2(1, 0, range(3))
-        fetch_last(2)
-        fetch(6, x6_late[:], 3 * CH, M)
-        quant_z(1, 1)
-        product2(1, 1, range(3))
-        nc.vector.tensor_scalar(z_plane(6, 2)[:, CH : 2 * CH], x6_late[:], bias[6][:], 0.0, ADD, MAX)
-        rectify_last(2)
-        quant_z(0, 2)
-        quant_z(1, 2)
+        for c in (2, 3):
+            fetch_last(c)
+            fetch(6, x6_late[c][:], CH * c, CH * (c + 1))
+            if c == 2:
+                quant_z(1, 1)
+                product2(1, 1, range(3))
+            rectify_last(c)
+            nc.vector.tensor_scalar(z_plane(6, c), x6_late[c][:], bias[6][:], 0.0, ADD, MAX)
+            quant_z(0, c)
+            quant_z(1, c)
         for j in range(2):
             nc.scalar.copy(out=stage[0][0][:, CH * j : CH * (j + 1)], in_=out_bank(0, 0)[:, CH * j : CH * (j + 1)])
             nc.sync.dma_start(out=out[P * j : P * (j + 1), 0:CH], in_=stage[0][0][:, CH * j : CH * (j + 1)])
@@ -410,8 +384,8 @@ def tile_list_pacing_board_kernel(
             finish(0, i)
         for i in range(3):
             finish(1, i)
-        for i in range(3):
-            for a in range(2):
-                product2_wide(2 * i, a)
-                product2_wide(2 * i + 1, a)
-            finish_wide(i)
+        for c in (2, 3):
+            for i in range(3):
+                product2(c, 0, (i,))
+                product2(c, 1, (i,))
+                finish(c, i)

@@ -1,6 +1,7 @@
 from contextlib import ExitStack
 
 import concourse.mybir as mybir
+from concourse.masks import make_identity
 
 K, T, S, H, T2, M, N = 1536, 4096, 1024, 1024, 2048, 1024, 768
 FLOPS = 2 * K * H * S + 2 * H * N * M
@@ -25,7 +26,9 @@ TILES = 8
 HALF = 512
 CH = 256
 CHUNKS = M // CH
-PLANE = (2, 0, 1, 3)
+PLANE = (3, 0, 1, 2)
+W1C = KP * P
+SCALE_AT = (0, 48, 64, 112)
 
 
 def tile_list_pacing_board_kernel(
@@ -42,72 +45,61 @@ def tile_list_pacing_board_kernel(
         idx3 = keep.tile([P, M // 16], U16, name="idx3", align_bytes=64)
         banks = [psum.tile([P, 512], F32, name="bank%d" % i) for i in range(8)]
 
-        def wt(name, offset, shape, dtype):
-            return work.tile(shape, dtype, name=name, offset=offset, align_bytes=64)
+        def wt(name, kb, shape, dtype):
+            return work.tile(shape, dtype, name=name, offset=int(kb * KB), align_bytes=64)
 
-        table_at, scale_at, picked_at, rawn_at, rawq_at = 0, 48 * KB, 52 * KB, 61 * KB, 85 * KB
-        page_at, wg_at, h_at, x_at, zn_at = 109 * KB, 141 * KB, 161 * KB, 169 * KB, 177 * KB
-        wb_at, wc_at, misc_at = 185 * KB, 197 * KB, 209 * KB
-
-        tabw = [wt("tabw%d" % a, table_at + 16 * KB * a, [P, T], I32) for a in range(KP)]
-        tabs = wt("tabs", scale_at, [P, T], U8)
-        gt = [wt("gt%d" % a, picked_at + 4 * KB * a, [P, S], U32) for a in range(2)]
-        gt_last = [wt("gt2_0", scale_at, [P, HALF], U32), wt("gt2_1", wb_at, [P, HALF], U32)]
-        gs = wt("gs", table_at + 28 * KB, [P, S], U8)
-        raw_n = [
-            [wt("rawn%d_%d" % (n, a), rawn_at + 6 * KB * n + 2 * KB * a, [P, 512], F32) for a in range(KP)]
-            for n in range(4)
-        ]
-        raw_q = [wt("rawq%d" % a, rawq_at + 8 * KB * a, [P, 2048], F32) for a in range(KP)]
-        pages = [wt("page%d" % n, page_at + 8 * KB * n, [P, T2], F32) for n in range(4)]
-        pages = pages + [wt("page%d" % (4 + n), table_at + 8 * KB * n + 16 * KB * (n // 2), [P, T2], F32) for n in range(4)]
-        wg_n = wt("wg_n", wg_at, [P, S], F32)
-        wg_q = [wt("wg_q%d" % t, wg_at + 4 * KB * (t + 1), [P, S], F32) for t in range(4)]
-        wb_n = [wt("wbn%d" % n, wb_at + 3 * KB * n, [P, KP * 512], BF16) for n in range(4)]
-        wb_q = wt("wbq", table_at + 16 * KB, [P, 4 * KP * 512], BF16)
-        more_at = 216 * KB
-        x_place = [x_at + 2 * KB] + [x_at + 2 * KB, x_at, x_at + 4 * KB] * 2
-        small_at = more_at + 8 * KB
-        wc_place = [small_at, zn_at, small_at + 2 * KB] + [wc_at + 2 * KB * n for n in range(4)] + [x_at + 6 * KB]
-        wc = [wt("wc%d" % n, wc_place[n], [P, KP * P], U32) for n in range(TILES)]
-
-        halved = (0,)
-
-        def h_place(n, hh=0):
-            return h_at + 4 * KB * (n % 2) + 2 * KB * hh
-
-        hs = [
-            [wt("h%d_%d" % (n, hh), h_place(n, hh), [P, HALF], F32) for hh in range(2)]
-            if n in halved
-            else wt("h%d" % n, {1: rawn_at + 14 * KB, 3: rawq_at, 7: rawn_at}.get(n, h_place(n)), [P, S], F32)
-            for n in range(TILES)
-        ]
-        ws_at = [misc_at] + [small_at + 8 * KB + 512 * n for n in range(3)]
-        ws_at = ws_at + [small_at + 6 * KB + 512 * n for n in range(3)] + [small_at + 6 * KB + 1536]
-        ws = [wt("ws%d" % n, ws_at[n], [P, KP * P], U8) for n in range(TILES)]
-        xs = [wt("x%d" % n, x_place[n], [P, M], F32) for n in range(TILES - 1)]
-        x7 = [wt("x7_%d" % c, x_at + (2 * KB if c == 1 else 0), [P, CH], F32) for c in range(CHUNKS)]
-        x6_late = {c: wt("x6_late%d" % c, rawq_at, [P, CH], F32) for c in (2, 3)}
-        zn = [wt("zn%d" % n, rawq_at + 18 * KB if n == 1 else zn_at + 2 * KB * n, [P, M], BF16) for n in range(4)]
-        zt0 = wt("zt0", rawn_at, [P, 4 * M], BF16)
-        zb0 = wt("zb0", rawn_at + 12 * KB, [P, 4 * M], BF16)
-        zb1 = [wt("zb1_%d" % c, rawq_at + 2 * KB * c, [P, 4 * CH], BF16) for c in range(CHUNKS)]
-        zc_at = [[x_at + 4 * KB, x_at + 5 * KB, rawq_at + 2 * KB, rawq_at + 4 * KB], [rawq_at + (12 + c) * KB for c in range(CHUNKS)]]
-        zc = [[wt("zc%d_%d" % (a, c), zc_at[a][c], [P, CH], U32) for c in range(CHUNKS)] for a in range(2)]
-        zs = [[wt("zs%d_%d" % (a, c), rawq_at + (16 + a) * KB + CH * c, [P, CH], U8) for c in range(CHUNKS)] for a in range(2)]
-        stage = [[wt("st%d_%d" % (c, i), rawn_at + 2 * KB * (3 * c + i), [P, 512], F32) for i in range(3)] for c in range(CHUNKS)]
-        w2w = wt("w2w", misc_at + 512, [P, 2, 2 * N], U8)
-        w2s = wt("w2s", misc_at + 512 + 3 * KB, [P, 2, N], U8)
-        bias = [wt("bias%d" % n, misc_at + 5 * KB + 64 * n, [P, 1], F32) for n in range(TILES)]
+        tabw = [wt("tabw%d" % a, 16 * a, [P, T], I32) for a in range(KP)]
+        tabs = wt("tabs", 48, [P, T], U8)
+        gt = [wt("gt%d" % a, 52 + 4 * a, [P, S], U32) for a in range(2)]
+        gt_last = [wt("gt2_%d" % hh, 48 + 12 * hh, [P, HALF], U32) for hh in range(2)]
+        gs_raw = wt("gs_raw", 212, [P, S], U8)
+        gs = wt("gs", 213, [P, S], U8)
+        rawn_at = (62, 68, 80, 74)
+        raw_n = [[wt("rawn%d_%d" % (n, a), rawn_at[n] + 2 * a, [P, 512], F32) for a in range(KP)] for n in range(4)]
+        rawq_at = (87, 103, 95)
+        raw_q = [wt("rawq%d" % a, rawq_at[a], [P, 2048], F32) for a in range(KP)]
+        page_at = (111, 119, 127, 135, 0, 8, 32, 40)
+        pages = [wt("page%d" % n, page_at[n], [P, T2], F32) for n in range(TILES)]
+        wg_n = wt("wg_n", 143, [P, S], F32)
+        wg_q = [wt("wg_q%d" % t, 147 + 4 * t, [P, S], F32) for t in range(4)]
+        wb_n = [wt("wbn%d" % n, 171 + 3 * n, [P, KP * 512], BF16) for n in range(4)]
+        wb_q = wt("wbq", 16, [P, 4 * KP * 512], BF16)
+        wc_n = [wt("wc%d" % n, 183 + 1.5 * n, [P, W1C], U32) for n in range(4)]
+        wc_q = wt("wcq", 189, [P, 4 * W1C], U32)
+        ws_n = [wt("ws%d" % n, 195 + 0.5 * n, [P, W1C], U8) for n in range(4)]
+        ws_q = wt("wsq", 197, [P, 4 * W1C], U8)
+        h_halves = [[wt("h0_0", 163, [P, HALF], F32), wt("h0_1", 165, [P, HALF], F32)], [wt("h1_0", 167, [P, HALF], F32), wt("h1_1", 85, [P, HALF], F32)]]
+        h_at = {2: 163, 3: 91, 4: 163, 5: 167, 6: 163, 7: 167}
+        h_whole = {n: wt("h%d" % n, h_at[n], [P, S], F32) for n in range(2, TILES)}
+        x_at = (81, 87, 95, 99, 95, 101)
+        xs = [wt("x%d" % n, x_at[n], [P, M], F32) for n in range(6)]
+        x6_early = wt("x6_early", 99, [P, HALF], F32)
+        x7 = [wt("x7_%d" % c, (207, 209, 70, 205.75)[c], [P, CH], F32) for c in range(CHUNKS)]
+        x6_late = {2: wt("x6_late2", 206.25, [P, CH], F32), 3: wt("x6_late3", 72, [P, CH], F32)}
+        zt = [wt("zt%d" % hf, 62 + 4 * hf, [P, 4 * 512], BF16) for hf in range(2)]
+        zb0 = [wt("zb0_%d" % c, 135 + 2 * c, [P, 4 * CH], BF16) for c in range(CHUNKS)]
+        zb1 = [wt("zb1_%d" % c, 70 + 2 * c, [P, 4 * CH], BF16) for c in range(CHUNKS)]
+        zc0 = [wt("zc0_%d" % c, (99, 100, 207.75, 70.5)[c], [P, CH], U32) for c in range(CHUNKS)]
+        zs0 = [wt("zs0_%d" % c, 175 + 0.25 * c, [P, CH], U8) for c in range(CHUNKS)]
+        zc1 = [wt("zc1_%d" % c, 171 + c, [P, CH], U32) for c in range(CHUNKS)]
+        zs1 = [wt("zs1_%d" % c, 176 + 0.25 * c, [P, CH], U8) for c in range(CHUNKS)]
+        stage = [[wt("st%d_%d" % (c, i), 111 + 2 * (3 * c + i), [P, 512], F32) for i in range(3)] for c in range(CHUNKS)]
+        w2w = wt("w2w", 199, [P, 2, 2 * N], U8)
+        w2s = wt("w2s", 202, [P, 2, N], U8)
+        bias = [wt("bias%d" % n, 204 + n / 16, [P, 1], F32) for n in range(TILES)]
+        ident = wt("ident", 205, [P, P], F32)
 
         def h_half(n, hh):
-            return hs[n][hh][:] if n in halved else hs[n][:, HALF * hh : HALF * (hh + 1)]
+            return h_halves[n][hh][:] if n < 2 else h_whole[n][:, HALF * hh : HALF * (hh + 1)]
+
+        def first_bank(n, hh, lo):
+            return banks[4] if lo else banks[2 * (n % 2) + hh]
 
         def load_table(a):
             nc.sync.dma_start(out=tabw[a][:], in_=tab_words[a].rearrange("p t i -> p (t i)").bitcast(I32))
 
-        def load_w1_natural(n, passes=range(KP)):
-            for a in passes:
+        def load_w1_natural(n):
+            for a in range(KP):
                 nc.sync.dma_start(
                     out=raw_n[n][a][:].rearrange("p (j c) -> p j c", j=4),
                     in_=w1[512 * a : 512 * (a + 1), P * n : P * (n + 1)].rearrange("(p j) c -> p j c", j=4),
@@ -158,42 +150,47 @@ def tile_list_pacing_board_kernel(
                 in_=raw_q[a][:].rearrange("p (j m t) -> p m t j", j=4, t=4),
             )
 
-        def quant_w1(n):
-            src = wb_n[n][:] if n < 4 else wb_q[:, 1536 * PLANE[n - 4] : 1536 * (PLANE[n - 4] + 1)]
-            cuts = (0, 1, 2, 3) if n < 2 else (0, 2, 3)
-            for lo, hi in zip(cuts, cuts[1:]):
-                nc.vector.quantize_mx(
-                    out=wc[n][:, P * lo : P * hi].bitcast(FP8X4),
-                    scales=ws[n][:, P * lo : P * hi],
-                    in_=src[:, 512 * lo : 512 * hi],
+        def quantise(codes, scales, src):
+            nc.vector.quantize_mx(out=codes.bitcast(FP8X4), scales=scales, in_=src)
+
+        def quant_natural(n):
+            for lo, hi in ((0, 2 * P), (2 * P, 3 * P)):
+                quantise(wc_n[n][:, lo:hi], ws_n[n][:, lo:hi], wb_n[n][:, 4 * lo : 4 * hi])
+
+        def quant_quad():
+            for lo, hi in ((1024, 1536), (0, 1024)):
+                quantise(wc_q[:, lo:hi], ws_q[:, lo:hi], wb_q[:, 4 * lo : 4 * hi])
+
+        def product1(n, hh, lo=0, hi=HALF):
+            cols = slice(HALF * hh + lo, HALF * hh + hi)
+            for a in range(KP):
+                if n < 4:
+                    codes, scales = wc_n[n][:, P * a : P * (a + 1)], ws_n[n][:, P * a : P * (a + 1)]
+                else:
+                    at = W1C * PLANE[n - 4] + P * a
+                    codes, scales = wc_q[:, at : at + P], ws_q[:, at : at + P]
+                nc.tensor.matmul_mx(
+                    out=first_bank(n, hh, lo)[:, lo:hi],
+                    lhsT=codes.bitcast(FP8X4),
+                    lhsT_scale=scales,
+                    rhs=(gt[a][:, cols] if a < KP - 1 else gt_last[hh][:, lo:hi]).bitcast(FP8X4),
+                    rhs_scale=gs[4 * a : P, cols],
+                    start=(a == 0),
+                    stop=(a == KP - 1),
                 )
 
-        def product1(n):
-            for hh in range(2):
-                cols = slice(HALF * hh, HALF * (hh + 1))
-                for a in range(KP):
-                    nc.tensor.matmul_mx(
-                        out=banks[2 * (n % 2) + hh][:],
-                        lhsT=wc[n][:, P * a : P * (a + 1)].bitcast(FP8X4),
-                        lhsT_scale=ws[n][:, P * a : P * (a + 1)],
-                        rhs=(gt[a][:, cols] if a < KP - 1 else gt_last[hh][:]).bitcast(FP8X4),
-                        rhs_scale=gs[4 * a : P, cols],
-                        start=(a == 0),
-                        stop=(a == KP - 1),
-                    )
-            for hh in range(2):
-                nc.scalar.copy(out=h_half(n, hh), in_=banks[2 * (n % 2) + hh][:])
+        def copy_h(n, hh, lo=0, hi=HALF):
+            nc.scalar.copy(out=h_half(n, hh)[:, lo:hi], in_=first_bank(n, hh, lo)[:, lo:hi])
 
         def make_h(n):
-            quant_w1(n)
-            product1(n)
+            for hh in range(2):
+                product1(n, hh)
+            for hh in range(2):
+                copy_h(n, hh)
 
-        def scatter(n, lo, hi):
-            if n < 4:
-                wg = wg_n[:, lo:hi]
-            else:
-                wg = wg_q[PLANE[n - 4]][:, lo:hi]
-            h = h_half(n, lo // HALF) if n in halved else hs[n][:, lo:hi]
+        def scatter(n, lo=0, hi=S):
+            wg = wg_n[:, lo:hi] if n < 4 else wg_q[PLANE[n - 4]][:, lo:hi]
+            h = h_half(n, lo // HALF) if n < 2 else h_whole[n][:]
             nc.vector.tensor_tensor(pages[n][:].indirect(idx2[:, lo // 16 : hi // 16]), h, wg, MULT)
 
         def fetch(n, x, lo, hi):
@@ -202,73 +199,166 @@ def tile_list_pacing_board_kernel(
         def z_plane(n, c):
             return zb1[c][:].rearrange("p (m t) -> p t m", t=4)[:, PLANE[n - 4]]
 
-        def rectify(n, x, lo, hi):
-            if n < 4:
-                nc.scalar.activation(out=zn[n][:, lo:hi], in_=x, func=RELU, bias=bias[n][:])
-            else:
-                for c in range(lo // CH, hi // CH):
-                    nc.scalar.activation(out=z_plane(n, c), in_=x[:, CH * c : CH * (c + 1)], func=RELU, bias=bias[n][:])
+        def rectify_scalar(n, x, c):
+            nc.scalar.activation(out=z_plane(n, c), in_=x, func=RELU, bias=bias[n][:])
 
-        def deal_rows(n):
-            nc.gpsimd.dma_start(out=zt0[32 * n : 32 * (n + 1), :], in_=zn[n][:])
+        def rectify_vector(n, x, c):
+            nc.vector.tensor_scalar(z_plane(n, c), x, bias[n][:], 0.0, ADD, MAX)
+
+        def turn_rows(n):
+            for hf in range(2):
+                bank = banks[4 + 2 * (n % 2) + hf]
+                for j in range(4):
+                    cols = slice(P * j, P * (j + 1))
+                    lo = HALF * hf + P * j
+                    nc.tensor.matmul(bank[:, cols], bias[n][:].to_broadcast([P, P]), ident[:], start=True, stop=False, is_transpose=True)
+                    nc.tensor.matmul(bank[:, cols], xs[n][:, lo : lo + P], ident[:], start=False, stop=True, is_transpose=True)
+            for hf in range(2):
+                nc.scalar.activation(
+                    out=zt[hf][:].rearrange("p (j r) -> p j r", j=4)[:, :, P * n : P * (n + 1)],
+                    in_=banks[4 + 2 * (n % 2) + hf][:].rearrange("p (j r) -> p j r", j=4),
+                    func=RELU,
+                )
+
+        def turn_back(c):
+            words = zt[c // 2][:].bitcast(F32)
+            for j in range(2):
+                lo = 256 * (2 * (c % 2) + j)
+                for u in range(2):
+                    nc.tensor.transpose(banks[4 + c][:, P * (2 * j + u) : P * (2 * j + u + 1)], words[:, lo + u : lo + 256 : 2], ident[:])
+            nc.scalar.copy(
+                out=zb0[c][:].bitcast(F32).rearrange("p (j m u) -> p j m u", j=2, u=2),
+                in_=banks[4 + c][:].rearrange("p (j u m) -> p j m u", j=2, u=2),
+            )
+
+        def fetch_natural(n):
+            fetch(n, xs[n][:], 0, M)
+            turn_rows(n)
+
+        def fetch_dealt(n, x, chunks):
+            fetch(n, x[:], 0, CH * chunks)
+            for c in range(chunks):
+                rectify_scalar(n, x[:, CH * c : CH * (c + 1)], c)
 
         nc.vector.memset(tabs[:].bitcast(I32), 0)
         nc.vector.memset(w2s[:].bitcast(I32), 0)
         for q in range(4):
             nc.gpsimd.dma_start(
-                out=tabs[32 * q : 32 * q + 4 * KP, :].bitcast(I32),
+                out=tabs[SCALE_AT[q] : SCALE_AT[q] + 4 * KP, :].bitcast(I32),
                 in_=tab_scales[:, 4 * q : 4 * q + 4, :].bitcast(I32),
             )
+        make_identity(nc, ident[:])
         load_table(0)
         nc.sync.dma_start(idx1[:], offs)
         load_table(1)
-        load_w1_natural(0, (0, 1))
+        load_w1_natural(0)
         load_table(2)
-        load_w1_natural(0, (2,))
         nc.sync.dma_start(idx2[:], offs2)
         load_page(0)
         nc.sync.dma_start(out=wg_n[:, 0:HALF], in_=wgs[:, 0:HALF])
         load_w1_natural(1)
+        nc.sync.dma_start(idx3[:], offs3)
         nc.sync.dma_start(out=wg_n[:, HALF:S], in_=wgs[:, HALF:S])
 
         def pick_words(dst, a, lo, hi):
             nc.vector.tensor_copy(dst, tabw[a][:].bitcast(U32).indirect(idx1[:, lo // 16 : hi // 16]))
 
-        for a in range(KP - 1):
-            pick_words(gt[a][:], a, 0, S)
-        nc.vector.tensor_copy(gs[:], tabs[:].indirect(idx1[:]))
-        pick_words(gt_last[0][:], KP - 1, 0, HALF)
+        pick_words(gt[0][:], 0, 0, S)
+        nc.vector.tensor_copy(gs_raw[:], tabs[:].indirect(idx1[:]))
+        nc.vector.tensor_copy(gs[:].bitcast(I32), gs_raw[:].bitcast(I32))
+        for q in (1, 3):
+            nc.gpsimd.dma_start(
+                out=gs[32 * q : 32 * q + 4 * KP, :].bitcast(I32),
+                in_=gs_raw[SCALE_AT[q] : SCALE_AT[q] + 4 * KP, :].bitcast(I32),
+            )
+        pick_words(gt[1][:], 1, 0, S)
+        cast_natural(0)
+        quant_natural(0)
+        for hh in range(2):
+            pick_words(gt_last[hh][:], KP - 1, HALF * hh, HALF * (hh + 1))
 
-        load_w1_natural(2)
-        nc.sync.dma_start(idx3[:], offs3)
         load_page(1)
+        load_w1_natural(2)
         load_w1_natural(3)
         load_page(2)
-        load_bias(0)
         load_w1_quad(0)
         load_w1_quad(1)
         load_page(3)
-        load_bias(1)
         load_w1_quad(2)
+        load_bias(0)
+        load_bias(1)
+        load_wg_quad(4)
+        load_page(4)
+        load_wg_quad(5)
+        load_page(5)
         load_bias(2)
-        for later in range(4, TILES - 1):
-            load_wg_quad(later)
-            load_page(later)
-            if later == 4:
-                load_bias(3)
-            if later == 6:
-                for n in (4, 5, 7):
-                    load_bias(n)
-                load_w2()
+        load_bias(4)
+        load_wg_quad(6)
+        load_page(6)
+        load_bias(3)
+        load_bias(5)
+        load_bias(7)
+        load_w2()
         load_wg_quad(7)
         load_page(7, 0, 3 * T2 // 4)
         load_bias(6)
         load_page(7, 3 * T2 // 4, T2)
 
+        for lo in (0, CH):
+            product1(0, 0, lo, lo + CH)
+            copy_h(0, 0, lo, lo + CH)
+        product1(0, 1)
+        copy_h(0, 1)
+        cast_natural(1)
+        scatter(0, 0, HALF)
+        quant_natural(1)
+        scatter(0, HALF, S)
+        product1(1, 0)
+        product1(1, 1)
+        copy_h(1, 0)
+        scatter(1, 0, HALF)
+        cast_natural(2)
+        copy_h(1, 1)
+        quant_natural(2)
+        fetch(0, xs[0][:], 0, M)
+        scatter(1, HALF, S)
+        cast_natural(3)
+        make_h(2)
+        quant_natural(3)
+        scatter(2)
+        cast_quad(0)
+        make_h(3)
+        fetch(1, xs[1][:], 0, M)
+        cast_quad(1)
+        scatter(3)
+        cast_quad(2)
+        turn_rows(0)
+        turn_rows(1)
+        quant_quad()
+        fetch(2, xs[2][:], 0, M)
+        fetch(3, xs[3][:], 0, M)
+        make_h(4)
+        make_h(5)
+        scatter(4)
+        make_h(6)
+        scatter(5)
+        make_h(7)
+        turn_rows(2)
+        fetch_dealt(4, xs[4], CHUNKS)
+        scatter(6)
+        turn_rows(3)
+        for c in range(CHUNKS):
+            turn_back(c)
+        fetch_dealt(5, xs[5], CHUNKS)
+        fetch_dealt(6, x6_early, 2)
+        last = TILES - 1
+        scatter(last)
+
         def out_bank(c, i):
             return banks[(3 * c + i) % 8]
 
-        def product2(c, a, which):
+        def product2(c, a, which=range(3)):
+            codes, scales = (zc0, zc1)[a][c], (zs0, zs1)[a][c]
             for i in which:
                 for j in range(2):
                     nt = 2 * i + j
@@ -278,65 +368,17 @@ def tile_list_pacing_board_kernel(
                             out=out_bank(c, i)[:, CH * j + P * h : CH * j + P * (h + 1)],
                             lhsT=w2w[:, a, 2 * P * nt : 2 * P * (nt + 1)].bitcast(FP4X4),
                             lhsT_scale=w2s[:, a, P * nt : P * (nt + 1)],
-                            rhs=zc[a][c][:, cols].bitcast(FP8X4),
-                            rhs_scale=zs[a][c][:, cols],
+                            rhs=codes[:, cols].bitcast(FP8X4),
+                            rhs_scale=scales[:, cols],
                             start=(a == 0 and j == 0 and h == 0),
                             stop=(a == 1 and j == 1 and h == 1),
                         )
 
-        def quant_z(a, c):
-            src = zb0[:, 4 * CH * c : 4 * CH * (c + 1)] if a == 0 else zb1[c][:]
-            nc.vector.quantize_mx(out=zc[a][c][:].bitcast(FP8X4), scales=zs[a][c][:], in_=src)
+        def quant_z0(k):
+            quantise(zc0[k][:], zs0[k][:], zb0[k][:])
 
-        def fetch_whole(n):
-            fetch(n, xs[n][:], 0, M)
-            rectify(n, xs[n][:], 0, M)
-            if n < 4:
-                deal_rows(n)
-
-        cast_natural(0)
-        quant_w1(0)
-        pick_words(gt_last[1][:], KP - 1, HALF, S)
-        product1(0)
-        cast_natural(1)
-        scatter(0, 0, HALF)
-        make_h(1)
-        scatter(0, HALF, S)
-        cast_natural(2)
-        fetch_whole(0)
-        make_h(2)
-        cast_natural(3)
-        scatter(1, 0, S)
-        cast_quad(0)
-        make_h(3)
-        cast_quad(1)
-        cast_quad(2)
-        scatter(2, 0, S)
-        fetch_whole(1)
-        scatter(3, 0, S)
-        for n in range(4, TILES - 1):
-            quant_w1(n)
-        product1(4)
-        product1(5)
-        fetch_whole(2)
-        fetch_whole(3)
-        scatter(4, 0, S)
-        product1(6)
-        quant_w1(7)
-        fetch_whole(4)
-        for c in range(CHUNKS):
-            nc.scalar.copy(
-                out=zb0[:, 4 * CH * c : 4 * CH * (c + 1)].rearrange("p (c i t) -> p c t i", i=4, t=4),
-                in_=zt0[:].rearrange("p (t m) -> p t m", t=4)[:, :, CH * c : CH * (c + 1)].rearrange("p t (c i) -> p c t i", i=4),
-            )
-        scatter(5, 0, S)
-        product1(7)
-        scatter(6, 0, S)
-        fetch_whole(5)
-        fetch(6, xs[6][:, 0:HALF], 0, HALF)
-        rectify(6, xs[6][:], 0, HALF)
-        last = TILES - 1
-        scatter(last, 0, S)
+        def quant_z1(c):
+            quantise(zc1[c][:], zs1[c][:], zb1[c][:])
 
         def finish(c, i):
             if c == CHUNKS - 1 and i != 1:
@@ -351,41 +393,42 @@ def tile_list_pacing_board_kernel(
         def fetch_last(c):
             fetch(last, x7[c][:], CH * c, CH * (c + 1))
 
-        def rectify_last(c):
-            if c == 1:
-                nc.scalar.activation(out=z_plane(last, c), in_=x7[c][:], func=RELU, bias=bias[last][:])
-            else:
-                nc.vector.tensor_scalar(z_plane(last, c), x7[c][:], bias[last][:], 0.0, ADD, MAX)
-
-        quant_z(0, 0)
-        product2(0, 0, range(3))
+        quant_z0(0)
+        product2(0, 0)
         fetch_last(0)
-        quant_z(0, 1)
-        rectify_last(0)
+        quant_z0(1)
+        rectify_vector(last, x7[0][:], 0)
         fetch_last(1)
-        rectify_last(1)
-        quant_z(1, 0)
-        product2(0, 1, range(3))
-        product2(1, 0, range(3))
-        for c in (2, 3):
-            fetch_last(c)
-            fetch(6, x6_late[c][:], CH * c, CH * (c + 1))
-            if c == 2:
-                quant_z(1, 1)
-                product2(1, 1, range(3))
-            rectify_last(c)
-            nc.vector.tensor_scalar(z_plane(6, c), x6_late[c][:], bias[6][:], 0.0, ADD, MAX)
-            quant_z(0, c)
-            quant_z(1, c)
+        rectify_scalar(last, x7[1][:], 1)
+        quant_z1(0)
+        product2(0, 1)
+        product2(1, 0)
+        fetch(6, x6_late[2][:], 2 * CH, 3 * CH)
+        quant_z0(2)
+        fetch_last(2)
+        quant_z1(1)
+        product2(1, 1)
         for j in range(2):
             nc.scalar.copy(out=stage[0][0][:, CH * j : CH * (j + 1)], in_=out_bank(0, 0)[:, CH * j : CH * (j + 1)])
             nc.sync.dma_start(out=out[P * j : P * (j + 1), 0:CH], in_=stage[0][0][:, CH * j : CH * (j + 1)])
         for i in range(1, 3):
             finish(0, i)
+        product2(2, 0)
         for i in range(3):
             finish(1, i)
-        for c in (2, 3):
-            for i in range(3):
-                product2(c, 0, (i,))
-                product2(c, 1, (i,))
-                finish(c, i)
+        rectify_vector(6, x6_late[2][:], 2)
+        rectify_vector(last, x7[2][:], 2)
+        fetch(6, x6_late[3][:], 3 * CH, M)
+        quant_z1(2)
+        product2(2, 1)
+        fetch_last(3)
+        quant_z0(3)
+        product2(3, 0)
+        rectify_vector(6, x6_late[3][:], 3)
+        rectify_vector(last, x7[3][:], 3)
+        for i in range(3):
+            finish(2, i)
+        quant_z1(3)
+        for i in range(3):
+            product2(3, 1, (i,))
+            finish(3, i)

@@ -26,9 +26,8 @@ TILES = 8
 HALF = 512
 CH = 256
 CHUNKS = M // CH
-PLANE = (3, 0, 1, 2)
+PLANE = (0, 1, 2, 3)
 W1C = KP * P
-SCALE_AT = (0, 48, 64, 112)
 
 
 def tile_list_pacing_board_kernel(
@@ -52,8 +51,7 @@ def tile_list_pacing_board_kernel(
         tabs = wt("tabs", 48, [P, T], U8)
         gt = [wt("gt%d" % a, 52 + 4 * a, [P, S], U32) for a in range(2)]
         gt_last = [wt("gt2_%d" % hh, 48 + 12 * hh, [P, HALF], U32) for hh in range(2)]
-        gs_raw = wt("gs_raw", 212, [P, S], U8)
-        gs = wt("gs", 213, [P, S], U8)
+        gs = wt("gs", 28, [P, S], U8)
         rawn_at = (62, 68, 80, 74)
         raw_n = [[wt("rawn%d_%d" % (n, a), rawn_at[n] + 2 * a, [P, 512], F32) for a in range(KP)] for n in range(4)]
         rawq_at = (87, 103, 95)
@@ -74,12 +72,14 @@ def tile_list_pacing_board_kernel(
         x_at = (81, 87, 95, 99, 95, 101)
         xs = [wt("x%d" % n, x_at[n], [P, M], F32) for n in range(6)]
         x6_early = wt("x6_early", 99, [P, HALF], F32)
-        x7 = [wt("x7_%d" % c, (207, 209, 70, 205.75)[c], [P, CH], F32) for c in range(CHUNKS)]
-        x6_late = {2: wt("x6_late2", 206.25, [P, CH], F32), 3: wt("x6_late3", 72, [P, CH], F32)}
+        x7 = [wt("x7_%d" % c, (208, 210)[c], [P, CH], F32) for c in range(2)]
+        x_pair = wt("x_pair", 206.25, [P, 2, CH], F32)
+        x_quad = wt("x_quad", 70, [P, 4, CH], F32)
+        bias_wide = {n: wt("bias_wide%d" % n, 208 + n, [P, CH], F32) for n in range(4, TILES)}
         zt = [wt("zt%d" % hf, 62 + 4 * hf, [P, 4 * 512], BF16) for hf in range(2)]
         zb0 = [wt("zb0_%d" % c, 135 + 2 * c, [P, 4 * CH], BF16) for c in range(CHUNKS)]
         zb1 = [wt("zb1_%d" % c, 70 + 2 * c, [P, 4 * CH], BF16) for c in range(CHUNKS)]
-        zc0 = [wt("zc0_%d" % c, (99, 100, 207.75, 70.5)[c], [P, CH], U32) for c in range(CHUNKS)]
+        zc0 = [wt("zc0_%d" % c, (99, 208.75, 210.5, 206.25)[c], [P, CH], U32) for c in range(CHUNKS)]
         zs0 = [wt("zs0_%d" % c, 175 + 0.25 * c, [P, CH], U8) for c in range(CHUNKS)]
         zc1 = [wt("zc1_%d" % c, 171 + c, [P, CH], U32) for c in range(CHUNKS)]
         zs1 = [wt("zs1_%d" % c, 176 + 0.25 * c, [P, CH], U8) for c in range(CHUNKS)]
@@ -158,7 +158,7 @@ def tile_list_pacing_board_kernel(
                 quantise(wc_n[n][:, lo:hi], ws_n[n][:, lo:hi], wb_n[n][:, 4 * lo : 4 * hi])
 
         def quant_quad():
-            for lo, hi in ((1024, 1536), (0, 1024)):
+            for lo, hi in ((0, 512), (512, 1536)):
                 quantise(wc_q[:, lo:hi], ws_q[:, lo:hi], wb_q[:, 4 * lo : 4 * hi])
 
         def product1(n, hh, lo=0, hi=HALF):
@@ -202,8 +202,27 @@ def tile_list_pacing_board_kernel(
         def rectify_scalar(n, x, c):
             nc.scalar.activation(out=z_plane(n, c), in_=x, func=RELU, bias=bias[n][:])
 
-        def rectify_vector(n, x, c):
-            nc.vector.tensor_scalar(z_plane(n, c), x, bias[n][:], 0.0, ADD, MAX)
+        def rectify_vector(n, x, c, h):
+            nc.vector.tensor_scalar(z_plane(n, c)[:, P * h : P * (h + 1)], x, bias[n][:], 0.0, ADD, MAX)
+
+        def fetch_biased(n, c):
+            window = pages[n][:].indirect(idx3[:, CH * c // 16 : CH * (c + 1) // 16])
+            x = x_pair[:, n - 6, :] if c == 2 else x_quad[:, n - 4, :]
+            nc.vector.tensor_tensor(x, window, bias_wide[n][:], ADD)
+
+        def rectify_quad(h):
+            nc.vector.tensor_scalar_max(
+                zb1[3][:, 4 * P * h : 4 * P * (h + 1)].rearrange("p (c i t) -> p c t i", i=4, t=4),
+                x_quad[:, :, P * h : P * (h + 1)].rearrange("p t (c i) -> p c t i", i=4),
+                0.0,
+            )
+
+        def rectify_pair(c):
+            nc.vector.tensor_scalar_max(
+                zb1[c][:].rearrange("p (m w e) -> p w m e", w=2, e=2)[:, 1],
+                x_pair[:].rearrange("p e m -> p m e"),
+                0.0,
+            )
 
         def turn_rows(n):
             for hf in range(2):
@@ -236,7 +255,7 @@ def tile_list_pacing_board_kernel(
             turn_rows(n)
 
         def fetch_dealt(n, x, chunks):
-            fetch(n, x[:], 0, CH * chunks)
+            fetch(n, x[:, 0 : CH * chunks], 0, CH * chunks)
             for c in range(chunks):
                 rectify_scalar(n, x[:, CH * c : CH * (c + 1)], c)
 
@@ -244,7 +263,7 @@ def tile_list_pacing_board_kernel(
         nc.vector.memset(w2s[:].bitcast(I32), 0)
         for q in range(4):
             nc.gpsimd.dma_start(
-                out=tabs[SCALE_AT[q] : SCALE_AT[q] + 4 * KP, :].bitcast(I32),
+                out=tabs[32 * q : 32 * q + 4 * KP, :].bitcast(I32),
                 in_=tab_scales[:, 4 * q : 4 * q + 4, :].bitcast(I32),
             )
         make_identity(nc, ident[:])
@@ -263,15 +282,9 @@ def tile_list_pacing_board_kernel(
         def pick_words(dst, a, lo, hi):
             nc.vector.tensor_copy(dst, tabw[a][:].bitcast(U32).indirect(idx1[:, lo // 16 : hi // 16]))
 
-        pick_words(gt[0][:], 0, 0, S)
-        nc.vector.tensor_copy(gs_raw[:], tabs[:].indirect(idx1[:]))
-        nc.vector.tensor_copy(gs[:].bitcast(I32), gs_raw[:].bitcast(I32))
-        for q in (1, 3):
-            nc.gpsimd.dma_start(
-                out=gs[32 * q : 32 * q + 4 * KP, :].bitcast(I32),
-                in_=gs_raw[SCALE_AT[q] : SCALE_AT[q] + 4 * KP, :].bitcast(I32),
-            )
-        pick_words(gt[1][:], 1, 0, S)
+        for a in range(KP - 1):
+            pick_words(gt[a][:], a, 0, S)
+        nc.vector.tensor_copy(gs[:], tabs[:].indirect(idx1[:]))
         cast_natural(0)
         quant_natural(0)
         for hh in range(2):
@@ -344,13 +357,15 @@ def tile_list_pacing_board_kernel(
         scatter(5)
         make_h(7)
         turn_rows(2)
-        fetch_dealt(4, xs[4], CHUNKS)
+        fetch_dealt(4, xs[4], CHUNKS - 1)
         scatter(6)
         turn_rows(3)
         for c in range(CHUNKS):
             turn_back(c)
-        fetch_dealt(5, xs[5], CHUNKS)
+        fetch_dealt(5, xs[5], CHUNKS - 1)
         fetch_dealt(6, x6_early, 2)
+        for n in range(4, TILES):
+            nc.scalar.copy(out=bias_wide[n][:], in_=bias[n][:].to_broadcast([P, CH]))
         last = TILES - 1
         scatter(last)
 
@@ -360,9 +375,9 @@ def tile_list_pacing_board_kernel(
         def product2(c, a, which=range(3)):
             codes, scales = (zc0, zc1)[a][c], (zs0, zs1)[a][c]
             for i in which:
-                for j in range(2):
-                    nt = 2 * i + j
-                    for h in range(2):
+                for h in range(2):
+                    for j in range(2):
+                        nt = 2 * i + j
                         cols = slice(P * h, P * (h + 1))
                         nc.tensor.matmul_mx(
                             out=out_bank(c, i)[:, CH * j + P * h : CH * j + P * (h + 1)],
@@ -380,6 +395,10 @@ def tile_list_pacing_board_kernel(
         def quant_z1(c):
             quantise(zc1[c][:], zs1[c][:], zb1[c][:])
 
+        def quant_halves(c):
+            for h in range(2):
+                quantise(zc1[c][:, P * h : P * (h + 1)], zs1[c][:, P * h : P * (h + 1)], zb1[c][:, 4 * P * h : 4 * P * (h + 1)])
+
         def finish(c, i):
             if c == CHUNKS - 1 and i != 1:
                 nc.vector.tensor_copy(out=stage[c][i][:], in_=out_bank(c, i)[:])
@@ -396,18 +415,19 @@ def tile_list_pacing_board_kernel(
         quant_z0(0)
         product2(0, 0)
         fetch_last(0)
-        quant_z0(1)
-        rectify_vector(last, x7[0][:], 0)
         fetch_last(1)
         rectify_scalar(last, x7[1][:], 1)
-        quant_z1(0)
+        for h in range(2):
+            rectify_vector(last, x7[0][:, P * h : P * (h + 1)], 0, h)
+        quant_halves(0)
         product2(0, 1)
+        quant_z0(1)
         product2(1, 0)
-        fetch(6, x6_late[2][:], 2 * CH, 3 * CH)
-        quant_z0(2)
-        fetch_last(2)
+        fetch_biased(6, 2)
         quant_z1(1)
         product2(1, 1)
+        fetch_biased(last, 2)
+        quant_z0(2)
         for j in range(2):
             nc.scalar.copy(out=stage[0][0][:, CH * j : CH * (j + 1)], in_=out_bank(0, 0)[:, CH * j : CH * (j + 1)])
             nc.sync.dma_start(out=out[P * j : P * (j + 1), 0:CH], in_=stage[0][0][:, CH * j : CH * (j + 1)])
@@ -416,19 +436,19 @@ def tile_list_pacing_board_kernel(
         product2(2, 0)
         for i in range(3):
             finish(1, i)
-        rectify_vector(6, x6_late[2][:], 2)
-        rectify_vector(last, x7[2][:], 2)
-        fetch(6, x6_late[3][:], 3 * CH, M)
+        rectify_pair(2)
+        fetch_biased(4, 3)
         quant_z1(2)
         product2(2, 1)
-        fetch_last(3)
+        for n in range(5, TILES):
+            fetch_biased(n, 3)
         quant_z0(3)
         product2(3, 0)
-        rectify_vector(6, x6_late[3][:], 3)
-        rectify_vector(last, x7[3][:], 3)
+        for h in range(2):
+            rectify_quad(h)
         for i in range(3):
             finish(2, i)
-        quant_z1(3)
+        quant_halves(3)
         for i in range(3):
             product2(3, 1, (i,))
             finish(3, i)

@@ -16,7 +16,6 @@ FP8X4 = mybir.dt.float8_e4m3fn_x4
 FP4X4 = mybir.dt.float4_e2m1fn_x4
 MULT = mybir.AluOpType.mult
 ADD = mybir.AluOpType.add
-MAX = mybir.AluOpType.max
 RELU = mybir.ActivationFunctionType.Relu
 
 P = 128
@@ -72,14 +71,14 @@ def tile_list_pacing_board_kernel(
         x_at = (81, 87, 95, 99, 95, 101)
         xs = [wt("x%d" % n, x_at[n], [P, M], F32) for n in range(6)]
         x6_early = wt("x6_early", 99, [P, HALF], F32)
-        x7 = [wt("x7_%d" % c, (208, 210)[c], [P, CH], F32) for c in range(2)]
-        x_pair = wt("x_pair", 206.25, [P, 2, CH], F32)
+        x_pair = wt("x_pair", 168, [P, 2, CH], F32)
+        x7 = [x_pair[:, 1, :], wt("x7_1", 210, [P, CH], F32)[:]]
         x_quad = wt("x_quad", 70, [P, 4, CH], F32)
         bias_wide = {n: wt("bias_wide%d" % n, 208 + n, [P, CH], F32) for n in range(4, TILES)}
         zt = [wt("zt%d" % hf, 62 + 4 * hf, [P, 4 * 512], BF16) for hf in range(2)]
         zb0 = [wt("zb0_%d" % c, 135 + 2 * c, [P, 4 * CH], BF16) for c in range(CHUNKS)]
         zb1 = [wt("zb1_%d" % c, 70 + 2 * c, [P, 4 * CH], BF16) for c in range(CHUNKS)]
-        zc0 = [wt("zc0_%d" % c, (99, 208.75, 210.5, 206.25)[c], [P, CH], U32) for c in range(CHUNKS)]
+        zc0 = [wt("zc0_%d" % c, (99, 167, 210.5, 168)[c], [P, CH], U32) for c in range(CHUNKS)]
         zs0 = [wt("zs0_%d" % c, 175 + 0.25 * c, [P, CH], U8) for c in range(CHUNKS)]
         zc1 = [wt("zc1_%d" % c, 171 + c, [P, CH], U32) for c in range(CHUNKS)]
         zs1 = [wt("zs1_%d" % c, 176 + 0.25 * c, [P, CH], U8) for c in range(CHUNKS)]
@@ -154,7 +153,7 @@ def tile_list_pacing_board_kernel(
             nc.vector.quantize_mx(out=codes.bitcast(FP8X4), scales=scales, in_=src)
 
         def quant_natural(n):
-            for lo, hi in ((0, 2 * P), (2 * P, 3 * P)):
+            for lo, hi in ((0, 2 * P), (2 * P, 3 * P)) if n < 2 else ((0, 3 * P),):
                 quantise(wc_n[n][:, lo:hi], ws_n[n][:, lo:hi], wb_n[n][:, 4 * lo : 4 * hi])
 
         def quant_quad():
@@ -201,9 +200,6 @@ def tile_list_pacing_board_kernel(
 
         def rectify_scalar(n, x, c):
             nc.scalar.activation(out=z_plane(n, c), in_=x, func=RELU, bias=bias[n][:])
-
-        def rectify_vector(n, x, c, h):
-            nc.vector.tensor_scalar(z_plane(n, c)[:, P * h : P * (h + 1)], x, bias[n][:], 0.0, ADD, MAX)
 
         def fetch_biased(n, c):
             window = pages[n][:].indirect(idx3[:, CH * c // 16 : CH * (c + 1) // 16])
@@ -374,19 +370,21 @@ def tile_list_pacing_board_kernel(
 
         def product2(c, a, which=range(3)):
             codes, scales = (zc0, zc1)[a][c], (zs0, zs1)[a][c]
+            pieces = 2 if (c, a) == (CHUNKS - 1, 1) else 1
+            w = CH // pieces
             for i in which:
-                for h in range(2):
+                for h in range(pieces):
                     for j in range(2):
                         nt = 2 * i + j
-                        cols = slice(P * h, P * (h + 1))
+                        cols = slice(w * h, w * (h + 1))
                         nc.tensor.matmul_mx(
-                            out=out_bank(c, i)[:, CH * j + P * h : CH * j + P * (h + 1)],
+                            out=out_bank(c, i)[:, CH * j + w * h : CH * j + w * (h + 1)],
                             lhsT=w2w[:, a, 2 * P * nt : 2 * P * (nt + 1)].bitcast(FP4X4),
                             lhsT_scale=w2s[:, a, P * nt : P * (nt + 1)],
                             rhs=codes[:, cols].bitcast(FP8X4),
                             rhs_scale=scales[:, cols],
                             start=(a == 0 and j == 0 and h == 0),
-                            stop=(a == 1 and j == 1 and h == 1),
+                            stop=(a == 1 and j == 1 and h == pieces - 1),
                         )
 
         def quant_z0(k):
@@ -410,23 +408,22 @@ def tile_list_pacing_board_kernel(
             )
 
         def fetch_last(c):
-            fetch(last, x7[c][:], CH * c, CH * (c + 1))
+            fetch(last, x7[c], CH * c, CH * (c + 1))
 
         quant_z0(0)
         product2(0, 0)
         fetch_last(0)
         fetch_last(1)
-        rectify_scalar(last, x7[1][:], 1)
-        for h in range(2):
-            rectify_vector(last, x7[0][:, P * h : P * (h + 1)], 0, h)
-        quant_halves(0)
-        product2(0, 1)
+        for c in range(2):
+            rectify_scalar(last, x7[c], c)
         quant_z0(1)
-        product2(1, 0)
         fetch_biased(6, 2)
+        quant_z1(0)
+        product2(0, 1)
+        product2(1, 0)
+        fetch_biased(last, 2)
         quant_z1(1)
         product2(1, 1)
-        fetch_biased(last, 2)
         quant_z0(2)
         for j in range(2):
             nc.scalar.copy(out=stage[0][0][:, CH * j : CH * (j + 1)], in_=out_bank(0, 0)[:, CH * j : CH * (j + 1)])

@@ -70,15 +70,15 @@ def tile_list_pacing_board_kernel(
         h_whole = {n: wt("h%d" % n, h_at[n], [P, S], F32) for n in range(2, TILES)}
         x_at = (81, 87, 95, 99, 95, 101)
         xs = [wt("x%d" % n, x_at[n], [P, M], F32) for n in range(6)]
-        x6_early = wt("x6_early", 99, [P, HALF], F32)
-        x_pair = wt("x_pair", 168, [P, 2, CH], F32)
-        x7 = [x_pair[:, 1, :], wt("x7_1", 210, [P, CH], F32)[:]]
+        x6_early = wt("x6_early", 99, [P, CH], F32)
+        x7_first = wt("x7_first", 208, [P, CH], F32)
+        x_pair = {c: wt("x_pair%d" % c, (159, 206.25)[c - 1], [P, 2, CH], F32) for c in (1, 2)}
         x_quad = wt("x_quad", 70, [P, 4, CH], F32)
         bias_wide = {n: wt("bias_wide%d" % n, 208 + n, [P, CH], F32) for n in range(4, TILES)}
         zt = [wt("zt%d" % hf, 62 + 4 * hf, [P, 4 * 512], BF16) for hf in range(2)]
         zb0 = [wt("zb0_%d" % c, 135 + 2 * c, [P, 4 * CH], BF16) for c in range(CHUNKS)]
         zb1 = [wt("zb1_%d" % c, 70 + 2 * c, [P, 4 * CH], BF16) for c in range(CHUNKS)]
-        zc0 = [wt("zc0_%d" % c, (99, 167, 210.5, 168)[c], [P, CH], U32) for c in range(CHUNKS)]
+        zc0 = [wt("zc0_%d" % c, (99, 167, 159, 206.25)[c], [P, CH], U32) for c in range(CHUNKS)]
         zs0 = [wt("zs0_%d" % c, 175 + 0.25 * c, [P, CH], U8) for c in range(CHUNKS)]
         zc1 = [wt("zc1_%d" % c, 171 + c, [P, CH], U32) for c in range(CHUNKS)]
         zs1 = [wt("zs1_%d" % c, 176 + 0.25 * c, [P, CH], U8) for c in range(CHUNKS)]
@@ -203,7 +203,7 @@ def tile_list_pacing_board_kernel(
 
         def fetch_biased(n, c):
             window = pages[n][:].indirect(idx3[:, CH * c // 16 : CH * (c + 1) // 16])
-            x = x_pair[:, n - 6, :] if c == 2 else x_quad[:, n - 4, :]
+            x = x_pair[c][:, n - 6, :] if c in x_pair else x_quad[:, n - 4, :]
             nc.vector.tensor_tensor(x, window, bias_wide[n][:], ADD)
 
         def rectify_quad(h):
@@ -214,11 +214,12 @@ def tile_list_pacing_board_kernel(
             )
 
         def rectify_pair(c):
-            nc.vector.tensor_scalar_max(
-                zb1[c][:].rearrange("p (m w e) -> p w m e", w=2, e=2)[:, 1],
-                x_pair[:].rearrange("p e m -> p m e"),
-                0.0,
-            )
+            z = zb1[c][:].rearrange("p (m w e) -> p w m e", w=2, e=2)[:, 1]
+            x = x_pair[c][:].rearrange("p e m -> p m e")
+            if c == 1:
+                nc.scalar.activation(out=z, in_=x, func=RELU)
+            else:
+                nc.vector.tensor_scalar_max(z, x, 0.0)
 
         def turn_rows(n):
             for hf in range(2):
@@ -359,7 +360,7 @@ def tile_list_pacing_board_kernel(
         for c in range(CHUNKS):
             turn_back(c)
         fetch_dealt(5, xs[5], CHUNKS - 1)
-        fetch_dealt(6, x6_early, 2)
+        fetch_dealt(6, x6_early, 1)
         for n in range(4, TILES):
             nc.scalar.copy(out=bias_wide[n][:], in_=bias[n][:].to_broadcast([P, CH]))
         last = TILES - 1
@@ -407,21 +408,19 @@ def tile_list_pacing_board_kernel(
                 in_=stage[c][i][:].rearrange("p (j m) -> p j m", j=2),
             )
 
-        def fetch_last(c):
-            fetch(last, x7[c], CH * c, CH * (c + 1))
-
         quant_z0(0)
         product2(0, 0)
-        fetch_last(0)
-        fetch_last(1)
-        for c in range(2):
-            rectify_scalar(last, x7[c], c)
+        fetch(last, x7_first[:], 0, CH)
+        rectify_scalar(last, x7_first[:], 0)
+        for n in (6, last):
+            fetch_biased(n, 1)
+        rectify_pair(1)
         quant_z0(1)
-        fetch_biased(6, 2)
         quant_z1(0)
         product2(0, 1)
         product2(1, 0)
-        fetch_biased(last, 2)
+        for n in (6, last):
+            fetch_biased(n, 2)
         quant_z1(1)
         product2(1, 1)
         quant_z0(2)

@@ -72,8 +72,8 @@ def tile_list_pacing_board_kernel(
         xs = [wt("x%d" % n, x_at[n], [P, M], F32) for n in range(6)]
         x6_early = wt("x6_early", 99, [P, CH], F32)
         x7_first = wt("x7_first", 208, [P, CH], F32)
-        x_pair = {c: wt("x_pair%d" % c, (159, 206.25)[c - 1], [P, 2, CH], F32) for c in (1, 2)}
-        x_quad = wt("x_quad", 70, [P, 4, CH], F32)
+        x_pair = wt("x_pair", 159, [P, 2, CH], F32)
+        x_quad = {c: wt("x_quad%d" % c, (205.5, 70)[c - 2], [P, 4, CH], F32) for c in (2, 3)}
         bias_wide = {n: wt("bias_wide%d" % n, 208 + n, [P, CH], F32) for n in range(4, TILES)}
         zt = [wt("zt%d" % hf, 62 + 4 * hf, [P, 4 * 512], BF16) for hf in range(2)]
         zb0 = [wt("zb0_%d" % c, 135 + 2 * c, [P, 4 * CH], BF16) for c in range(CHUNKS)]
@@ -203,23 +203,19 @@ def tile_list_pacing_board_kernel(
 
         def fetch_biased(n, c):
             window = pages[n][:].indirect(idx3[:, CH * c // 16 : CH * (c + 1) // 16])
-            x = x_pair[c][:, n - 6, :] if c in x_pair else x_quad[:, n - 4, :]
+            x = x_pair[:, n - 6, :] if c == 1 else x_quad[c][:, n - 4, :]
             nc.vector.tensor_tensor(x, window, bias_wide[n][:], ADD)
 
-        def rectify_quad(h):
+        def rectify_quad(c, lo, hi):
             nc.vector.tensor_scalar_max(
-                zb1[3][:, 4 * P * h : 4 * P * (h + 1)].rearrange("p (c i t) -> p c t i", i=4, t=4),
-                x_quad[:, :, P * h : P * (h + 1)].rearrange("p t (c i) -> p c t i", i=4),
+                zb1[c][:, 4 * lo : 4 * hi].rearrange("p (c i t) -> p c t i", i=4, t=4),
+                x_quad[c][:, :, lo:hi].rearrange("p t (c i) -> p c t i", i=4),
                 0.0,
             )
 
         def rectify_pair(c):
             z = zb1[c][:].rearrange("p (m w e) -> p w m e", w=2, e=2)[:, 1]
-            x = x_pair[c][:].rearrange("p e m -> p m e")
-            if c == 1:
-                nc.scalar.activation(out=z, in_=x, func=RELU)
-            else:
-                nc.vector.tensor_scalar_max(z, x, 0.0)
+            nc.scalar.activation(out=z, in_=x_pair[:].rearrange("p e m -> p m e"), func=RELU)
 
         def turn_rows(n):
             for hf in range(2):
@@ -354,12 +350,12 @@ def tile_list_pacing_board_kernel(
         scatter(5)
         make_h(7)
         turn_rows(2)
-        fetch_dealt(4, xs[4], CHUNKS - 1)
+        fetch_dealt(4, xs[4], 2)
         scatter(6)
         turn_rows(3)
         for c in range(CHUNKS):
             turn_back(c)
-        fetch_dealt(5, xs[5], CHUNKS - 1)
+        fetch_dealt(5, xs[5], 2)
         fetch_dealt(6, x6_early, 1)
         for n in range(4, TILES):
             nc.scalar.copy(out=bias_wide[n][:], in_=bias[n][:].to_broadcast([P, CH]))
@@ -398,15 +394,25 @@ def tile_list_pacing_board_kernel(
             for h in range(2):
                 quantise(zc1[c][:, P * h : P * (h + 1)], zs1[c][:, P * h : P * (h + 1)], zb1[c][:, 4 * P * h : 4 * P * (h + 1)])
 
-        def finish(c, i):
+        def finish(c, i, j0=0, j1=2):
+            cols = slice(CH * j0, CH * j1)
             if c == CHUNKS - 1 and i != 1:
-                nc.vector.tensor_copy(out=stage[c][i][:], in_=out_bank(c, i)[:])
+                nc.vector.tensor_copy(out=stage[c][i][:, cols], in_=out_bank(c, i)[:, cols])
             else:
-                nc.scalar.copy(out=stage[c][i][:], in_=out_bank(c, i)[:])
+                nc.scalar.copy(out=stage[c][i][:, cols], in_=out_bank(c, i)[:, cols])
             nc.sync.dma_start(
-                out=out[2 * P * i : 2 * P * (i + 1), CH * c : CH * (c + 1)].rearrange("(j p) m -> p j m", p=P),
-                in_=stage[c][i][:].rearrange("p (j m) -> p j m", j=2),
+                out=out[P * (2 * i + j0) : P * (2 * i + j1), CH * c : CH * (c + 1)].rearrange("(j p) m -> p j m", p=P),
+                in_=stage[c][i][:, cols].rearrange("p (j m) -> p j m", m=CH),
             )
+
+        def finish_chunk(c):
+            if c in (0, CHUNKS - 1):
+                for j in range(2):
+                    finish(c, 0, j, j + 1)
+            else:
+                finish(c, 0)
+            for i in range(1, 3):
+                finish(c, i)
 
         quant_z0(0)
         product2(0, 0)
@@ -423,16 +429,13 @@ def tile_list_pacing_board_kernel(
             fetch_biased(n, 2)
         quant_z1(1)
         product2(1, 1)
+        for n in (4, 5):
+            fetch_biased(n, 2)
         quant_z0(2)
-        for j in range(2):
-            nc.scalar.copy(out=stage[0][0][:, CH * j : CH * (j + 1)], in_=out_bank(0, 0)[:, CH * j : CH * (j + 1)])
-            nc.sync.dma_start(out=out[P * j : P * (j + 1), 0:CH], in_=stage[0][0][:, CH * j : CH * (j + 1)])
-        for i in range(1, 3):
-            finish(0, i)
+        finish_chunk(0)
         product2(2, 0)
-        for i in range(3):
-            finish(1, i)
-        rectify_pair(2)
+        finish_chunk(1)
+        rectify_quad(2, 0, CH)
         fetch_biased(4, 3)
         quant_z1(2)
         product2(2, 1)
@@ -441,10 +444,8 @@ def tile_list_pacing_board_kernel(
         quant_z0(3)
         product2(3, 0)
         for h in range(2):
-            rectify_quad(h)
-        for i in range(3):
-            finish(2, i)
+            rectify_quad(3, P * h, P * (h + 1))
+        finish_chunk(2)
         quant_halves(3)
-        for i in range(3):
-            product2(3, 1, (i,))
-            finish(3, i)
+        product2(3, 1)
+        finish_chunk(3)

@@ -71,15 +71,16 @@ def tile_list_pacing_board_kernel(
         x_at = (81, 87, 95, 99, 95, 101)
         xs = [wt("x%d" % n, x_at[n], [P, M], F32) for n in range(6)]
         x6_early = wt("x6_early", 99, [P, CH], F32)
-        x7_first = wt("x7_first", 208, [P, CH], F32)
+        x7_first = wt("x7_first", 216, [P, CH], F32)
         x_pair = wt("x_pair", 159, [P, 2, CH], F32)
-        x_quad = {c: wt("x_quad%d" % c, (205.5, 70)[c - 2], [P, 4, CH], F32) for c in (2, 3)}
+        x_ring = wt("x_ring", 216, [P, 5, CH], F32)
+        x_quad = {2: x_ring[:, 1:5, :], 3: x_ring[:, 0:4, :]}
         bias_wide = {n: wt("bias_wide%d" % n, 208 + n, [P, CH], F32) for n in range(4, TILES)}
         zt = [wt("zt%d" % hf, 62 + 4 * hf, [P, 4 * 512], BF16) for hf in range(2)]
         zb0 = [wt("zb0_%d" % c, 135 + 2 * c, [P, 4 * CH], BF16) for c in range(CHUNKS)]
         zb1 = [wt("zb1_%d" % c, 70 + 2 * c, [P, 4 * CH], BF16) for c in range(CHUNKS)]
         zc0 = [wt("zc0_%d" % c, (99, 167, 159, 206.25)[c], [P, CH], U32) for c in range(CHUNKS)]
-        zs0 = [wt("zs0_%d" % c, 175 + 0.25 * c, [P, CH], U8) for c in range(CHUNKS)]
+        zs0 = [wt("zs0_%d" % c, (175, 175.25, 175.5, 74)[c], [P, CH], U8) for c in range(CHUNKS)]
         zc1 = [wt("zc1_%d" % c, 171 + c, [P, CH], U32) for c in range(CHUNKS)]
         zs1 = [wt("zs1_%d" % c, 176 + 0.25 * c, [P, CH], U8) for c in range(CHUNKS)]
         stage = [[wt("st%d_%d" % (c, i), 111 + 2 * (3 * c + i), [P, 512], F32) for i in range(3)] for c in range(CHUNKS)]
@@ -206,12 +207,13 @@ def tile_list_pacing_board_kernel(
             x = x_pair[:, n - 6, :] if c == 1 else x_quad[c][:, n - 4, :]
             nc.vector.tensor_tensor(x, window, bias_wide[n][:], ADD)
 
-        def rectify_quad(c, lo, hi):
-            nc.vector.tensor_scalar_max(
-                zb1[c][:, 4 * lo : 4 * hi].rearrange("p (c i t) -> p c t i", i=4, t=4),
-                x_quad[c][:, :, lo:hi].rearrange("p t (c i) -> p c t i", i=4),
-                0.0,
-            )
+        def rectify_quad(c, h, on_scalar=False):
+            z = zb1[c][:, 4 * P * h : 4 * P * (h + 1)].rearrange("p (c i t) -> p c t i", i=4, t=4)
+            x = x_quad[c][:, :, P * h : P * (h + 1)].rearrange("p t (c i) -> p c t i", i=4)
+            if on_scalar:
+                nc.scalar.activation(out=z, in_=x, func=RELU)
+            else:
+                nc.vector.tensor_scalar_max(z, x, 0.0)
 
         def rectify_pair(c):
             z = zb1[c][:].rearrange("p (m w e) -> p w m e", w=2, e=2)[:, 1]
@@ -369,6 +371,7 @@ def tile_list_pacing_board_kernel(
             codes, scales = (zc0, zc1)[a][c], (zs0, zs1)[a][c]
             pieces = 2 if (c, a) == (CHUNKS - 1, 1) else 1
             w = CH // pieces
+            opening = 1 if c == 1 else 0
             for i in which:
                 for h in range(pieces):
                     for j in range(2):
@@ -380,8 +383,8 @@ def tile_list_pacing_board_kernel(
                             lhsT_scale=w2s[:, a, P * nt : P * (nt + 1)],
                             rhs=codes[:, cols].bitcast(FP8X4),
                             rhs_scale=scales[:, cols],
-                            start=(a == 0 and j == 0 and h == 0),
-                            stop=(a == 1 and j == 1 and h == pieces - 1),
+                            start=(a == opening and j == 0 and h == 0),
+                            stop=(a != opening and j == 1 and h == pieces - 1),
                         )
 
         def quant_z0(k):
@@ -424,18 +427,22 @@ def tile_list_pacing_board_kernel(
         quant_z0(1)
         quant_z1(0)
         product2(0, 1)
-        product2(1, 0)
         for n in (6, last):
             fetch_biased(n, 2)
         quant_z1(1)
-        product2(1, 1)
+        for i in range(3):
+            product2(1, 1, (i,))
+            product2(1, 0, (i,))
         for n in (4, 5):
             fetch_biased(n, 2)
         quant_z0(2)
         finish_chunk(0)
         product2(2, 0)
-        finish_chunk(1)
-        rectify_quad(2, 0, CH)
+        finish(1, 0)
+        rectify_quad(2, 0, on_scalar=True)
+        rectify_quad(2, 1)
+        for i in range(1, 3):
+            finish(1, i)
         fetch_biased(4, 3)
         quant_z1(2)
         product2(2, 1)
@@ -444,7 +451,7 @@ def tile_list_pacing_board_kernel(
         quant_z0(3)
         product2(3, 0)
         for h in range(2):
-            rectify_quad(3, P * h, P * (h + 1))
+            rectify_quad(3, h)
         finish_chunk(2)
         quant_halves(3)
         product2(3, 1)

@@ -403,10 +403,11 @@ def tile_list_pacing_board_kernel(
                 nc.vector.tensor_copy(out=stage[c][i][:, cols], in_=out_bank(c, i)[:, cols])
             else:
                 nc.scalar.copy(out=stage[c][i][:, cols], in_=out_bank(c, i)[:, cols])
-            nc.sync.dma_start(
-                out=out[P * (2 * i + j0) : P * (2 * i + j1), CH * c : CH * (c + 1)].rearrange("(j p) m -> p j m", p=P),
-                in_=stage[c][i][:, cols].rearrange("p (j m) -> p j m", m=CH),
-            )
+            for j in range(j0, j1):
+                nc.sync.dma_start(
+                    out=out[P * (2 * i + j) : P * (2 * i + j + 1), CH * c : CH * (c + 1)],
+                    in_=stage[c][i][:, CH * j : CH * (j + 1)],
+                )
 
         def finish_chunk(c):
             if c in (0, CHUNKS - 1):

from contextlib import ExitStack

import concourse.mybir as mybir
from concourse.masks import make_identity

K, T, S, H, T2, M, N = 1536, 4096, 1024, 1024, 2048, 1024, 768
FLOPS = 2 * K * H * S + 2 * H * N * M

F32 = mybir.dt.float32
BF16 = mybir.dt.bfloat16
I32 = mybir.dt.int32
U32 = mybir.dt.uint32
U16 = mybir.dt.uint16
U8 = mybir.dt.uint8
FP8X4 = mybir.dt.float8_e4m3fn_x4
FP4X4 = mybir.dt.float4_e2m1fn_x4
MULT = mybir.AluOpType.mult
ADD = mybir.AluOpType.add
RELU = mybir.ActivationFunctionType.Relu

P = 128
KB = 1024
KP = 3
TILES = 8
HALF = 512
CH = 256
CHUNKS = M // CH
PLANE = (0, 1, 2, 3)
W1C = KP * P


def tile_list_pacing_board_kernel(
    tc, tab_words, tab_scales, offs, w1, wgs, page0, offs2, offs3, b, w2_words, w2_scales, out
):
    nc = tc.nc
    with ExitStack() as ctx:
        keep = ctx.enter_context(tc.tile_pool(name="keep", bufs=1))
        psum = ctx.enter_context(tc.psum_pool(name="psum", bufs=1))
        work = ctx.enter_context(tc.tile_pool(name="work", bufs=1))

        idx1 = keep.tile([P, S // 16], U16, name="idx1", align_bytes=64)
        idx2 = keep.tile([P, S // 16], U16, name="idx2", align_bytes=64)
        idx3 = keep.tile([P, M // 16], U16, name="idx3", align_bytes=64)
        banks = [psum.tile([P, 512], F32, name="bank%d" % i) for i in range(8)]

        def wt(name, kb, shape, dtype):
            return work.tile(shape, dtype, name=name, offset=int(kb * KB), align_bytes=64)

        tabw = [wt("tabw%d" % a, 16 * a, [P, T], I32) for a in range(KP)]
        tabs = wt("tabs", 48, [P, T], U8)
        gt = [wt("gt%d" % a, 52 + 4 * a, [P, S], U32) for a in range(2)]
        gt_last = [wt("gt2_%d" % hh, 48 + 12 * hh, [P, HALF], U32) for hh in range(2)]
        gs = wt("gs", 28, [P, S], U8)
        rawn_at = (62, 68, 80, 74)
        raw_n = [[wt("rawn%d_%d" % (n, a), rawn_at[n] + 2 * a, [P, 512], F32) for a in range(KP)] for n in range(4)]
        rawq_at = (87, 103, 95)
        raw_q = [wt("rawq%d" % a, rawq_at[a], [P, 2048], F32) for a in range(KP)]
        page_at = (111, 119, 127, 135, 0, 8, 32, 40)
        pages = [wt("page%d" % n, page_at[n], [P, T2], F32) for n in range(TILES)]
        wg_n = wt("wg_n", 143, [P, S], F32)
        wg_q = [wt("wg_q%d" % t, 147 + 4 * t, [P, S], F32) for t in range(4)]
        wb_n = [wt("wbn%d" % n, 171 + 3 * n, [P, KP * 512], BF16) for n in range(4)]
        wb_q = wt("wbq", 16, [P, 4 * KP * 512], BF16)
        wc_n = [wt("wc%d" % n, 183 + 1.5 * n, [P, W1C], U32) for n in range(4)]
        wc_q = wt("wcq", 189, [P, 4 * W1C], U32)
        ws_n = [wt("ws%d" % n, 195 + 0.5 * n, [P, W1C], U8) for n in range(4)]
        ws_q = wt("wsq", 197, [P, 4 * W1C], U8)
        h_halves = [[wt("h0_0", 163, [P, HALF], F32), wt("h0_1", 165, [P, HALF], F32)], [wt("h1_0", 167, [P, HALF], F32), wt("h1_1", 85, [P, HALF], F32)]]
        h_at = {2: 163, 3: 91, 4: 163, 5: 167, 6: 163, 7: 167}
        h_whole = {n: wt("h%d" % n, h_at[n], [P, S], F32) for n in range(2, TILES)}
        x_at = (81, 87, 95, 99, 95, 101)
        xs = [wt("x%d" % n, x_at[n], [P, M], F32) for n in range(6)]
        x6_early = wt("x6_early", 99, [P, CH], F32)
        x7_first = wt("x7_first", 216, [P, CH], F32)
        x_pair = wt("x_pair", 159, [P, 2, CH], F32)
        x_ring = wt("x_ring", 216, [P, 5, CH], F32)
        x_quad = {2: x_ring[:, 1:5, :], 3: x_ring[:, 0:4, :]}
        bias_wide = {n: wt("bias_wide%d" % n, 208 + n, [P, CH], F32) for n in range(4, TILES)}
        zt = [wt("zt%d" % hf, 62 + 4 * hf, [P, 4 * 512], BF16) for hf in range(2)]
        zb0 = [wt("zb0_%d" % c, 135 + 2 * c, [P, 4 * CH], BF16) for c in range(CHUNKS)]
        zb1 = [wt("zb1_%d" % c, 70 + 2 * c, [P, 4 * CH], BF16) for c in range(CHUNKS)]
        zc0 = [wt("zc0_%d" % c, (99, 167, 159, 206.25)[c], [P, CH], U32) for c in range(CHUNKS)]
        zs0 = [wt("zs0_%d" % c, (175, 175.25, 175.5, 74)[c], [P, CH], U8) for c in range(CHUNKS)]
        zc1 = [wt("zc1_%d" % c, 171 + c, [P, CH], U32) for c in range(CHUNKS)]
        zs1 = [wt("zs1_%d" % c, 176 + 0.25 * c, [P, CH], U8) for c in range(CHUNKS)]
        stage = [[wt("st%d_%d" % (c, i), 111 + 2 * (3 * c + i), [P, 512], F32) for i in range(3)] for c in range(CHUNKS)]
        w2w = wt("w2w", 199, [P, 2, 2 * N], U8)
        w2s = wt("w2s", 202, [P, 2, N], U8)
        bias = [wt("bias%d" % n, 204 + n / 16, [P, 1], F32) for n in range(TILES)]
        ident = wt("ident", 205, [P, P], F32)

        def h_half(n, hh):
            return h_halves[n][hh][:] if n < 2 else h_whole[n][:, HALF * hh : HALF * (hh + 1)]

        def first_bank(n, hh, lo):
            return banks[4] if lo else banks[2 * (n % 2) + hh]

        def load_table(a):
            nc.sync.dma_start(out=tabw[a][:], in_=tab_words[a].rearrange("p t i -> p (t i)").bitcast(I32))

        def load_w1_natural(n):
            for a in range(KP):
                nc.sync.dma_start(
                    out=raw_n[n][a][:].rearrange("p (j c) -> p j c", j=4),
                    in_=w1[512 * a : 512 * (a + 1), P * n : P * (n + 1)].rearrange("(p j) c -> p j c", j=4),
                )

        def load_w1_quad(a):
            nc.sync.dma_start(
                out=raw_q[a][:].rearrange("p (j c) -> p j c", j=4),
                in_=w1[512 * a : 512 * (a + 1), 512:1024].rearrange("(p j) c -> p j c", j=4),
            )

        def load_page(n, lo=0, hi=T2):
            if n < 4:
                rows = page0[P * n : P * (n + 1), :]
            else:
                rows = page0[512:1024, :].rearrange("(p t) c -> t p c", t=4)[PLANE[n - 4]]
            nc.sync.dma_start(out=pages[n][:, lo:hi], in_=rows[:, lo:hi])

        def load_wg_quad(n):
            t = PLANE[n - 4]
            for q in (0, 2, 1, 3):
                nc.sync.dma_start(out=wg_q[t][32 * q : 32 * (q + 1), :], in_=wgs.rearrange("(u t) j -> t u j", t=4)[t])

        def load_bias(n):
            if n < 4:
                rows = b[P * n : P * (n + 1)].rearrange("(p g) -> p g", g=1)
            else:
                rows = b[512:1024].rearrange("(p t) -> p t", t=4)[:, PLANE[n - 4] : PLANE[n - 4] + 1]
            with nc.allow_non_contiguous_dma(reason="one bias value a partition"):
                nc.sync.dma_start(out=bias[n][:], in_=rows)

        def load_w2():
            nc.sync.dma_start(out=w2w[:].bitcast(I32), in_=w2_words.rearrange("a p c -> p a c").bitcast(I32))
            for q in range(4):
                nc.sync.dma_start(
                    out=w2s[32 * q : 32 * q + 4, :, :].bitcast(I32),
                    in_=w2_scales[:, 4 * q : 4 * q + 4, :].rearrange("a r c -> r a c").bitcast(I32),
                )

        def cast_natural(n):
            for a in range(KP):
                src = raw_n[n][a][:].rearrange("p (j c i) -> p c j i", j=4, i=4)
                nc.scalar.copy(out=wb_n[n][:, 512 * a : 512 * (a + 1)].rearrange("p (c i j) -> p c j i", i=4, j=4), in_=src)

        def cast_quad(a):
            nc.scalar.copy(
                out=wb_q[:].rearrange("p (t a m j) -> p a m t j", t=4, a=KP, j=4)[:, a],
                in_=raw_q[a][:].rearrange("p (j m t) -> p m t j", j=4, t=4),
            )

        def quantise(codes, scales, src):
            nc.vector.quantize_mx(out=codes.bitcast(FP8X4), scales=scales, in_=src)

        def quant_natural(n):
            for lo, hi in ((0, 2 * P), (2 * P, 3 * P)) if n < 2 else ((0, 3 * P),):
                quantise(wc_n[n][:, lo:hi], ws_n[n][:, lo:hi], wb_n[n][:, 4 * lo : 4 * hi])

        def quant_quad():
            for lo, hi in ((0, 512), (512, 1536)):
                quantise(wc_q[:, lo:hi], ws_q[:, lo:hi], wb_q[:, 4 * lo : 4 * hi])

        def product1(n, hh, lo=0, hi=HALF):
            cols = slice(HALF * hh + lo, HALF * hh + hi)
            for a in range(KP):
                if n < 4:
                    codes, scales = wc_n[n][:, P * a : P * (a + 1)], ws_n[n][:, P * a : P * (a + 1)]
                else:
                    at = W1C * PLANE[n - 4] + P * a
                    codes, scales = wc_q[:, at : at + P], ws_q[:, at : at + P]
                nc.tensor.matmul_mx(
                    out=first_bank(n, hh, lo)[:, lo:hi],
                    lhsT=codes.bitcast(FP8X4),
                    lhsT_scale=scales,
                    rhs=(gt[a][:, cols] if a < KP - 1 else gt_last[hh][:, lo:hi]).bitcast(FP8X4),
                    rhs_scale=gs[4 * a : P, cols],
                    start=(a == 0),
                    stop=(a == KP - 1),
                )

        def copy_h(n, hh, lo=0, hi=HALF):
            nc.scalar.copy(out=h_half(n, hh)[:, lo:hi], in_=first_bank(n, hh, lo)[:, lo:hi])

        def make_h(n):
            for hh in range(2):
                product1(n, hh)
            for hh in range(2):
                copy_h(n, hh)

        def scatter(n, lo=0, hi=S):
            wg = wg_n[:, lo:hi] if n < 4 else wg_q[PLANE[n - 4]][:, lo:hi]
            h = h_half(n, lo // HALF) if n < 2 else h_whole[n][:]
            nc.vector.tensor_tensor(pages[n][:].indirect(idx2[:, lo // 16 : hi // 16]), h, wg, MULT)

        def fetch(n, x, lo, hi):
            nc.vector.tensor_copy(x, pages[n][:].indirect(idx3[:, lo // 16 : hi // 16]))

        def z_plane(n, c):
            return zb1[c][:].rearrange("p (m t) -> p t m", t=4)[:, PLANE[n - 4]]

        def rectify_scalar(n, x, c):
            nc.scalar.activation(out=z_plane(n, c), in_=x, func=RELU, bias=bias[n][:])

        def fetch_biased(n, c):
            window = pages[n][:].indirect(idx3[:, CH * c // 16 : CH * (c + 1) // 16])
            x = x_pair[:, n - 6, :] if c == 1 else x_quad[c][:, n - 4, :]
            nc.vector.tensor_tensor(x, window, bias_wide[n][:], ADD)

        def rectify_quad(c, h, on_scalar=False):
            z = zb1[c][:, 4 * P * h : 4 * P * (h + 1)].rearrange("p (c i t) -> p c t i", i=4, t=4)
            x = x_quad[c][:, :, P * h : P * (h + 1)].rearrange("p t (c i) -> p c t i", i=4)
            if on_scalar:
                nc.scalar.activation(out=z, in_=x, func=RELU)
            else:
                nc.vector.tensor_scalar_max(z, x, 0.0)

        def rectify_pair(c):
            z = zb1[c][:].rearrange("p (m w e) -> p w m e", w=2, e=2)[:, 1]
            nc.scalar.activation(out=z, in_=x_pair[:].rearrange("p e m -> p m e"), func=RELU)

        def turn_rows(n):
            for hf in range(2):
                bank = banks[4 + 2 * (n % 2) + hf]
                for j in range(4):
                    cols = slice(P * j, P * (j + 1))
                    lo = HALF * hf + P * j
                    nc.tensor.matmul(bank[:, cols], bias[n][:].to_broadcast([P, P]), ident[:], start=True, stop=False, is_transpose=True)
                    nc.tensor.matmul(bank[:, cols], xs[n][:, lo : lo + P], ident[:], start=False, stop=True, is_transpose=True)
            for hf in range(2):
                nc.scalar.activation(
                    out=zt[hf][:].rearrange("p (j r) -> p j r", j=4)[:, :, P * n : P * (n + 1)],
                    in_=banks[4 + 2 * (n % 2) + hf][:].rearrange("p (j r) -> p j r", j=4),
                    func=RELU,
                )

        def turn_back(c):
            words = zt[c // 2][:].bitcast(F32)
            for j in range(2):
                lo = 256 * (2 * (c % 2) + j)
                for u in range(2):
                    nc.tensor.transpose(banks[4 + c][:, P * (2 * j + u) : P * (2 * j + u + 1)], words[:, lo + u : lo + 256 : 2], ident[:])
            nc.scalar.copy(
                out=zb0[c][:].bitcast(F32).rearrange("p (j m u) -> p j m u", j=2, u=2),
                in_=banks[4 + c][:].rearrange("p (j u m) -> p j m u", j=2, u=2),
            )

        def fetch_natural(n):
            fetch(n, xs[n][:], 0, M)
            turn_rows(n)

        def fetch_dealt(n, x, chunks):
            fetch(n, x[:, 0 : CH * chunks], 0, CH * chunks)
            for c in range(chunks):
                rectify_scalar(n, x[:, CH * c : CH * (c + 1)], c)

        nc.vector.memset(tabs[:].bitcast(I32), 0)
        nc.vector.memset(w2s[:].bitcast(I32), 0)
        for q in range(4):
            nc.gpsimd.dma_start(
                out=tabs[32 * q : 32 * q + 4 * KP, :].bitcast(I32),
                in_=tab_scales[:, 4 * q : 4 * q + 4, :].bitcast(I32),
            )
        make_identity(nc, ident[:])
        load_table(0)
        nc.sync.dma_start(idx1[:], offs)
        load_table(1)
        load_w1_natural(0)
        load_table(2)
        nc.sync.dma_start(idx2[:], offs2)
        load_page(0)
        nc.sync.dma_start(out=wg_n[:, 0:HALF], in_=wgs[:, 0:HALF])
        load_w1_natural(1)
        nc.sync.dma_start(idx3[:], offs3)
        nc.sync.dma_start(out=wg_n[:, HALF:S], in_=wgs[:, HALF:S])

        def pick_words(dst, a, lo, hi):
            nc.vector.tensor_copy(dst, tabw[a][:].bitcast(U32).indirect(idx1[:, lo // 16 : hi // 16]))

        for a in range(KP - 1):
            pick_words(gt[a][:], a, 0, S)
        nc.vector.tensor_copy(gs[:], tabs[:].indirect(idx1[:]))
        cast_natural(0)
        quant_natural(0)
        for hh in range(2):
            pick_words(gt_last[hh][:], KP - 1, HALF * hh, HALF * (hh + 1))

        load_page(1)
        load_w1_natural(2)
        load_w1_natural(3)
        load_page(2)
        load_w1_quad(0)
        load_w1_quad(1)
        load_page(3)
        load_w1_quad(2)
        load_bias(0)
        load_bias(1)
        load_wg_quad(4)
        load_page(4)
        load_wg_quad(5)
        load_page(5)
        load_bias(2)
        load_bias(4)
        load_wg_quad(6)
        load_page(6)
        load_bias(3)
        load_bias(5)
        load_bias(7)
        load_w2()
        load_wg_quad(7)
        load_page(7, 0, 3 * T2 // 4)
        load_bias(6)
        load_page(7, 3 * T2 // 4, T2)

        for lo in (0, CH):
            product1(0, 0, lo, lo + CH)
            copy_h(0, 0, lo, lo + CH)
        product1(0, 1)
        copy_h(0, 1)
        cast_natural(1)
        scatter(0, 0, HALF)
        quant_natural(1)
        scatter(0, HALF, S)
        product1(1, 0)
        product1(1, 1)
        copy_h(1, 0)
        scatter(1, 0, HALF)
        cast_natural(2)
        copy_h(1, 1)
        quant_natural(2)
        fetch(0, xs[0][:], 0, M)
        scatter(1, HALF, S)
        cast_natural(3)
        make_h(2)
        quant_natural(3)
        scatter(2)
        cast_quad(0)
        make_h(3)
        fetch(1, xs[1][:], 0, M)
        cast_quad(1)
        scatter(3)
        cast_quad(2)
        turn_rows(0)
        turn_rows(1)
        quant_quad()
        fetch(2, xs[2][:], 0, M)
        fetch(3, xs[3][:], 0, M)
        make_h(4)
        make_h(5)
        scatter(4)
        make_h(6)
        scatter(5)
        make_h(7)
        turn_rows(2)
        fetch_dealt(4, xs[4], 2)
        scatter(6)
        turn_rows(3)
        for c in range(CHUNKS):
            turn_back(c)
        fetch_dealt(5, xs[5], 2)
        fetch_dealt(6, x6_early, 1)
        for n in range(4, TILES):
            nc.scalar.copy(out=bias_wide[n][:], in_=bias[n][:].to_broadcast([P, CH]))
        last = TILES - 1
        scatter(last)

        def out_bank(c, i):
            return banks[(3 * c + i) % 8]

        def product2(c, a, which=range(3)):
            codes, scales = (zc0, zc1)[a][c], (zs0, zs1)[a][c]
            pieces = 2 if (c, a) == (CHUNKS - 1, 1) else 1
            w = CH // pieces
            opening = 1 if c == 1 else 0
            for i in which:
                for h in range(pieces):
                    for j in range(2):
                        nt = 2 * i + j
                        cols = slice(w * h, w * (h + 1))
                        nc.tensor.matmul_mx(
                            out=out_bank(c, i)[:, CH * j + w * h : CH * j + w * (h + 1)],
                            lhsT=w2w[:, a, 2 * P * nt : 2 * P * (nt + 1)].bitcast(FP4X4),
                            lhsT_scale=w2s[:, a, P * nt : P * (nt + 1)],
                            rhs=codes[:, cols].bitcast(FP8X4),
                            rhs_scale=scales[:, cols],
                            start=(a == opening and j == 0 and h == 0),
                            stop=(a != opening and j == 1 and h == pieces - 1),
                        )

        def quant_z0(k):
            quantise(zc0[k][:], zs0[k][:], zb0[k][:])

        def quant_z1(c):
            quantise(zc1[c][:], zs1[c][:], zb1[c][:])

        def quant_halves(c):
            for h in range(2):
                quantise(zc1[c][:, P * h : P * (h + 1)], zs1[c][:, P * h : P * (h + 1)], zb1[c][:, 4 * P * h : 4 * P * (h + 1)])

        def finish(c, i, j0=0, j1=2):
            cols = slice(CH * j0, CH * j1)
            if c == CHUNKS - 1 and i != 1:
                nc.vector.tensor_copy(out=stage[c][i][:, cols], in_=out_bank(c, i)[:, cols])
            else:
                nc.scalar.copy(out=stage[c][i][:, cols], in_=out_bank(c, i)[:, cols])
            for j in range(j0, j1):
                nc.sync.dma_start(
                    out=out[P * (2 * i + j) : P * (2 * i + j + 1), CH * c : CH * (c + 1)],
                    in_=stage[c][i][:, CH * j : CH * (j + 1)],
                )

        def finish_chunk(c):
            if c in (0, CHUNKS - 1):
                for j in range(2):
                    finish(c, 0, j, j + 1)
            else:
                finish(c, 0)
            for i in range(1, 3):
                finish(c, i)

        quant_z0(0)
        product2(0, 0)
        fetch(last, x7_first[:], 0, CH)
        rectify_scalar(last, x7_first[:], 0)
        for n in (6, last):
            fetch_biased(n, 1)
        rectify_pair(1)
        quant_z0(1)
        quant_z1(0)
        product2(0, 1)
        for n in (6, last):
            fetch_biased(n, 2)
        quant_z1(1)
        for i in range(3):
            product2(1, 1, (i,))
            product2(1, 0, (i,))
        for n in (4, 5):
            fetch_biased(n, 2)
        quant_z0(2)
        finish_chunk(0)
        product2(2, 0)
        finish(1, 0)
        rectify_quad(2, 0, on_scalar=True)
        rectify_quad(2, 1)
        for i in range(1, 3):
            finish(1, i)
        fetch_biased(4, 3)
        quant_z1(2)
        product2(2, 1)
        for n in range(5, TILES):
            fetch_biased(n, 3)
        quant_z0(3)
        product2(3, 0)
        for h in range(2):
            rectify_quad(3, h)
        finish_chunk(2)
        quant_halves(3)
        product2(3, 1)
        finish_chunk(3)
